import numpy as np, ml_dtypes
CORES = [5,29,101,125,133,157,229,253]
N = 8
BF = ml_dtypes.bfloat16
V, C, T, S, VT, DR, DG = 2048, 256, 5, 48, 9, 1, 5
def start(s0, w0):
    H = np.full((N, 8, 16, C), -1, np.int64); H[:, :, 0] = s0; live = s0 >= 0
    return H, np.where(live[:, :, None], w0, np.float32(0)), live
def grow(t, H, W, live, nt, qt, u):
    nk = np.take_along_axis(nt, np.where(live, H[:, :, t], 0)[:, :, None, :], 3)
    shut = np.zeros(nk.shape, bool)
    for p in range(t + 1): shut |= nk == H[:, :, p:p + 1]
    x = np.take_along_axis(qt, nk.reshape(N, 8, 1, 16 * C), 3).reshape(N, 8, 16, 16, C)
    P = np.add.accumulate(np.where(shut[:, :, None], 0, x), axis=3); full = P[:, :, :, 15]
    votes = np.sum(256 * P > u[:, :, None, None, :] * full[:, :, :, None], axis=2)
    k = np.argmax((votes >= VT) & ~shut, axis=2); site = np.take_along_axis(nk, k[:, :, None, :], 2)[:, :, 0]
    moved = live & ~np.all(shut, axis=2)
    H = H.copy(); H[:, :, t + 1] = np.where(moved, site, -1)
    W = np.where(moved[:, :, None], W * full.astype(np.float32) * np.float32(2.0 ** -11), np.float32(0))
    return H, W, moved
def breed(H, W, live, old, lo, hi, coin):
    low = live & (np.sum(W < lo[..., None], axis=2) >= VT); high = live & (np.sum(W > hi[..., None], axis=2) >= VT)
    W = np.where(high[:, :, None], W * np.float32(0.5), np.where(low[:, :, None], W * np.float32(2), W))
    live = live & ~(low & (coin == 0)); H = H.copy()
    up = np.sum(high, axis=(0, 2)) > np.sum(old & ~live, axis=(0, 2))
    over, left = {}, {}
    for a in range(N):
        for g in range(8):
            src = np.flatnonzero(high[a, g]); hole = np.flatnonzero(~live[a, g]); n = min(len(src), len(hole))
            H[a, g][:, hole[:n]] = H[a, g][:, src[:n]]; W[a, g][:, hole[:n]] = W[a, g][:, src[:n]]; live[a, g, hole[:n]] = True
            over[a, g] = (H[a, g][:, src[n:n + S]], W[a, g][:, src[n:n + S]]); left[a, g] = hole[n:]
    for a in range(N):
        for g in range(8):
            h, w = over[(a - DR) % N, (g - DG) % 8]; hole = left[a, g][:h.shape[1]]; m = len(hole)
            H[a, g][:, hole] = h[:, :m]; W[a, g][:, hole] = w[:, :m]; live[a, g, hole] = True
    return H, W, live, up
def land(rng, traps):
    ring = np.argsort(rng.random((N, 8, V)), axis=-1); x = np.arange(V); sh = (N, 8, 16, V)
    to = np.where(rng.random(sh) < 0.4, (x + rng.integers(-6, 7, sh)) % V, rng.integers(0, V, sh))
    m = np.repeat(rng.integers(1, 5, (N, 8, V // 4)), 4, axis=-1)[:, :, None]; trap = np.repeat(rng.random((N, 8, V // 4)) < traps, 4, axis=-1)[:, :, None]
    to = np.where(trap, 4 * (x // 4) + (rng.random(sh) * m).astype(np.int64), to)
    return np.take_along_axis(np.take_along_axis(ring[:, :, None], to, 3), np.argsort(ring, axis=-1)[:, :, None], 3)
def base(rng, traps, dead):
    qt = np.clip(np.rint(rng.uniform(40, 200, (N, 8, 1, V)) * rng.uniform(0.6, 1.4, (N, 8, 16, V))), 16, 255).astype(np.int32)
    s0 = np.where(rng.random((N, 8, C)) < dead * rng.random((N, 8, 1)), -1, rng.integers(0, V, (N, 8, C)))
    w0 = np.exp2(rng.uniform(-2, 2, (N, 8, 1, C)) + rng.uniform(-1, 1, (N, 8, 16, 1)) + rng.uniform(-0.2, 0.2, (N, 8, 16, C))).astype(np.float32)
    return dict(nt=land(rng, traps), qt=qt, s0=s0, w0=w0, u=rng.integers(0, 256, (N, 8, T, C)), coin=rng.integers(0, 2, (N, 8, T, C)))
def limits(rng, W, live, na, nh, sharp):
    lo = np.ones((N, 8, 16), np.float32); hi = np.ones((N, 8, 16), np.float32); tiny = np.float32(0); huge = np.float32(2.0 ** 100)
    for a in range(N):
        for g in range(8):
            m = np.flatnonzero(live[a, g]); n = len(m)
            if n == 0: continue
            w = W[a, g][:, m]; o = np.argsort(np.add.reduce(np.log2(w), axis=0), kind="stable"); i = int(na[a, g]); j = n - 1 - int(nh[a, g])
            least = np.minimum.reduce(w, axis=1) * np.float32(0.5); most = np.maximum.reduce(w, axis=1) * np.float32(2)
            r1 = rng.permutation(16) < rng.choice(np.array([0, VT - 1, VT, 16])); r2 = rng.permutation(16) < rng.choice(np.array([0, VT - 1, VT, 16]))
            if i < 0: l = least
            elif i >= n: l = most
            elif sharp[a, g]: l = np.where(r1, np.nextafter(w[:, o[i]], huge), w[:, o[i]])
            else: l = w[:, o[i]] * np.float32(0.25)
            if j >= n: h = most
            elif j < 0: h = least
            elif sharp[a, g] == 2:
                v = np.sort(w, axis=0)[16 - VT]
                h = np.full(16, np.max(v[v < np.max(v)], initial=np.min(v) * np.float32(0.5)), np.float32)
            elif sharp[a, g]: h = np.where(r2, np.nextafter(w[:, o[j]], tiny), w[:, o[j]])
            else: h = w[:, o[j]] * np.float32(4)
            lo[a, g] = np.minimum(l, h); hi[a, g] = h
    return lo, hi
def tilt(rng, coin, W, live, old, lo, hi, tip):
    low = live & (np.sum(W < lo[..., None], axis=2) >= VT); high = live & (np.sum(W > hi[..., None], axis=2) >= VT)
    for g in tip:
        m = np.flatnonzero(low[:, g].reshape(-1)); k = int(np.sum(high[:, g])) - int(np.sum(old[:, g] & ~live[:, g])) - tip[g]
        z = coin[:, g].copy().reshape(-1); z[m] = 1; z[rng.permutation(m)[:max(k, 0)]] = 0
        coin[:, g] = z.reshape(N, C)
def finish(rng, d, goal):
    H, W, live = start(d["s0"], d["w0"]); f = np.ones(8, np.float32); lo = np.ones((N, 8, 16, T), np.float32); hi = np.ones((N, 8, 16, T), np.float32)
    for t in range(T):
        old = live
        H, W, live = grow(t, H, W, live, d["nt"], d["qt"], d["u"][:, :, t])
        aim = goal(t, np.sum(live, axis=2))
        l, h = limits(rng, W, live, aim[0], aim[1], aim[2])
        if len(aim) > 3: tilt(rng, d["coin"][:, :, t], W, live, old, l, h, aim[3])
        lo[..., t] = l * f[:, None]; hi[..., t] = h * f[:, None]
        H, W, live, up = breed(H, W, live, old, l, h, d["coin"][:, :, t])
        f = np.where(up, f * np.float32(0.5), f)
    return {"nb": np.ascontiguousarray(d["nt"].reshape(N, 128, V)).astype(np.int32), "qs": d["qt"].reshape(N, 128, V).astype(np.float32).astype(BF),
            "s0": d["s0"].astype(np.int32), "w0": np.ascontiguousarray(d["w0"].reshape(N, 128, C)).astype(np.float32),
            "us": np.ascontiguousarray(d["u"].reshape(N, 8, T * C)).astype(np.int32), "coin": np.ascontiguousarray(d["coin"].reshape(N, 8, T * C)).astype(np.int32),
            "lo": lo.reshape(N, 128, T), "hi": hi.reshape(N, 128, T)}
def sway(rng, n, k):
    up = (rng.permutation(8) < k)[None, :]
    a = np.where(up, rng.uniform(0.03, 0.12, (N, 8)), rng.uniform(0.3, 0.5, (N, 8))); b = np.where(up, rng.uniform(0.25, 0.45, (N, 8)), rng.uniform(0.03, 0.12, (N, 8)))
    return (a * n).astype(np.int64), (b * n).astype(np.int64), np.ones((N, 8), bool)
def setup_inputs(rng):
    return finish(rng, base(rng, 0.1, 0.3), lambda t, n: sway(rng, n, 4))
def setup_inputs_calm(rng):
    o = rng.permutation(8); num = np.zeros(8, np.int64); few = np.zeros(8, bool); num[o] = np.arange(8) % 4; few[o[:4]] = True
    d = base(rng, np.where(few, 0.0, 0.05)[:, None], 0.0)
    odd = (np.arange(N)[:, None] + np.arange(8)[None, :]) % 2 == 1
    d["qt"] = np.where(odd[:, :, None, None], rng.integers(60, 200, (N, 8, 16, 1)), d["qt"]).astype(np.int32)
    d["u"] = np.where(odd[:, :, None, None], 16 * rng.integers(0, 16, (N, 8, T, C)), d["u"])
    def goal(t, n):
        rich = (np.arange(N)[:, None] + t + num[None, :]) % 2 == 0; tip = {}
        a = np.where(few[None, :], 0.3, np.where(rich, 0.12, 0.5)) * rng.uniform(0.9, 1.0, (N, 8)); b = np.where(rich, 0.3, 0.05) * rng.uniform(0.9, 1.0, (N, 8))
        na = (a * n).astype(np.int64); nh = (b * n).astype(np.int64); sharp = np.ones((N, 8), np.int64)
        for g in range(8):
            k = int(num[g])
            if few[g]:
                c = 1 + t % 3 if t < k else (t + k) % 4
                q = rng.permutation(N)[:c]; nh[:, g] = -1; nh[q, g] = 1; sharp[q, g] = 2
                tip[g] = 1 if t < k else 0
            else: tip[g] = 1 + (t + g) % 3 if t < k else -((t + k) % 2)
        return na, nh, sharp, tip
    return finish(rng, d, goal)
def setup_inputs_corners(rng):
    d = base(rng, 0.0, 0.0); d["s0"] = rng.integers(0, V, (N, 8, C))
    d["w0"] = np.exp2(rng.uniform(-0.4, 0.4, (N, 8, 1, C)) + rng.uniform(-1, 1, (N, 8, 16, 1))).astype(np.float32)
    d["u"] = np.where(rng.random(d["u"].shape) < 0.3, 255 * rng.integers(0, 2, d["u"].shape), d["u"])
    cases = [(0, 0, S), (0, 0, C), (C, 0, 0), (C - 1, 0, 1), (40, 24, 64), (40, 24, 65 + S), (40, 24, 63 + S), (40, 24, 64 - S), (40, 24, 65 - S), (0, C, 0), (0, C - 1, 0), (0, 0, 0)]
    kind = rng.integers(0, 12, (N, 8)); o = rng.permutation(8)
    for a in range(N): kind[a, a % 8] = 5
    for i in range(8):
        kind[0, o[i]] = (0, 1, 5, 6, 0, 5, 1, 6)[i]; kind[DR % N, (o[i] + DG) % 8] = (7, 8, 7, 8, 2, 3, 4, 7)[i]
    na = np.zeros((N, 8), np.int64); nh = np.zeros((N, 8), np.int64)
    for a in range(N):
        for g in range(8):
            z, k, m = cases[kind[a, g]]; p = rng.permutation(C); na[a, g] = k; nh[a, g] = m
            d["s0"][a, g, p[:z]] = -1; d["coin"][a, g, 0, p[z:z + k]] = 0
            d["w0"][a, g][:, p[z:z + k]] *= np.float32(2.0 ** -6); d["w0"][a, g][:, p[z + k:z + k + m]] *= np.float32(64)
    return finish(rng, d, lambda t, n: (na, nh, np.zeros((N, 8), bool)) if t == 0 else sway(rng, n, 4))
def setup_inputs_crowd(rng):
    d = base(rng, 0.0, 0.0); kind = [list("ABDFGHIJ")[i] for i in rng.permutation(8)]; far = int(rng.integers(0, N))
    i = kind.index("A"); j = (kind.index("D") - DG) % 8; kind[i], kind[j] = kind[j], kind[i]
    fall = rng.permutation(N)[:(N // 2 if C > 255 else N - 2)].tolist()
    d["w0"] = np.exp2(rng.uniform(-0.4, 0.4, (N, 8, 1, C)) + rng.uniform(-1, 1, (N, 8, 16, 1))).astype(np.float32)
    na = np.full((N, 8), -1, np.int64); nh = np.full((N, 8), -1, np.int64); big = np.float32(64); small = np.float32(2.0 ** -6)
    for a in range(N):
        for g in range(8):
            c = kind[g]; one = (0, C - 1, int(rng.integers(0, C)))[int(rng.integers(0, 3))]; w = d["w0"][a, g]
            if c == "A":
                nh[a, g] = C
                if a % 2 == 0: d["s0"][a, g] = V - 1
            elif c == "B": nh[a, g] = C - 1; w[:, one] *= small
            elif (c == "H" and a % 2 == 0) or (c == "J" and a not in fall): nh[a, g] = C
            elif c == "D" or c == "J": d["coin"][a, g, 0] = 0; na[a, g] = C
            elif c == "H": d["coin"][a, g, 0] = 0; na[a, g] = C - 1; w[:, one] *= big
            elif c == "G":
                b = C // 4; p = rng.permutation(C); v = int(rng.integers(1, V - 1)); s = d["s0"][a, g]
                s[s == v] = 0; s[p[:b]] = v; d["nt"][a, g][:, v] = v
                na[a, g] = b; nh[a, g] = C - 2 * b; d["coin"][a, g, 0] = 0; w[:, p[b:2 * b]] *= small; w[:, p[2 * b:]] *= big
            else:
                k = C // 2; m = C - k; p = rng.permutation(C)
                if a == far and c == "F": k = k - 1
                if a == far and c == "I": m = m - 1
                na[a, g] = k; nh[a, g] = m
                d["coin"][a, g, 0] = 0; w[:, p[:k]] *= small; w[:, p[C - m:]] *= big
    def goal(t, n):
        if t == 0: return na, nh, np.zeros((N, 8), bool)
        a, b, s = sway(rng, n, 4)
        for g in range(8):
            if t < T - 1 and (kind[g] == "A" or kind[g] == "B"): a[:, g] = -1; b[:, g] = -1 if (kind[g] == "B" and t == 1) else C
        return a, b, s
    return finish(rng, d, goal)
def setup_inputs_ends(rng):
    d = base(rng, 0.0, 0.0); sh = (N, 8, 16, V)
    end = rng.random(sh) < np.where(rng.random((N, 8, 1, V)) < 0.3, 1.0, 0.55)
    d["nt"] = np.where(end, (V - 1) * rng.integers(0, 2, sh), d["nt"])
    bit = np.where(rng.random((N, 8, 1, V)) < 0.5, rng.integers(0, 2, (N, 8, 1, V)), rng.integers(0, 2, sh))
    d["qt"] = (16 + 239 * bit).astype(np.int32)
    d["w0"] = np.ascontiguousarray(np.broadcast_to(np.exp2(32.0 * rng.integers(0, 2, (N, 8, 1, C)) - 16), (N, 8, 16, C))).astype(np.float32)
    for a in range(N):
        for g in range(8):
            p = 1 + rng.permutation(V - 2)[:40]; nt = d["nt"][a, g]; qt = d["qt"][a, g]; m = (a + g) % 4
            nt[::2, p] = rng.integers(1, V - 1, (8, 40)); nt[:, 0] = p[17:33]; qt[:, p[17:32]] = 255; qt[:, p[32]] = rng.integers(144, 255, 16)
            d["w0"][a, g][:, [0, C - 1]] = np.float32(2.0 ** 16 if m % 2 == 0 else 2.0 ** -16)
            if m % 2 == 0:
                nt[:, V - 1] = p[:16]; qt[:, p[:16]] = 255
                if m == 0: nt[:, p[:16]] = p[17:33][:, None]; nt[:, p[17:33]] = p[:16][:, None]
            else:
                nt[:, V - 1] = V - 1; nt[15, V - 1] = p[16]; qt[:, p[16]] = 16; nt[:, p[16]] = p[:16]
                if m == 1:
                    way = [V - 1, int(p[16])] + p[33:32 + T].tolist()
                    for j in range(T):
                        nt[:, way[j]] = way[j]; nt[15 if j == 0 else int(rng.integers(0, 16)), way[j]] = way[j + 1]; qt[:, way[j + 1]] = 16
                    d["coin"][a, g][:, ::3] = 1; d["coin"][a, g][:, C - 1] = 1
    r = rng.random((N, 8, C)); d["s0"] = np.where(r < 0.2, -1, np.where(r < 0.55, V - 1, np.where(r < 0.75, 0, rng.integers(0, V, (N, 8, C))))); d["s0"][..., 0] = V - 1; d["s0"][..., 1] = 0; d["s0"][..., C - 1] = V - 1
    d["u"] = np.where(rng.random(d["u"].shape) < 0.85, 255 * rng.integers(0, 2, d["u"].shape), d["u"])
    return finish(rng, d, lambda t, n: sway(rng, n, 6))
def setup_inputs_spread(rng):
    d = base(rng, 0.08, 0.3)
    d["qt"] = np.clip(np.rint(np.exp2(4 + 4 * rng.random((N, 8, 1, V)) + rng.uniform(-1, 1, (N, 8, 16, V)))), 16, 255).astype(np.int32)
    d["u"] = (256 * rng.random((N, 8, T, C)) ** 3).astype(np.int64)
    d["w0"] = np.exp2(rng.uniform(-6, 6, (N, 8, 1, C)) + rng.uniform(-2, 2, (N, 8, 16, 1)) + rng.uniform(-0.3, 0.3, (N, 8, 16, C))).astype(np.float32)
    return finish(rng, d, lambda t, n: sway(rng, n, 4))
def check_inputs(d):
    bad = []
    for k, a, b in (("nb", 0, V - 1), ("qs", 16, 255), ("s0", -1, V - 1), ("us", 0, 255), ("coin", 0, 1), ("w0", 2.0 ** -16, 2.0 ** 16), ("lo", 2.0 ** -90, 2.0 ** 90), ("hi", 2.0 ** -90, 2.0 ** 90)):
        v = np.asarray(d[k]).astype(np.float64)
        if not (np.min(v) >= a and np.max(v) <= b): bad.append("range of " + k)
    v = np.asarray(d["qs"]).astype(np.float64)
    if not np.all(v == np.floor(v)): bad.append("qs not whole")
    if not np.all(np.asarray(d["lo"]) <= np.asarray(d["hi"])): bad.append("lo over hi")
    return bad
def reference(nb, qs, s0, w0, us, coin, lo, hi):
    nt = nb.reshape(N, 8, 16, V); qt = qs.astype(np.float32).astype(np.int32).reshape(N, 8, 16, V)
    u = us.astype(np.int64).reshape(N, 8, T, C); cn = coin.reshape(N, 8, T, C)
    l = lo.astype(np.float32).reshape(N, 8, 16, T); h = hi.astype(np.float32).reshape(N, 8, 16, T)
    H, W, live = start(s0.astype(np.int64), w0.astype(np.float32).reshape(N, 8, 16, C)); F = np.ones(8, np.float32)
    for t in range(T):
        old = live
        H, W, live = grow(t, H, W, live, nt, qt, u[:, :, t])
        H, W, live, up = breed(H, W, live, old, l[..., t] * F[:, None], h[..., t] * F[:, None], cn[:, :, t])
        F = np.where(up, F * np.float32(2), F)
    H = np.where(live[:, :, None], H, -1); W = np.where(live[:, :, None], W, np.float32(0))
    return {"yh": H.reshape(N, 128, C).astype(np.float32), "yw": W.reshape(N, 128, C).astype(np.float32)}

@@ -1,0 +1,799 @@
+from concourse.bass import DstId, RemoteDMATransfer
+from concourse.mybir import AluOpType, AxisListType, ActivationFunctionType
+
+ALU = AluOpType
+AF = ActivationFunctionType
+N, V, C, NT, S, DG = 8, 2048, 256, 5, 48, 5
+NONE = C
+WN = C + 2 * S + 16
+PAYN, PAYW = 2 * S + 1, 2 * S + 4
+OFFS = 2036.0
+MAGIC = 12582912.0
+RH, RC, RD, RI, MW = 0, 7 * S, 8 * S + C, 8 * S + 2 * C, 8 * S + 3 * C
+
+F32, BF, F16, I32, U16 = "float32", "bfloat16", "float16", "int32", "uint16"
+_SB = {
+    "nbt": (V, I32), "qt": (V + 16, BF), "w0s": (C, F32), "lh": (16, F32), "s0i": (C, I32), "usi": (C, I32),
+    "cni": (NT * C, I32), "s0h": (C, F16), "usb": (C, BF), "cnb": (NT * C, BF), "ub": (NT * C + WN - C, BF),
+    "ones": (640, BF), "ident": (128, BF), "bo": (128, BF), "bo1": (128, BF), "nbo": (128, BF), "l2a": (128, BF), "l2": (128, BF),
+    "dma_": (128, F32), "dm": (128, F32), "jj": (256, BF), "z8": (144, BF), "bo8a": (128, BF), "bo8": (128, BF), "zt": (640, BF),
+    "zz": (144, BF), "i11": (128, BF), "i2k": (128, BF), "ip": (128, BF), "im": (128, BF), "sel": (640, BF),
+    "bo2": (128, BF), "bo16": (128, BF), "hb_": (C, BF), "pcb": (C, BF), "bia": (12, F32), "jnk": (3 * C, BF), "mk1": (16, BF), "rb": (C + S, F32),
+    "mki": (C + S, I32), "mki2": (C + S, I32), "mask": (C + S, BF), "ids": (C, BF), "c16": (128, BF), "pci": (8, I32),
+    "pci2": (8, I32), "cc": (144, F16), "cw": (16, F32), "zr": (576, BF), "rs16": (C + S, BF), "rs32": (72, BF), "rsx": (120, F32),
+    "th": (NT * 48, F32), "thb": (NT * 16, F32),
+    "oq": (C + S, U16), "of": (C + S, F32), "xx": (16 * (C + S), BF), "ee": (16 * (C + S), BF),
+    "sg": (16 * (C + S), BF), "d0a": (1024, F16), "d0b": (1024, F16), "thr": (C + S, F32), "yy": (C + S, F32),
+    "wc": (WN, F32), "wv": (3 * WN, F32), "w1i": (S, F32), "h32": (WN, F32), "h16": (C + S, F16), "hw": (WN, F32),
+    "fl": (3 * C, BF), "fw": (72, BF), "dbl": (16, BF), "sc": (72, BF), "rr": (120, F32), "of2": (40, U16),
+    "mm_": (MW, BF), "ga": (S, BF), "gb": (C + S, BF), "ra": (S, BF), "osu": (4, U16), "oh": (20, U16),
+    "owf": (16, F32), "owu": (16, U16), "av": (16, F32), "ssm": (S, F32), "ge": (C + S, F16), "mv": (C + S, F16),
+    "hwi": (S, F32), "sm": (C + S, F16), "sn": (C + S, F16), "swu": (20, U16), "nk": (C + S, F16), "eq": (5 * C, F16), "eqi": (5 * S, F16), "uin": (S, BF),
+    "al0": (C, BF), "col": (32, F32), "dcol": (8 * NT, BF), "tmp0": (C, F32), "tmp1": (128, F32),
+    "pay": (NT * PAYW, F32), "land": (NT * PAYW, F32), "cnt": (NT * N, BF),
+}
+SCRATCH = {k: ("sbuf", [128, w], d) for k, (w, d) in _SB.items()}
+for _b in range(8):
+    SCRATCH["ps%d" % _b] = ("psum", [128, 512], F32)
+_LOADS = ["s0", "nb", "qs", "w0", "us", "coin", "lo", "hi"]
+SEMAPHORES = (["ev", "ea", "ep", "eg", "loc", "outw", "outh"] + ["ld_" + x for x in _LOADS]
+              + ["arr%d" % t for t in range(NT)] + ["cnt%d" % t for t in range(NT - 1)])
+ESEM = {"v": "ev", "a": "ea", "p": "ep", "g": "eg"}
+
+PAR = (1.04, 0.55, 1.56, 3.8, 5500.0, 7000.0, 90.0)
+LAT = 110.0
+SEED, ROUNDS, NOISE = 1, 4, 200.0
+WHO = {"gx": "avaaa", "sign": "vva", "y": "v", "cnb": "g", "big": "vvgg"}
+CHUNKS = [(0, 64), (64, 128), (128, 192), (192, 256)]
+CHUNK2 = [(0, 192), (192, 256)]
+HEADS = [(0, 64), (64, 160), (160, 256)]
+GSTEP = 32
+OPT = {"count": False, "rbv": False, "early": 3000.0, "wrapv": "il"}
+ORDER = (
+    "02090L0p010500030b0e0c0g0d0v0G060R1a0M0704080V0H1Q0X0a0f1P0r0I0W180Y1R171o1r0F0t0s0T1w1q111d191v1p1i1e1g1B1m1kvf0Z101s0S"
+    "0U1C1tvhvl0hvjvn1u1G1x0o0K0w1yv21A0OvDvEvUvV1Ww42f2526162e1X1cvFvH1Iwpwo0n1Z1Y2728200J0Q0uw9210xv32q2gw21O0i0z140N152r2s"
+    "2a1J2i0j0lwJ0m0k232H2I2M2h2bwtwj2k2u2N0P2O2P2lvzwc1b0y2Qwm2y2R2S2d2n1T1S0q2v2T2X2U2Z2z0Bww2x2Y3O1K302Wx6wK312A0E2D1M2E2B"
+    "2F37320A2Vx3wL2G2C343839yG3c1N3o3d3p3f3A3g3r3h3s3e353q3i3B3t3j3a3kxb3l3u3D3m3w3N3M4F3C3n3E3v3F0D3G3x3y3I1L0C3HxSxT433J3U"
+    "y23K3V4c443PxX463Y3Wyd4e3Q453Z474H4f4I4Z4K4J4L4M4h4N4iymyny04o4P4O4j4Q4RyT484U414V4g494p4q4X4W4Y50ykxRyS5c5dze4lxLxz515h"
+    "4ayr4sz24t5i5j4b5k4w5m534x5l544y5nyu5o5s5p5t6pz54z564v5uzgzfyA57585v4BzB5w594C4D5a5x5r4Ezq5Czy5bzz5A6o5D5E5H5I5V695F5L5W"
+    "5Z6aBh5M6d5Y5J5K6b5N605O6e5P5Q5R616f62zG5X5S6c6n7g5T6gAuAt6j6i6h6465636k666v5U676lAD6EAOAXAY6F6q6w6N6y6GA86z6I6A6P6J6Q6x"
+    "7i6K7j7k7l7mAS7n7o6r6ZAL7p6T7s7q707rAsAm7t6UB27u7C7x6R716VBw6M7y6H7A737B7zABBR7P7Q6W6CBS74Bv7U77787W7VBF7G7X7D7Y7Z7HB580"
+    "798182BI767E7a7J877c7K7dBTBbC3Ce7L887e7MBf897N8a7O8fCb8c848d9Z858g8A8k8Q8B8l8F8p8q8R8V8r8n868m8S8o9698E08G8h8s8H8i8u8w8I"
+    "8t8v978D8E8C8x8L8J8M8WCj8y8X8KCz8Y8U8T8NDc8Z90918O92DmDn9d939e948P959Q9o9ga1a29fDwDxa6a4a5a3ana79h9pa8DGDH9ia99r9yab9qaa"
+    "acad9jaeafEhEiao9s9z9I9t9k9B999a9A9K9CDuaj9J9DalakDbamaAaB9Lag9MECaq9NDE9l9vaFapaGaraHaIasaJDO9F9RaKaL9SaMEtaNaQ9P9TauaS"
+    "DUEDEZ9Vav9WawaT9XaxaPaUDYayaVEOazaRbZb0EWaXEEb1aYbYb2bnb5bFbob6bGbtGRbbbXcQbqbabcbLbdbubpb7b8b9bJbHbIbrbebvb3bMbiF4bwbj"
+    "bfbAbNbsbKbgbhbkbObBbTbxbSbPbybzbRblbQbCc3G4bUbDbVceGdc5cfcocgc0c6c7c8cScic9cjcTcYGxcZchd0ckd1cXcUcVcWd6d4d5d3d2Gncpcacq"
+    "GyFWd7czd8GlcbGscmcAc1d9ctcrcuHbHabmcvcBGCdgdccccwG2cDdedddfFEHhHtdrdscEdidwcHcIdxdydzdAdjdBdCcJdDGFHkdEcGdlcKHudHdmcMdn"
+    "cNdIdFdJdodpGLcOcPdKHLdqdMHOdPdQdGdRHvdNdVdSHTdUdXdWdYdZ")
+
+
+def A(name, c0=0, c1=None, st=1, p0=0, p1=128):
+    if c1 is None:
+        c1 = _SB[name][0] if name in _SB else 512
+    return (name, p0, p1, c0, c1, st)
+
+
+def nel(r):
+    return 16 * nel(r[2]) if r[0] == "#" else len(range(r[3], r[4], r[5]))
+
+
+def IND(win, off):
+    return ("#", win, off)
+
+
+def wide(r):
+    r = r[1] if r[0] == "#" else r
+    return r[0] not in _SB or _SB[r[0]][1] in (F32, I32)
+
+
+def parts(r):
+    if not isinstance(r, tuple):
+        return []
+    return [r[1], r[2]] if r[0] == "#" else [r]
+
+
+def build(T, rank, par=PAR):
+    CY, PCY, GR, SCR, HOP2, HOPC, FIXA = par
+    ops = []
+    early = [0.0]
+
+    def ap(r):
+        if not isinstance(r, tuple):
+            return r
+        if r[0] == "#":
+            return ap(r[1]).indirect(ap(r[2]))
+        if r[5] == 1:
+            return T[r[0]][r[1]:r[2], r[3]:r[4]]
+        return T[r[0]][r[1]:r[2], r[3]:r[4]:r[5]]
+
+    def add(alts, reads, writes, tag="", **kw):
+        rd = [x for r in reads for x in parts(r)]
+        wr = []
+        for r in writes:
+            if r[0] == "#":
+                wr.append(r[1]); rd.append(r[2])
+            else:
+                wr.append(r)
+        o = dict(alts=alts, rd=rd, wr=wr, tag=tag, eng=None, early=early[0])
+        o.update(kw)
+        ops.append(o)
+        return o
+
+    def vcost(out, ins, two=False):
+        if out[0] == "#":
+            return 50 + nel(out) * SCR * CY
+        if ins and ins[0][0] == "#":
+            return 50 + nel(out) * GR * CY
+        n = nel(out)
+        rate = 1.0 if any(wide(r) for r in [out] + ins) else 0.5
+        if two and all(r[0] in _SB for r in ins):
+            rate *= 2
+        return 20 + max(64, n * rate) * CY
+
+    def acost(out, in_):
+        return 65 + nel(out) * GR * CY if in_[0] == "#" else FIXA + nel(out) * CY
+
+    def copy(out, in_, eng="v", tag=""):
+        alts = {}
+        if "v" in eng:
+            alts["v"] = (vcost(out, [in_]), lambda q: q.tensor_copy(ap(out), ap(in_)))
+        if "a" in eng:
+            alts["a"] = (acost(out, in_), lambda q: q.activation(ap(out), ap(in_), AF.Identity))
+        if "g" in eng:
+            alts["g"] = (170 + 2 * CY * nel(out), lambda q: q.affine_select(ap(out), ap(in_), [[0, nel(out)]], ALU.is_ge, 0.0, 0, 0))
+        return add(alts, [in_], [out], tag)
+
+    def ts(out, in0, s1, s2, op0, op1=None, tag="", act=None):
+        if op1 is None:
+            f = lambda q: q.tensor_scalar(ap(out), ap(in0), ap(s1), None, op0)
+        else:
+            f = lambda q: q.tensor_scalar(ap(out), ap(in0), ap(s1), ap(s2), op0, op1)
+        alts = {"v": (vcost(out, [in0]), f)}
+        if act is not None:
+            alts["a"] = (acost(out, in0), lambda q: q.activation(ap(out), ap(in0), act[0], bias=ap(act[1]), scale=ap(act[2])))
+        return add(alts, [in0, s1, s2], [out], tag)
+
+    def tt(out, in0, in1, op, tag=""):
+        return add({"v": (vcost(out, [in0, in1], True), lambda q: q.tensor_tensor(ap(out), ap(in0), ap(in1), op))}, [in0, in1], [out], tag)
+
+    def scan(out, d0, d1, init, op0, op1, tag=""):
+        return add({"v": (vcost(out, [d0, d1]), lambda q: q.tensor_tensor_scan(ap(out), ap(d0), ap(d1), init, op0, op1))}, [d0, d1], [out], tag)
+
+    def memset(out, val, tag=""):
+        return add({"v": (vcost(out, []), lambda q: q.memset(ap(out), val))}, [], [out], tag)
+
+    def reduce_(out, in_, tag=""):
+        return add({"v": (20 + max(64, nel(in_)) * CY, lambda q: q.tensor_reduce(ap(out), ap(in_), AxisListType.X, ALU.add))}, [in_], [out], tag)
+
+    def act(out, in_, func, bias=0.0, scale=1.0, accum=None, tag=""):
+        if accum is None:
+            f = lambda q: q.activation(ap(out), ap(in_), func, bias=ap(bias), scale=ap(scale))
+        else:
+            f = lambda q: q.activation(ap(out), ap(in_), func, bias=ap(bias), scale=ap(scale), accum_out=ap(accum))
+        return add({"a": (acost(out, in_), f)}, [in_, bias, scale], [out] + ([accum] if accum else []), tag)
+
+    def mm(trip, tag="", extra=None, opens=True, closes=True):
+        def f(q):
+            tr = trip + (extra[0]() if extra else [])
+            r = None
+            for i, (o, l, x) in enumerate(tr):
+                r = q.matmul(ap(o), ap(l), ap(x), opens and i == 0, closes and i == len(tr) - 1)
+            return r
+        cost = 60 + sum(max(64, nel(x)) * (4 if wide(x) else 1) * PCY for _, _, x in trip)
+        return add({"p": (cost, f)}, [r for tr in trip for r in tr[1:]] + (extra[1] if extra else []), [tr[0] for tr in trip], tag)
+
+    def iota(out, pat, base, cm, tag=""):
+        if _SB[out[0]][1] == I32:
+            f = lambda q: q.iota(ap(out), pat, base, cm)
+        else:
+            f = lambda q: q.iota(ap(out), pat, base, cm, allow_small_or_imprecise_dtypes=True)
+        return add({"g": (130 + 2 * CY * nel(out), f)}, [], [out], tag)
+
+    def sel(out, in_, pat, cmp_, fill, base, cm, tag=""):
+        return add({"g": (170 + 2 * CY * nel(out), lambda q: q.affine_select(ap(out), ap(in_), pat, cmp_, fill, base, cm))}, [in_], [out], tag)
+
+    rot = (-DG * rank) % 8
+
+    def pieces(rows):
+        if rot == 0:
+            return [(0, 0, 8 * rows)]
+        return [(0, rot * rows, (8 - rot) * rows), ((8 - rot) * rows, 0, rot * rows)]
+
+    def load(name, buf, c0, c1, rows_h, rows_c, q, lat):
+        ph, pc = pieces(rows_h), pieces(rows_c)
+
+        def f(e):
+            for (h0, _, hn), (_, s0, sn) in zip(ph, pc):
+                e.dma_start(T[buf][s0:s0 + sn, c0:c1], T[name][h0:h0 + hn, :]).then_inc(T.sem["ld_" + name], 16)
+        return add({q: (60.0 * len(ph), f)}, [], [A(buf, c0, c1)], "ld" + name, done=("ld_" + name, 16 * len(ph)), lat=lat)
+
+    def store(name, buf, q, sem):
+        def f(e):
+            for h0, s0, n in pieces(16):
+                e.dma_start(T[name][h0:h0 + n, :], T[buf][s0:s0 + n, 0:C]).then_inc(T.sem[sem], 16)
+        return add({q: (120.0, f)}, [A(buf, 0, C)], [], "st" + name, done=(sem, 16 * len(pieces(16))), lat=2500.0)
+
+    def O(b):
+        return A("zz", 15 - b, 143 - b)
+
+    def O8(b):
+        return A("z8", 15 - b, 143 - b, 1, 0, 8)
+
+    load("s0", "s0i", 0, C, 1, 1, "s", 2000.0)
+    load("nb", "nbt", 0, V, 16, 16, "s", 5000.0)
+    load("qs", "qt", 16, V + 16, 16, 16, "a", 5500.0)
+    load("us", "usi", 0, C, 1, NT, "a", 3000.0)
+    load("w0", "w0s", 0, C, 16, 16, "s", 5500.0)
+    load("coin", "cni", 0, NT * C, 1, 1, "s", 5500.0)
+    memset(A("lh"), 0.0)
+    load("lo", "lh", 0, NT, 16, 16, "s", 5500.0)
+    load("hi", "lh", 8, 8 + NT, 16, 16, "s", 5500.0)
+    memset(A("ones"), 1.0)
+    memset(A("qt", 0, 16), 0.0)
+    sel(A("z8", p1=8), A("ones", 0, 144, p1=8), [[1, 144]], ALU.is_equal, 0.0, -15, -16)
+    sel(A("bo8a", p1=8), A("ones", 0, 128, p1=8), [[1, 128]], ALU.is_ge, 0.0, 0, -16)
+    sel(A("bo8", p1=8), A("bo8a", p1=8), [[-1, 128]], ALU.is_ge, 0.0, 15, 16)
+    sel(A("ident"), A("ones", 0, 128), [[-1, 128]], ALU.is_equal, 0.0, 0, 1)
+    sel(A("zt", p1=40), A("ones", p1=40), [[-1, NT], [-NT, 8], [0, 16]], ALU.is_equal, 0.0, 0, 1)
+    sel(A("bo1"), A("ones", 0, 128), [[-16, 8], [0, 16]], ALU.is_ge, 0.0, 0, 1)
+    sel(A("bo"), A("bo1"), [[16, 8], [0, 16]], ALU.is_ge, 0.0, 15, -1)
+    ts(A("nbo"), A("bo"), -1.0, None, ALU.mult)
+    sel(A("dma_"), A("nbo"), [[-1, 128]], ALU.is_equal, 0.0, -1, 1)
+    sel(A("dm"), A("dma_"), [[-1, 128]], ALU.not_equal, 1.0, 0, 1)
+    sel(A("l2a"), A("nbo"), [[-1, 128]], ALU.is_gt, 0.0, 0, 1)
+    sel(A("l2"), A("l2a"), [[-1, 128]], ALU.not_equal, -1024.0, 0, 1)
+    nmk = C + S if OPT["rbv"] else 2 * S if "l" in OPT["wrapv"] else S
+    iota(A("mki", 0, nmk), [[0, nmk // 16], [-1, 16]], 16, 1)
+    iota(A("ids"), [[1, C]], 0, 0)
+    iota(A("pci"), [[0, 8]], 0, 1)
+    sel(A("jj"), A("ones", 0, 256), [[0, 2], [-1, 128]], ALU.is_equal, 0.0, 0, 1)
+    ts(A("i11"), A("ident"), 2.0 ** -11, None, ALU.mult)
+    ts(A("i2k"), A("ident"), -4096.0, None, ALU.mult)
+    ts(A("ip"), A("ident"), 16.0 * WN, None, ALU.mult)
+    ts(A("im"), A("ident"), -16.0 * WN, None, ALU.mult)
+    memset(A("zz"), 0.0)
+    copy(A("zz", 15, 143, 16), A("bo", 0, 128, 16))
+    ts(A("mki2", 0, nmk), A("mki", 0, nmk), 15, None, ALU.bitwise_and)
+    ts(A("mk1"), A("mki2", 0, 16), 0.0, None, ALU.is_equal)
+    if OPT["rbv"]:
+        ts(A("mask"), A("mki2"), 0.0, 16.0, ALU.is_equal, ALU.mult)
+    else:
+        ts(A("mask", 0, nmk), A("mki2", 0, nmk), 0.0, None, ALU.is_equal)
+    for p in range(5):
+        ts(A("sel", 128 * p, 128 * p + 128), A("bo"), A("mk1", p, p + 1), None, ALU.mult)
+    memset(A("c16"), 16.0)
+    ts(A("pci2"), A("pci"), 15, None, ALU.bitwise_and)
+    copy(A("col", 0, 1), A("pci2", 0, 1))
+    ts(A("col", 1, 2), A("col", 0, 1), 15.0, 18.0, ALU.is_lt, ALU.mult)
+    ts(A("col", 2, 3), A("col", 1, 2), -1.0, None, ALU.add)
+    ts(A("cw"), A("ids", 0, C, 16), A("col", 0, 1), None, ALU.add)
+    memset(A("cc"), 1023.0 + RC)
+    memset(A("cc", 0, 48, 3), 1023.0)
+    ts(A("cc", 2, 48, 3), A("cw"), float(RD), None, ALU.add)
+    ts(A("cc", 50, 96, 3), A("cw"), float(RI), None, ALU.add)
+    copy(A("cc", 98, 108, 3), A("cw", 0, 4))
+    ts(A("cc", 110, 120, 3), A("cw", 0, 4), float(RC), None, ALU.add)
+    memset(A("cc", 120, 136), 16.0 * WN)
+    memset(A("cc", 136, 144), 0.0)
+    memset(A("rs16"), 1.0); memset(A("rs16", 0, C + S, 16), 0.0)
+    if OPT["count"]:
+        ts(A("bo2"), A("bo"), -2.0, None, ALU.mult)
+        ts(A("bo16", p1=8), A("bo8", p1=8), -16.0, None, ALU.mult)
+        memset(A("col", 15, 16), 23.5)
+        ts(A("bia", 4, 7), A("cw", 0, 3), 2.0, C + 1.0, ALU.mult, ALU.add)
+    memset(A("rs32"), 1.0); memset(A("rs32", 0, 72, 52), 0.0)
+    memset(A("fw"), 0.0)
+    memset(A("rsx"), 0.0); memset(A("rsx", 0, 120, 3), 4096.0)
+    for t in range(1, NT if OPT["wrapv"] != "il" else 0):
+        ts(A("zr", 144 * (t - 1), 144 * t), A("zz"), A("mk1", t, t + 1), None, ALU.mult)
+    for name in ("d0a", "d0b"):
+        for a in (0, 512):
+            o = memset(A(name, a, a + 512), 8192.0, "big")
+            o["alts"]["g"] = sel(A(name, a, a + 512), A("ones", 0, 512), [[0, 512]], ALU.is_gt, 8192.0, 0, 0)["alts"]["g"]
+            o["rd"] = ops.pop()["rd"]
+    memset(A("ub", NT * C, NT * C + WN - C), 0.0)
+    memset(A("wv", C, WN), 0.0); memset(A("wv", WN + C, 2 * WN), 0.0)
+    memset(A("hw", C, WN), -1.0);
+    memset(A("wc", C, WN), 0.0); memset(A("h32", C, WN), 0.0)
+    memset(A("th"), 9.0)
+    copy(A("mm_", RD, RI), A("ids"), "va"); copy(A("mm_", RI, MW), A("ids"), "va")
+    ts(A("usb", p1=40), A("usi", p1=40), -8.0, None, ALU.mult)
+    for t in range(NT):
+        bank = A(["ps2", "ps4", "ps4", "ps5", "ps5"][t], [0, 0, 256, 0, 256][t], [256, 256, 512, 256, 512][t])
+        mm([(bank, A("zt", 128 * t, 128 * t + 128, 1, 0, 40), A("usb", p1=40))])
+        copy(A("ub", C * t, C * t + C), bank, "va")
+    ts(A("s0h", p1=8), A("s0i", p1=8), 1.0, None, ALU.add)
+    s0h = A("s0h", p1=8)
+    mm([(A("ps3", 320, 336), O8(b), A("s0h", b, C, 16, 0, 8)) for b in range(16)])
+    mm([(A("ps6", 0, C), A("bo8", p1=8), s0h)])
+    mm([(A("ps1", 0, C), O8(0), s0h)])
+    ts(A("swu", 0, 16), A("ps3", 320, 336), -1.0, None, ALU.add)
+    ts(A("nk", 0, C), IND(A("nbt"), A("swu", 0, 16)), 1.0, None, ALU.add)
+    tt(A("eq", 0, C), A("nk", 0, C), A("ps6", 0, C), ALU.is_equal)
+    ts(A("tmp0"), A("ps6", 0, C), 0.0, None, ALU.is_gt)
+    copy(A("h16", 0, C), A("ps1", 0, C))
+    mm([(A("ps1", C, 2 * C), A("ident"), A("nk", 0, C)), (A("ps1", C, 2 * C), A("i2k"), A("eq", 0, C))])
+    ts(A("oq", 0, C), A("ps1", C, 2 * C), 0.0, 15.0, ALU.max, ALU.add)
+    ts(A("of", 0, C), A("ps1", C, 2 * C), 0.0, None, ALU.max, act=(AF.Relu, 0.0, 1.0))
+    tt(A("wc", 0, C), A("w0s"), A("tmp0"), ALU.mult)
+    act(A("al0"), A("tmp0"), AF.Identity, accum=A("col", 4, 5))
+    ts(A("col", 8, 9), A("col", 4, 5), -float(C), None, ALU.add)
+    for t in range(NT):
+        copy(A("cnb", C * t, C * t + C, 1, 0, 8), A("cni", C * t, C * t + C, 1, 0, 8), "vg", "cnb")
+    mm([(A("ps7", 0, 80), O8(b), A("cnb", b, NT * C, 16, 0, 8)) for b in range(16)])
+    for t in range(NT):
+        ts(A("th", 48 * t, 48 * t + 16), A("ps7", 16 * t, 16 * t + 16), 90.0, 9.0, ALU.mult, ALU.add)
+    ts(A("thb"), A("ps7", 0, 80), -90.0, 99.0, ALU.mult, ALU.add)
+
+    nd0 = [0]
+
+    def grow1(t, c0, c1, fb, ucol, step):
+        for a in range(c0, c1, step):
+            copy(A("xx", 16 * a, 16 * (a + step)), IND(A("qt"), A("oq", a, a + step)), "va", "gx")
+        mm([(fb, A("i11"), A("xx", 16 * c0 + k, 16 * c1, 16)) for k in range(16)], "f")
+        tt(A("thr", c0, c1), fb, ucol, ALU.mult, "thr")
+
+    def grow2(c0, c1, vb):
+        d0 = ["d0a", "d0b"][nd0[0] % 2]; nd0[0] += 1
+        n = 16 * (c1 - c0)
+        y = OFFS + 255.0 / 512.0
+        ts(A("yy", c0, c1), A("thr", c0, c1), y, None, ALU.add, tag="y", act=(AF.Identity, A("col", 13, 14), 1.0))["rd"].append(A("col", 13, 14))
+        ts(A(d0, 0, n, 16), A("yy", c0, c1), MAGIC, -MAGIC, ALU.add, ALU.add, tag="d0")
+        scan(A("ee", 16 * c0, 16 * c1), A(d0, 0, n), A("xx", 16 * c0, 16 * c1), 4096.0, ALU.min, ALU.add, "scan")
+        so = ts(A("sg", 16 * c0, 16 * c1), A("ee", 16 * c0, 16 * c1), OFFS, 2.0, ALU.is_gt, ALU.mult, "sign", act=(AF.Sign, A("col", 12, 13), 1.0))
+        so["rd"].append(A("col", 12, 13))
+        ex = (lambda: [(vb, A("ident"), A("c16", 0, c1 - c0))] if so["eng"] == "a" else [], [A("ident"), A("c16")])
+        mm([(vb, O(k), A("sg", 16 * c0 + k, 16 * c1, 16)) for k in range(15)], "V", ex)
+
+    def sites(t, c0, c1, vb, dn, ph, hw, x):
+        ge, mv = A("ge", c0, c1), A("mv", c0, c1)
+        ts(ge, vb, A("col", 2, 3), None, ALU.is_gt, tag="ge" + x)
+        tt(mv, dn, ge, ALU.mult, "mv" + x)
+        mm([(ph, A("ident"), A("h16", c0, c1)), (ph, O(t + 1), mv)], "hnew" + x)
+        if t == NT - 1:
+            ts(hw, ph, -1.0, None, ALU.add, tag="hw" + x, act=(AF.Identity, A("col", 14, 15), 1.0))["rd"].append(A("col", 14, 15))
+        else:
+            copy(hw, ph, "va", "hw" + x)
+
+    def head(t, c0, c1, pw, hb, po, eq, x):
+        swu, nk = A("swu", c0 // 16, c1 // 16), A("nk", c0, c1)
+        byv = ("i" if x else "l") in OPT["wrapv"]
+        if not byv:
+            mm([(pw, A("zr", 144 * (t - 1) + 15 - b, 144 * (t - 1) + 143 - b), A("h16", c0 + b, c1, 16)) for b in range(16)], "siw" + x)
+        for p in range(t, -1, -1):
+            mm([(hb[p], A("sel", 128 * p, 128 * p + 128), A("h16", c0, c1))], "hb" + x)
+        if byv:
+            tt(A("sm", c0, c1), hb[t], A("mask", 0, c1 - c0), ALU.mult, "sm" + x)
+            scan(A("sn", c0, c1), A("rs16", 0, c1 - c0), A("sm", c0, c1), 0.0, ALU.mult, ALU.add, "sn" + x)
+            pw = A("sn", c0 + 15, c1, 16)
+        ts(swu, pw, -1.0, None, ALU.add, tag="swu" + x)
+        ts(nk, IND(A("nbt"), swu), 1.0, None, ALU.add, tag="nk" + x)
+        for p in range(t + 1):
+            tt(eq[p], nk, hb[p], ALU.is_equal, "eq" + x)
+        mm([(po, A("ident"), nk)] + [(po, A("i2k"), r) for r in eq], "o" + x)
+        ts(A("oq", c0, c1), po, 0.0, 15.0, ALU.max, ALU.add, tag="oq" + x)
+        ts(A("of", c0, c1), po, 0.0, None, ALU.max, tag="of" + x, act=(AF.Relu, 0.0, 1.0))
+
+    memset(A("col", 12, 13), -OFFS)
+    memset(A("col", 13, 14), OFFS + 255.0 / 512.0)
+    memset(A("col", 14, 15), -1.0)
+    HL = A("oh", 16, 19)
+    for t in range(NT):
+        last = t == NT - 1
+        P0 = t * PAYW
+        L0 = (t - 1) * PAYW
+        iota(A("mm_", 0, RC), [[0, RC // S], [2, S]], NONE + 2, 0, "refill")
+        iota(A("mm_", RC, RD), [[0, RD - RC]], NONE, 0, "refill")
+        if t > 0:
+            add({}, [], [A("cnt", N * (t - 1), N * t)], "arrc", done=("cnt%d" % (t - 1), None), lat=HOPC, after="sc%d" % (t - 1))
+            tr = []
+            for r in range(N):
+                s = (-16 * DG * (r - rank)) % 128
+                x = A("dcol", 8 * (t - 1), 8 * (t - 1) + 1) if r == rank else A("cnt", N * (t - 1) + r, N * (t - 1) + r + 1)
+                tr.append((A("ps3", 304, 305), A("jj", s, s + 128), x))
+            mm(tr, "tot")
+            ts(A("col", 16, 17), A("ps3", 304, 305), 0.0, 1.0, ALU.is_gt, ALU.add, tag="up")
+            ts(A("lh"), A("lh"), A("col", 16, 17), None, ALU.mult, tag="lh", act=(AF.Identity, 0.0, A("col", 16, 17)))
+        for i, (c0, c1) in enumerate(CHUNKS):
+            early[0] = 1.0 - c1 / C
+            fb = A("ps%d" % (i % 2), c0, c1)
+            grow1(t, c0, c1, fb, A("ub", C * t + c0, C * t + c1), GSTEP)
+            tt(A("wv", WN + c0, WN + c1), fb, A("wc", c0, c1), ALU.mult, "w1")
+            grow2(c0, c1, A("ps2", c0, c1))
+        mm([(A("ps3", 0, C), A("dm"), A("of", 0, C))], "dn")
+        for c0, c1 in CHUNK2:
+            early[0] = 1.0 - c1 / C
+            sites(t, c0, c1, A("ps2", c0, c1), A("ps3", c0, c1), A("ps0", C + c0, C + c1), A("hw", c0, c1), "")
+        if t > 0:
+            add({}, [], [A("land", L0, L0 + PAYW)], "arr", done=("arr%d" % (t - 1), None), lat=HOP2, after="sp%d" % (t - 1))
+            copy(A("uin"), IND(A("ub", C * t, C * t + WN), HL), "va", "uin")
+            copy(A("h16", C, C + S), A("land", L0 + S, L0 + 2 * S), tag="hi16")
+            head(t, C, C + S, A("ps3", 504, 507), [A("ps7", S * p, S * p + S) for p in range(t + 1)], A("ps3", 456, 504),
+                 [A("eqi", S * p, S * p + S) for p in range(t + 1)], "i")
+            fb = A("ps7", 240, 288)
+            grow1(t, C, C + S, fb, A("uin"), 24)
+            tt(A("w1i"), fb, A("land", L0, L0 + S), ALU.mult, "w1i")
+            copy(IND(A("wv", WN, 2 * WN), HL), A("w1i"), tag="scw")
+            if not last:
+                ts(A("col", 20, 21), A("land", L0 + 2 * S, L0 + 2 * S + 1), 0.0, float(S), ALU.max, ALU.min, tag="nin")
+                ts(A("col", 8, 9), A("col", 20, 21), A("pay", L0 + 2 * S, L0 + 2 * S + 1), 0.0, ALU.add, ALU.min, tag="db")
+            mm([(A("ps3", 360, 408), A("dm"), A("of", C, C + S))], "dni")
+            grow2(C, C + S, A("ps3", C, C + S))
+            sites(t, C, C + S, A("ps3", C, C + S), A("ps3", 360, 408), A("ps3", 408, 456), A("hwi"), "i")
+            copy(IND(A("hw"), HL), A("hwi"), tag="sch")
+        W1 = A("wv", WN, WN + C)
+        ts(A("fl", 2 * C, 3 * C), W1, A("lh", 8 + t, 9 + t), None, ALU.is_gt, tag="ch")
+        ts(A("fl", 0, C), W1, A("lh", t, t + 1), None, ALU.is_lt, tag="cl")
+        ts(A("fl", C, 2 * C), W1, 0.0, None, ALU.is_gt, tag="al", act=(AF.Sign, 0.0, 1.0))
+        ts(A("wv", 0, C), W1, 0.5, None, ALU.mult, tag="half", act=(AF.Identity, 0.0, 0.5))
+        ts(A("wv", 2 * WN, 2 * WN + C), W1, 2.0, None, ALU.mult, tag="twice", act=(AF.Identity, 0.0, 2.0))
+        mm([(A("ps7", 288, 336), O(b), A("fl", b, 3 * C, 16)) for b in range(16)], "pw")
+        tt(A("fw", 20, 68), A("ps7", 288, 336), A("th", 48 * t, 48 * t + 48), ALU.is_ge, "fw")
+        tt(A("dbl"), A("ps7", 288, 304), A("thb", 16 * t, 16 * t + 16), ALU.is_ge, "dbl")
+        die, alive, high, hole = A("fw", 20, 36), A("fw", 36, 52), A("fw", 52, 68), A("fw", 0, 16)
+        tt(hole, die, alive, ALU.is_ge, "hole")
+        scan(A("sc"), A("rs32"), A("fw"), 0.0, ALU.mult, ALU.add, "sc")
+        X = 368
+        sh, sc_ = A("sc", 0, 16), A("sc", 52, 68)
+        xa, xb, xc, xv = A("ps7", X, X + 48, 3), A("ps7", X + 1, X + 48, 3), A("ps7", X + 48, X + 96, 3), A("ps7", X + 120, X + 136)
+        ex = A("ps7", X + 136, X + 137)
+        mm([(A("ps7", X, X + 144), A("ident"), A("cc")),
+            (xv, A("ip"), A("dbl")), (xv, A("im"), die), (xv, A("im"), high),
+            (xb, A("l2"), high), (xa, A("l2"), hole), (xc, A("l2"), hole)], "px0", closes=False)
+        mm([(xa, A("bo"), sh), (xb, A("bo"), sc_), (xc, A("bo"), sh),
+            (A("ps7", X + 98, X + 108, 3), A("bo"), A("sc", 68, 72)), (A("ps7", X + 110, X + 120, 3), A("bo"), A("sc", 16, 20)),
+            (ex, A("bo"), A("sc", 68, 69)), (ex, A("nbo"), A("sc", 16, 17))], "px", opens=False)
+        scan(A("rr"), A("rsx"), A("ps7", X, X + 120), 0.0, ALU.max, ALU.min, "rr")
+        copy(A("of2"), A("rr", 2, 120, 3), tag="of2")
+        ec = A("pay", P0 + 2 * S, P0 + 2 * S + 1)
+        copy(ec, ex, "va", "e")
+        tt(A("av"), xv, alive, ALU.mult, "av")
+        if not last:
+            dc = A("dcol", 8 * t, 8 * t + 1)
+            ts(dc, ex, A("col", 8, 9), None, ALU.subtract, tag="d")
+            add({"g": (1200.0, ("cnt", t))}, [dc], [], "sc%d" % t, remote=True)
+        copy(IND(A("mm_"), A("of2", 0, 16)), A("ids"), tag="scat")
+        if OPT["count"]:
+            mm([(A("ps0", 0, C), A("bo"), A("fl", 2 * C, 3 * C))], "bh")
+            mm([(A("ps1", 0, C), A("bo"), A("fl", 0, C)), (A("ps1", 0, C), A("bo2"), A("fl", C, 2 * C)),
+                (A("ps1", 0, C), A("bo16", p1=8), A("cnb", C * t, C * t + C, 1, 0, 8))], "ba")
+            ts(A("hb_"), A("ps0", 0, C), 9.0, None, ALU.is_ge, tag="hb_")
+            scan(A("pcb"), A("ones", 0, C), A("hb_"), 0.0, ALU.mult, ALU.add, "pcb")
+            act(A("al0"), A("ps1", 0, C), AF.Sign, bias=A("col", 15, 16), accum=A("col", 24, 25), tag="nhb")
+            ts(A("bia", 0, 3), A("bia", 4, 7), A("col", 24, 25), None, ALU.add, tag="bia", act=(AF.Identity, A("col", 24, 25), 1.0))
+            for a in range(3):
+                act(A("jnk", C * a, C * a + C), A("pcb"), AF.Sign, bias=A("bia", a, a + 1), scale=-2.0, accum=A("bia", 8 + a, 9 + a), tag="cnt")
+            ts(A("osu", 0, 3), A("bia", 8, 11), 0.5, C / 2.0, ALU.mult, ALU.add, tag="osu")
+        else:
+            tt(A("ga"), IND(A("mm_"), A("of2", 36, 39)), A("mask", 0, S), ALU.mult, "ga")
+            scan(A("ra"), A("rs16", 0, S), A("ga"), 0.0, ALU.mult, ALU.add, "ra")
+            copy(A("osu", 0, 3), A("ra", 15, S, 16), tag="osu")
+        OS = A("osu", 0, 3)
+        copy(A("pay", P0, P0 + S), IND(A("wv", 0, WN), OS), "va", "payw")
+        copy(A("pay", P0 + S, P0 + 2 * S), IND(A("hw"), OS), "va", "payh")
+        add({"g": (1200.0, ("pay", t))}, [A("pay", P0, P0 + 2 * S + 1)], [], "sp%d" % t, remote=True)
+        if OPT["rbv"]:
+            tt(A("gb"), IND(A("mm_"), A("of2", 16, 35)), A("mask"), ALU.mult, "gb")
+            scan(A("rb"), A("rs16"), A("gb"), 0.0, ALU.mult, ALU.add, "rb")
+            rb = lambda n: A("rb", 15, 16 * n, 16)
+        else:
+            copy(A("gb"), IND(A("mm_"), A("of2", 16, 35)), "va", "gb")
+            mm([(A("ps3", 340, 359), O(b), A("gb", b, S + C, 16)) for b in range(16)], "rb")
+            rb = lambda n: A("ps3", 340, 340 + n)
+        ts(A("oh", 0, 19), rb(19), 1.0 / 16, None, ALU.mult, tag="oh")
+        tt(A("owf"), rb(16), A("av"), ALU.add, "owf")
+        ts(A("owu"), A("owf"), 1.0 / 16, None, ALU.mult, tag="owu")
+        copy(A("wc", 0, C), IND(A("wv", 0, 2 * WN + C), A("owu")), "va", "wc")
+        if last:
+            copy(A("h32", 0, C), IND(A("hw"), A("oh", 0, 16)), "va", "h32")
+        else:
+            for j, (c0, c1) in enumerate(HEADS):
+                early[0] = 1.0 - c1 / C
+                bank, w = "ps%d" % (4 + j), c1 - c0
+                copy(A("h16", c0, c1), IND(A("hw"), A("oh", c0 // 16, c1 // 16)), tag="h16")
+                head(t + 1, c0, c1, A(bank, 500, 500 + w // 16), [A(bank, w * p, w * p + w) for p in range(t + 2)], A("ps1", C + c0, C + c1),
+                     [A("eq", C * p + c0, C * p + c1) for p in range(t + 2)], "")
+    L0 = (NT - 1) * PAYW
+    add({}, [], [A("land", L0, L0 + PAYW)], "arr", done=("arr%d" % (NT - 1), None), lat=HOP2, after="sp%d" % (NT - 1))
+    copy(IND(A("wc"), HL), A("land", L0, L0 + S), tag="scw")
+    copy(IND(A("h32"), HL), A("land", L0 + S, L0 + 2 * S), tag="sch")
+    store("yw", "wc", "s", "outw")
+    store("yh", "h32", "a", "outh")
+    return ops
+
+
+def meet(a, b):
+    if a[0] != b[0] or a[4] <= b[3] or b[4] <= a[3]:
+        return False
+    if a[5] == b[5] and a[5] > 1 and (a[3] - b[3]) % a[5] != 0:
+        return False
+    return True
+
+
+def needs(ops):
+    byname, tags = {}, {}
+    for i, o in enumerate(ops):
+        tags[o["tag"]] = i
+        hard = set()
+        for kind, refs in (("r", o["rd"]), ("w", o["wr"])):
+            for r in refs:
+                for j, k2, r2 in byname.get(r[0], []):
+                    if j != i and (kind == "w" or k2 == "w") and meet(r, r2):
+                        hard.add(j)
+        for kind, refs in (("r", o["rd"]), ("w", o["wr"])):
+            for r in refs:
+                byname.setdefault(r[0], []).append((i, kind, r))
+        if "after" in o:
+            hard.add(tags[o["after"]])
+        o["banks"] = sorted(set(r[0] for r in o["rd"] + o["wr"] if r[0] not in _SB))
+        far = set()
+        for j in hard:
+            far |= ops[j]["hard"]
+        o["hard"] = hard
+        o["near"] = sorted(hard - far)
+
+
+def place(ops, prio, eng):
+    n = len(ops)
+    left = [len(o["near"]) for o in ops]
+    users = [[] for _ in ops]
+    for i, o in enumerate(ops):
+        for j in o["near"]:
+            users[j].append(i)
+    ready = [i for i in range(n) if left[i] == 0]
+    busy = {e: [] for e in "vapgs"}
+    bank = {"ps%d" % b: [] for b in range(8)}
+    start, end = [0.0] * n, [0.0] * n
+    while ready:
+        i = max(ready, key=lambda k: (prio[k], -k))
+        ready.remove(i)
+        o, e = ops[i], eng[i]
+        t0 = 0.0
+        for j in o["near"]:
+            t0 = max(t0, end[j] + (0.0 if eng[j] == e == "p" or e is None else LAT))
+        if e is None:
+            start[i], end[i] = t0, t0 + o["lat"]
+        else:
+            c = o["alts"][e][0]
+            taken = [x for x in busy[e] if x[1] > t0]
+            for b in o["banks"]:
+                taken += [(s - LAT, f + LAT) for s, f, e2 in bank[b] if e2 != e and f + LAT > t0]
+            for s, f in sorted(taken):
+                if s >= t0 + c:
+                    break
+                t0 = max(t0, f)
+            start[i], end[i] = t0, t0 + c + o.get("lat", 0.0)
+            busy[e].append((t0, t0 + c))
+            for b in o["banks"]:
+                bank[b].append((t0, t0 + c, e))
+        for k in users[i]:
+            left[k] -= 1
+            if left[k] == 0:
+                ready.append(k)
+    return sorted(range(n), key=lambda k: (start[k], k))
+
+
+def links(ops, order, eng):
+    last, lastb, before, soft = {}, {}, [None] * len(ops), [[] for _ in ops]
+    for i in order:
+        e = eng[i]
+        if e is not None:
+            before[i] = last.get(e)
+            last[e] = i
+        for b in ops[i]["banks"]:
+            d = lastb.setdefault(b, {})
+            soft[i] += [j for e2, j in d.items() if e2 != e]
+            d[e] = i
+    return before, soft
+
+
+def replay(ops, order, eng, lat=LAT):
+    before, soft = links(ops, order, eng)
+    n = len(ops)
+    start, free, end = [0.0] * n, [0.0] * n, [0.0] * n
+    for i in order:
+        o, e = ops[i], eng[i]
+        t0 = free[before[i]] if before[i] is not None else 0.0
+        for j in o["near"]:
+            t0 = max(t0, end[j] + (0.0 if eng[j] == e == "p" or e is None else lat))
+        for j in soft[i]:
+            t0 = max(t0, end[j] + lat)
+        start[i] = t0
+        free[i] = t0 + (o["alts"][e][0] if e is not None else 0.0)
+        end[i] = free[i] + o.get("lat", 0.0)
+    return start, free, end
+
+
+def tails(ops, order, eng, queues):
+    before, soft = links(ops, order, eng)
+    tail = [0.0] * len(ops)
+    for i in reversed(order):
+        o, e = ops[i], eng[i]
+        c = o["alts"][e][0] if e is not None else 0.0
+        tail[i] += c + o.get("lat", 0.0)
+        for j in o["near"]:
+            tail[j] = max(tail[j], tail[i] + LAT)
+        if queues and before[i] is not None:
+            tail[before[i]] = max(tail[before[i]], tail[i] - ops[before[i]].get("lat", 0.0))
+    return tail
+
+
+def choose(ops):
+    eng, seen = [], {}
+    for o in ops:
+        a = list(o["alts"])
+        if len(a) < 2:
+            eng.append(a[0] if a else None)
+            continue
+        k = seen.get(o["tag"], 0)
+        seen[o["tag"]] = k + 1
+        pick = WHO.get(o["tag"], "a")
+        eng.append(pick[k % len(pick)])
+    return eng
+
+
+def plan(ops, seed=SEED, rounds=ROUNDS, noise=NOISE):
+    needs(ops)
+    eng = choose(ops)
+    x = [seed]
+
+    def rnd():
+        x[0] = (x[0] * 1103515245 + 12345) % 2147483648
+        return x[0] / 2147483648.0
+    base = tails(ops, list(range(len(ops))), eng, False)
+    prio = [p + noise * rnd() + OPT["early"] * o["early"] for p, o in zip(base, ops)]
+    best = None
+    for _ in range(rounds):
+        order = place(ops, prio, eng)
+        span = max(replay(ops, order, eng)[2])
+        if best is None or span < best[0]:
+            best = (span, order)
+        t = tails(ops, order, eng, True)
+        w = rnd()
+        prio = [w * a + (1 - w) * b + noise * rnd() for a, b in zip(t, prio)]
+    return best[1], eng
+
+
+def unpack(ops, text):
+    ab = "0123456789abcdefghijklmnopqrstuvwxyzABCDEFGHIJKLMNOPQRSTUVWXYZ"
+    order, eng = [], [None] * len(ops)
+    for i in range(0, len(text), 2):
+        second, k = divmod(62 * ab.index(text[i]) + ab.index(text[i + 1]), 1860)
+        order.append(k)
+        eng[k] = (list(ops[k]["alts"]) or [None])[second]
+    return order, eng
+
+
+PLAN = {}
+
+
+def ways(T, topo, core):
+    rank = T.rank_of(core)
+    nxt = T.cores[(rank + 1) % N]
+    others = [c for c in T.cores if c != core]
+    direct = [c for c in others if topo.may_write(core, c)]
+    far = [c for c in others if c not in direct]
+    free = [c for c in topo.cores_of(core) if T.rank_of(c) is None and all(topo.may_write(c, d) for d in far)]
+    free.sort(key=lambda c: topo.die(c) != topo.die(core))
+    relay, helpers = free[0], free[1:3]
+    share = {h: far[i::len(helpers)] for i, h in enumerate(helpers)}
+    return nxt, relay, direct, share
+
+
+def bits(engines):
+    return sum(1 << e for e in engines)
+
+
+def dst(topo, d, s):
+    rid, pid = topo.addr(d, s)
+    return DstId(rid=rid, pnc=pid)
+
+
+def hand_on(g, core, T, topo):
+    for owner in T.cores:
+        if core not in topo.cores_of(owner):
+            continue
+        r = T.rank_of(owner)
+        nxt, relay, direct, share = ways(T, topo, owner)
+        sent = 0
+        if core == relay:
+            rid, pid = topo.addr(nxt, core)
+            n_in, n_out = len(topo.engines(owner, core)), len(topo.engines(core, nxt))
+            for t in range(NT):
+                piece = T.land[:, t * PAYW:t * PAYW + PAYN]
+                g.wait_ge(T.sem["arr%d" % t], n_in)
+                g.remote_dma(piece, piece, T.sem["arr%d" % t], T.sem.loc, pid, rid, topo.mask(core, nxt))
+                sent += n_out
+        elif core in share:
+            off = topo.engines(owner, direct[0])
+            n_in = len([e for e in topo.engines(owner, core) if e not in off])
+            to = share[core]
+            for t in range(NT - 1):
+                piece = T.cnt[:, N * t + r:N * t + r + 1]
+                g.wait_ge(T.sem["cnt%d" % t], n_in)
+                g.remote_dma_fused([RemoteDMATransfer(dst_ids=[dst(topo, d, core) for d in to], dma_engine_mask=topo.mask(core, to[0]),
+                                                      remote_sem=T.sem["cnt%d" % t], src=piece, dsts=[piece] * len(to))], local_sem=T.sem.loc)
+                sent += len(topo.engines(core, to[0]))
+        if sent:
+            g.wait_ge(T.sem.loc, sent)
+
+
+def rank_program(g, core, T, topo):
+    rank = T.rank_of(core)
+    if rank is None:
+        hand_on(g, core, T, topo)
+        return
+    nxt, relay, direct, share = ways(T, topo, core)
+    off = topo.engines(core, direct[0])
+    helpers = list(share)
+    on = [e for e in topo.engines(core, helpers[0]) if e not in off]
+    prev = T.cores[(rank - 1) % N]
+    n_arr = len(topo.engines(ways(T, topo, prev)[1], core))
+    n_cnt = 0
+    for o in T.cores:
+        if o != core:
+            w = ways(T, topo, o)
+            n_cnt += len(topo.engines(o, w[2][0])) if core in w[2] else sum(len(topo.engines(h, to[0])) for h, to in w[3].items() if core in to)
+    ops = build(T, rank)
+    if not PLAN:
+        PLAN["it"] = unpack(ops, ORDER) if ORDER else plan(build(T, 1))
+    order, eng = PLAN["it"]
+    needs(ops)
+    soft = links(ops, order, eng)[1]
+    for i, o in enumerate(ops):
+        o["eng"], o["soft"] = eng[i], soft[i]
+    Q = {"v": g.vector, "a": g.scalar, "p": g.tensor, "g": g, "s": g.sync}
+    count = {e: 0 for e in ESEM}
+    for i in order:
+        o = ops[i]
+        if "done" in o:
+            s, v = o["done"]
+            o["sig"] = (s, v if v is not None else (n_arr if s.startswith("arr") else n_cnt))
+        elif "remote" in o:
+            o["sig"] = None
+        else:
+            count[o["eng"]] += 1
+            o["sig"] = (ESEM[o["eng"]], count[o["eng"]])
+    seen = {e: {} for e in Q}
+    sent = 0
+    for i in order:
+        o = ops[i]
+        e = o["eng"]
+        if e is None:
+            continue
+        need = {}
+        for j in o["near"] + o["soft"]:
+            if ops[j]["eng"] == e == "p" or ops[j]["sig"] is None:
+                continue
+            s, v = ops[j]["sig"]
+            need[s] = max(need.get(s, 0), v)
+        for s in sorted(need):
+            if seen[e].get(s, 0) < need[s]:
+                Q[e].wait_ge(T.sem[s], need[s])
+                seen[e][s] = need[s]
+        f = o["alts"][e][1]
+        if "remote" in o:
+            kind, t = f
+            if kind == "pay":
+                rid, pid = topo.addr(relay, core)
+                g.remote_dma(T.land[:, t * PAYW:t * PAYW + PAYN], T.pay[:, t * PAYW:t * PAYW + PAYN], T.sem["arr%d" % t], T.sem.loc,
+                             pid, rid, topo.mask(core, relay))
+                sent += len(topo.engines(core, relay))
+            else:
+                src, to = T.dcol[:, 8 * t:8 * t + 1], T.cnt[:, N * t + rank:N * t + rank + 1]
+                g.remote_dma_fused([
+                    RemoteDMATransfer(dst_ids=[dst(topo, d, core) for d in helpers], dma_engine_mask=bits(on), remote_sem=T.sem["cnt%d" % t],
+                                      src=src, dsts=[to] * len(helpers)),
+                    RemoteDMATransfer(dst_ids=[dst(topo, d, core) for d in direct], dma_engine_mask=bits(off), remote_sem=T.sem["cnt%d" % t],
+                                      src=src, dsts=[to] * len(direct))], local_sem=T.sem.loc)
+                sent += len(on) + len(off)
+        elif "done" in o:
+            f(Q[e])
+        else:
+            f(Q[e]).then_inc(T.sem[ESEM[e]], 1)
+    g.wait_ge(T.sem.loc, sent)
+    for e in ESEM:
+        g.wait_ge(T.sem[ESEM[e]], count[e])
+    for o in ops:
+        if "done" in o:
+            g.wait_ge(T.sem[o["sig"][0]], o["sig"][1])

@@ -6,7 +6,7 @@ AF = ActivationFunctionType
 N, V, C, NT, S, DG = 8, 2048, 256, 5, 48, 5
 NONE = C
 WN = C + 2 * S + 16
-PAYN, PAYW = 2 * S + 1, 2 * S + 4
+PAYN, PAYW = S + 1, S + 4
 OFFS = 2036.0
 MAGIC = 12582912.0
 RH, RC, RD, RI, MW = 0, 7 * S, 8 * S + C, 8 * S + 2 * C, 8 * S + 3 * C
@@ -30,14 +30,14 @@ _SB = {
     "owf": (16, F32), "owu": (16, U16), "av": (16, F32), "ssm": (S, F32), "ge": (C + S, F16), "mv": (C + S, F16),
     "hwi": (S, F32), "sm": (C + S, F16), "sn": (C + S, F16), "swu": (20, U16), "nk": (C + S, F16), "eq": (5 * C, F16), "eqi": (5 * S, F16), "uin": (S, BF),
     "al0": (C, BF), "col": (32, F32), "dcol": (8 * NT, BF), "tmp0": (C, F32), "tmp1": (128, F32),
-    "pay": (NT * PAYW, F32), "land": (NT * PAYW, F32), "cnt": (NT * N, BF),
+    "pay": (NT * PAYW, F32), "land": (NT * PAYW, F32), "payh": (NT * S, F16), "landh": (NT * S, F16), "cnt": (NT * N, BF),
 }
 SCRATCH = {k: ("sbuf", [128, w], d) for k, (w, d) in _SB.items()}
 for _b in range(8):
     SCRATCH["ps%d" % _b] = ("psum", [128, 512], F32)
 _LOADS = ["s0", "nb", "qs", "w0", "us", "coin", "lo", "hi"]
 SEMAPHORES = (["ev", "ea", "ep", "eg", "loc", "outw", "outh"] + ["ld_" + x for x in _LOADS]
-              + ["arr%d" % t for t in range(NT)] + ["cnt%d" % t for t in range(NT - 1)])
+              + ["arr%d" % t for t in range(NT)] + ["arh%d" % t for t in range(NT)] + ["cnt%d" % t for t in range(NT - 1)])
 ESEM = {"v": "ev", "a": "ea", "p": "ep", "g": "eg"}
 
 PAR = (1.04, 0.55, 1.56, 3.8, 5500.0, 7000.0, 90.0)
@@ -50,21 +50,21 @@ HEADS = [(0, 64), (64, 160), (160, 256)]
 GSTEP = 32
 OPT = {"count": False, "rbv": False, "early": 3000.0, "wrapv": "il"}
 ORDER = (
-    "02090L0p010500030b0e0c0g0d0v0G060R1a0M0704080V0H1Q0X0a0f1P0r0I0W180Y1R171o1r0F0t0s0T1w1q111d191v1p1i1e1g1B1m1kvf0Z101s0S"
-    "0U1C1tvhvl0hvjvn1u1G1x0o0K0w1yv21A0OvDvEvUvV1Ww42f2526162e1X1cvFvH1Iwpwo0n1Z1Y2728200J0Q0uw9210xv32q2gw21O0i0z140N152r2s"
-    "2a1J2i0j0lwJ0m0k232H2I2M2h2bwtwj2k2u2N0P2O2P2lvzwc1b0y2Qwm2y2R2S2d2n1T1S0q2v2T2X2U2Z2z0Bww2x2Y3O1K302Wx6wK312A0E2D1M2E2B"
-    "2F37320A2Vx3wL2G2C343839yG3c1N3o3d3p3f3A3g3r3h3s3e353q3i3B3t3j3a3kxb3l3u3D3m3w3N3M4F3C3n3E3v3F0D3G3x3y3I1L0C3HxSxT433J3U"
-    "y23K3V4c443PxX463Y3Wyd4e3Q453Z474H4f4I4Z4K4J4L4M4h4N4iymyny04o4P4O4j4Q4RyT484U414V4g494p4q4X4W4Y50ykxRyS5c5dze4lxLxz515h"
-    "4ayr4sz24t5i5j4b5k4w5m534x5l544y5nyu5o5s5p5t6pz54z564v5uzgzfyA57585v4BzB5w594C4D5a5x5r4Ezq5Czy5bzz5A6o5D5E5H5I5V695F5L5W"
-    "5Z6aBh5M6d5Y5J5K6b5N605O6e5P5Q5R616f62zG5X5S6c6n7g5T6gAuAt6j6i6h6465636k666v5U676lAD6EAOAXAY6F6q6w6N6y6GA86z6I6A6P6J6Q6x"
-    "7i6K7j7k7l7mAS7n7o6r6ZAL7p6T7s7q707rAsAm7t6UB27u7C7x6R716VBw6M7y6H7A737B7zABBR7P7Q6W6CBS74Bv7U77787W7VBF7G7X7D7Y7Z7HB580"
-    "798182BI767E7a7J877c7K7dBTBbC3Ce7L887e7MBf897N8a7O8fCb8c848d9Z858g8A8k8Q8B8l8F8p8q8R8V8r8n868m8S8o9698E08G8h8s8H8i8u8w8I"
-    "8t8v978D8E8C8x8L8J8M8WCj8y8X8KCz8Y8U8T8NDc8Z90918O92DmDn9d939e948P959Q9o9ga1a29fDwDxa6a4a5a3ana79h9pa8DGDH9ia99r9yab9qaa"
-    "acad9jaeafEhEiao9s9z9I9t9k9B999a9A9K9CDuaj9J9DalakDbamaAaB9Lag9MECaq9NDE9l9vaFapaGaraHaIasaJDO9F9RaKaL9SaMEtaNaQ9P9TauaS"
-    "DUEDEZ9Vav9WawaT9XaxaPaUDYayaVEOazaRbZb0EWaXEEb1aYbYb2bnb5bFbob6bGbtGRbbbXcQbqbabcbLbdbubpb7b8b9bJbHbIbrbebvb3bMbiF4bwbj"
-    "bfbAbNbsbKbgbhbkbObBbTbxbSbPbybzbRblbQbCc3G4bUbDbVceGdc5cfcocgc0c6c7c8cScic9cjcTcYGxcZchd0ckd1cXcUcVcWd6d4d5d3d2Gncpcacq"
-    "GyFWd7czd8GlcbGscmcAc1d9ctcrcuHbHabmcvcBGCdgdccccwG2cDdedddfFEHhHtdrdscEdidwcHcIdxdydzdAdjdBdCcJdDGFHkdEcGdlcKHudHdmcMdn"
-    "cNdIdFdJdodpGLcOcPdKHLdqdMHOdPdQdGdRHvdNdVdSHTdUdXdWdYdZ")
+    "090p03020n010004050a100608071a111Q0c0e0b0d1P0v0L0V0G0S0R0H1o0t0f1q1p0I0M1v1r1d1s1i0r0J0W0X1g1k1evf1m0x0Y0F0y0s140T0u0z0Z"
+    "1R1t1Bvhvlvj0ov2v30U1u171x0gvFvnvG1H1y15vD1U1V1ww5w4wfwe1W26191C1A1X0hvE1Y0K1Z0i27200O29212gwowp1I1T2a0w2h2b2j2q1Sw20j1O"
+    "2k1N0P2lwc2r2i2m2818wt2s1b1J2I2H162u0Q0N2vwJvz0l0k0m0q232n2d2M2y2N2O2P2zwwwK2R2Q2S0A2A1c2T2X2U2B2x0E2Z2D0D302E312YwC3P2F"
+    "wV0BwL1K322G2W0C34x7381M1L393ax33pyH353q3d3B3e3C3s3g3b3f3h3E3t3i3F3j3r364I3D3u3G3l3k3H3v3m3N4G3Oxc3J3n3w3x3IxoxU3y3T3K3z"
+    "3L3Vy34K4J3Q443W3X4d4Lyeynyo3Y4M3M4f453Z4N3R4O4g4h4P4Q503A47464Ryiy84S40yUyV494p4j4x4WxSyT524a4k4q414Y4r42ys4t4Z4X5e5d4l"
+    "4uybzfzg4c5i4mzh5j5kz35l545m554yyv5nz65o5p4z5q4w4A57yB5vzr4C584D595w515x5a4E5t4FzDzb5E5y5c5s5A5FBj5G5J5B7k5Kzz5X6b606c5Y"
+    "5N5H5O5M5L5P615Q6f5R5T5SzI62635u5C6r5Z5U6g5V6465665W6h67AvAw6i6d6p7i6e686q6l696k6jAPAG6F6x7l6m6z7o6y7p6n7q6A7n7r7m6HAQ6B"
+    "7u7t7s7v706I7w6a6K6RAZ716s6C6LBzBy7A6T6S6M6tAU72AuB46J6N6V737C757B7D6WADBTBH7S7R7I6O6EAX7W767J7X7Y7Z7E6Y807K7aAoBx81827G"
+    "83B7BUBV84797L78897b7e7M7f7c7N7g7OCh8aBhBd7F8b7P8i878c889b867Q85Cd8j8e8n8o8D8T8s8E8U8rE38f8g8k8t8p8q8I8u8Y8v8J8l8z8y8w8x"
+    "8K8G9aa48H8FCm8A8V8X8W99a28Z8L908B8O9gDfCC9h8N8P918M8Q92959i94Dk8R939j9pDqDz96a59l97a99m9c9ra8a6a7aa9n9sabaq9uac9t9v98DA"
+    "9BadagafaeDKDJ9C9wah9o9Lai9dakDE9FElam9M9N9D9GDx9yDeCSao9TDOanapEF9HaEaD9PEtauaI9QaJaKaLarEj9IDRaMav9UaNaOas9SEwaPaTaQ9V"
+    "aV9Wax9Yay9ZazaUaWEHDXF3c3aAa0aXaBEGa1aYaCaSb0b4b5GVb6EZb9brbabJbfbsERbxbgbKbPbhbybQb1b2cWbbbebdbcbtbwbvbibuc1c2cUbNbLbO"
+    "bzbkbjbnblbAbmbobRbDbFbEbpbBbCb7G8F8bGc7bMc9bHbSbqGhGrGicXc4bWbXbUbVbIcad2cbccbTd3cdc5d4cYd0d1ced5cZbYbZd9d8d7dad6GCGscj"
+    "dbcBckdcc6cmdecDcnclc0ctHfcocvcucFcEdgGfcgdicwGGHddkdjHxcxdvdwdAcyGzcHdBdhdDHldCcLdEcpcIdFHzdmdGdHcAcqdndIcMdKGJcKHocNdL"
+    "dpHydJdMcQcOdNcRdOdqdrHPcSGPGTdsdtdSHTdudQdUdRe0dWdVdXHZdYe2e1e4e3e5")
 
 
 def A(name, c0=0, c1=None, st=1, p0=0, p1=128):
@@ -349,7 +349,7 @@ def build(T, rank, par=PAR):
         ge, mv = A("ge", c0, c1), A("mv", c0, c1)
         ts(ge, vb, A("col", 2, 3), None, ALU.is_gt, tag="ge" + x)
         tt(mv, dn, ge, ALU.mult, "mv" + x)
-        mm([(ph, A("ident"), A("h16", c0, c1)), (ph, O(t + 1), mv)], "hnew" + x)
+        mm([(ph, A("ident"), A("landh", S * (t - 1), S * t) if x else A("h16", c0, c1)), (ph, O(t + 1), mv)], "hnew" + x)
         if t == NT - 1:
             ts(hw, ph, -1.0, None, ALU.add, tag="hw" + x, act=(AF.Identity, A("col", 14, 15), 1.0))["rd"].append(A("col", 14, 15))
         else:
@@ -361,7 +361,7 @@ def build(T, rank, par=PAR):
         if not byv:
             mm([(pw, A("zr", 144 * (t - 1) + 15 - b, 144 * (t - 1) + 143 - b), A("h16", c0 + b, c1, 16)) for b in range(16)], "siw" + x)
         for p in range(t, -1, -1):
-            mm([(hb[p], A("sel", 128 * p, 128 * p + 128), A("h16", c0, c1))], "hb" + x)
+            mm([(hb[p], A("sel", 128 * p, 128 * p + 128), A("landh", S * (t - 1), S * t) if x else A("h16", c0, c1))], "hb" + x)
         if byv:
             tt(A("sm", c0, c1), hb[t], A("mask", 0, c1 - c0), ALU.mult, "sm" + x)
             scan(A("sn", c0, c1), A("rs16", 0, c1 - c0), A("sm", c0, c1), 0.0, ALU.mult, ALU.add, "sn" + x)
@@ -407,7 +407,7 @@ def build(T, rank, par=PAR):
         if t > 0:
             add({}, [], [A("land", L0, L0 + PAYW)], "arr", done=("arr%d" % (t - 1), None), lat=HOP2, after="sp%d" % (t - 1))
             copy(A("uin"), IND(A("ub", C * t, C * t + WN), HL), "va", "uin")
-            copy(A("h16", C, C + S), A("land", L0 + S, L0 + 2 * S), tag="hi16")
+            add({}, [], [A("landh", S * (t - 1), S * t)], "arh", done=("arh%d" % (t - 1), None), lat=HOP2 - 500, after="sh%d" % (t - 1))
             head(t, C, C + S, A("ps3", 504, 507), [A("ps7", S * p, S * p + S) for p in range(t + 1)], A("ps3", 456, 504),
                  [A("eqi", S * p, S * p + S) for p in range(t + 1)], "i")
             fb = A("ps7", 240, 288)
@@ -415,8 +415,8 @@ def build(T, rank, par=PAR):
             tt(A("w1i"), fb, A("land", L0, L0 + S), ALU.mult, "w1i")
             copy(IND(A("wv", WN, 2 * WN), HL), A("w1i"), tag="scw")
             if not last:
-                ts(A("col", 20, 21), A("land", L0 + 2 * S, L0 + 2 * S + 1), 0.0, float(S), ALU.max, ALU.min, tag="nin")
-                ts(A("col", 8, 9), A("col", 20, 21), A("pay", L0 + 2 * S, L0 + 2 * S + 1), 0.0, ALU.add, ALU.min, tag="db")
+                ts(A("col", 20, 21), A("land", L0 + S, L0 + S + 1), 0.0, float(S), ALU.max, ALU.min, tag="nin")
+                ts(A("col", 8, 9), A("col", 20, 21), A("pay", L0 + S, L0 + S + 1), 0.0, ALU.add, ALU.min, tag="db")
             mm([(A("ps3", 360, 408), A("dm"), A("of", C, C + S))], "dni")
             grow2(C, C + S, A("ps3", C, C + S))
             sites(t, C, C + S, A("ps3", C, C + S), A("ps3", 360, 408), A("ps3", 408, 456), A("hwi"), "i")
@@ -445,7 +445,7 @@ def build(T, rank, par=PAR):
             (ex, A("bo"), A("sc", 68, 69)), (ex, A("nbo"), A("sc", 16, 17))], "px", opens=False)
         scan(A("rr"), A("rsx"), A("ps7", X, X + 120), 0.0, ALU.max, ALU.min, "rr")
         copy(A("of2"), A("rr", 2, 120, 3), tag="of2")
-        ec = A("pay", P0 + 2 * S, P0 + 2 * S + 1)
+        ec = A("pay", P0 + S, P0 + S + 1)
         copy(ec, ex, "va", "e")
         tt(A("av"), xv, alive, ALU.mult, "av")
         if not last:
@@ -470,8 +470,9 @@ def build(T, rank, par=PAR):
             copy(A("osu", 0, 3), A("ra", 15, S, 16), tag="osu")
         OS = A("osu", 0, 3)
         copy(A("pay", P0, P0 + S), IND(A("wv", 0, WN), OS), "va", "payw")
-        copy(A("pay", P0 + S, P0 + 2 * S), IND(A("hw"), OS), "va", "payh")
-        add({"g": (1200.0, ("pay", t))}, [A("pay", P0, P0 + 2 * S + 1)], [], "sp%d" % t, remote=True)
+        copy(A("payh", S * t, S * t + S), IND(A("hw"), OS), "v", "payh")
+        add({"g": (1200.0, ("payh", t))}, [A("payh", S * t, S * t + S)], [], "sh%d" % t, remote=True)
+        add({"g": (1200.0, ("pay", t))}, [A("pay", P0, P0 + PAYN)], [], "sp%d" % t, remote=True)
         if OPT["rbv"]:
             tt(A("gb"), IND(A("mm_"), A("of2", 16, 35)), A("mask"), ALU.mult, "gb")
             scan(A("rb"), A("rs16"), A("gb"), 0.0, ALU.mult, ALU.add, "rb")
@@ -496,7 +497,8 @@ def build(T, rank, par=PAR):
     L0 = (NT - 1) * PAYW
     add({}, [], [A("land", L0, L0 + PAYW)], "arr", done=("arr%d" % (NT - 1), None), lat=HOP2, after="sp%d" % (NT - 1))
     copy(IND(A("wc"), HL), A("land", L0, L0 + S), tag="scw")
-    copy(IND(A("h32"), HL), A("land", L0 + S, L0 + 2 * S), tag="sch")
+    add({}, [], [A("landh", S * (NT - 1), S * NT)], "arh", done=("arh%d" % (NT - 1), None), lat=HOP2 - 500, after="sh%d" % (NT - 1))
+    copy(IND(A("h32"), HL), A("landh", S * (NT - 1), S * NT), tag="sch")
     store("yw", "wc", "s", "outw")
     store("yh", "h32", "a", "outh")
     return ops
@@ -675,8 +677,11 @@ def ways(T, topo, core):
     far = [c for c in others if c not in direct]
     free = [c for c in topo.cores_of(core) if T.rank_of(c) is None and all(topo.may_write(c, d) for d in far)]
     free.sort(key=lambda c: topo.die(c) != topo.die(core))
-    relay, helpers = free[0], free[1:3]
+    relay, helpers = free[0:2], free[2:4]
     share = {h: far[i::len(helpers)] for i, h in enumerate(helpers)}
+    near = [c for c in topo.cores_of(core) if T.rank_of(c) is None and c not in free and all(topo.may_write(c, d) for d in direct)]
+    near.sort(key=lambda c: topo.die(c) != topo.die(core))
+    share[near[0]] = direct
     return nxt, relay, direct, share
 
 
@@ -696,13 +701,16 @@ def hand_on(g, core, T, topo):
         r = T.rank_of(owner)
         nxt, relay, direct, share = ways(T, topo, owner)
         sent = 0
-        if core == relay:
+        if core in relay:
             rid, pid = topo.addr(nxt, core)
-            n_in, n_out = len(topo.engines(owner, core)), len(topo.engines(core, nxt))
+            off = topo.engines(owner, direct[0])
+            n_in = len(off) if core == relay[0] else len([e for e in topo.engines(owner, core) if e not in off])
+            n_out = len(topo.engines(core, nxt))
             for t in range(NT):
-                piece = T.land[:, t * PAYW:t * PAYW + PAYN]
-                g.wait_ge(T.sem["arr%d" % t], n_in)
-                g.remote_dma(piece, piece, T.sem["arr%d" % t], T.sem.loc, pid, rid, topo.mask(core, nxt))
+                piece = T.landh[:, t * S:t * S + S] if core == relay[0] else T.land[:, t * PAYW:t * PAYW + PAYN]
+                sem = T.sem[("arh%d" if core == relay[0] else "arr%d") % t]
+                g.wait_ge(sem, n_in)
+                g.remote_dma(piece, piece, sem, T.sem.loc, pid, rid, topo.mask(core, nxt))
                 sent += n_out
         elif core in share:
             off = topo.engines(owner, direct[0])
@@ -728,12 +736,12 @@ def rank_program(g, core, T, topo):
     helpers = list(share)
     on = [e for e in topo.engines(core, helpers[0]) if e not in off]
     prev = T.cores[(rank - 1) % N]
-    n_arr = len(topo.engines(ways(T, topo, prev)[1], core))
+    n_arr = len(topo.engines(ways(T, topo, prev)[1][0], core))
     n_cnt = 0
     for o in T.cores:
         if o != core:
             w = ways(T, topo, o)
-            n_cnt += len(topo.engines(o, w[2][0])) if core in w[2] else sum(len(topo.engines(h, to[0])) for h, to in w[3].items() if core in to)
+            n_cnt += sum(len(topo.engines(h, to[0])) for h, to in w[3].items() if core in to)
     ops = build(T, rank)
     if not PLAN:
         PLAN["it"] = unpack(ops, ORDER) if ORDER else plan(build(T, 1))
@@ -748,7 +756,7 @@ def rank_program(g, core, T, topo):
         o = ops[i]
         if "done" in o:
             s, v = o["done"]
-            o["sig"] = (s, v if v is not None else (n_arr if s.startswith("arr") else n_cnt))
+            o["sig"] = (s, v if v is not None else (n_arr if s.startswith("ar") else n_cnt))
         elif "remote" in o:
             o["sig"] = None
         else:
@@ -775,18 +783,20 @@ def rank_program(g, core, T, topo):
         if "remote" in o:
             kind, t = f
             if kind == "pay":
-                rid, pid = topo.addr(relay, core)
+                rid, pid = topo.addr(relay[1], core)
                 g.remote_dma(T.land[:, t * PAYW:t * PAYW + PAYN], T.pay[:, t * PAYW:t * PAYW + PAYN], T.sem["arr%d" % t], T.sem.loc,
-                             pid, rid, topo.mask(core, relay))
-                sent += len(topo.engines(core, relay))
+                             pid, rid, bits(on))
+                sent += len(on)
+            elif kind == "payh":
+                rid, pid = topo.addr(relay[0], core)
+                g.remote_dma(T.landh[:, t * S:t * S + S], T.payh[:, t * S:t * S + S], T.sem["arh%d" % t], T.sem.loc, pid, rid, bits(off))
+                sent += len(off)
             else:
                 src, to = T.dcol[:, 8 * t:8 * t + 1], T.cnt[:, N * t + rank:N * t + rank + 1]
                 g.remote_dma_fused([
                     RemoteDMATransfer(dst_ids=[dst(topo, d, core) for d in helpers], dma_engine_mask=bits(on), remote_sem=T.sem["cnt%d" % t],
-                                      src=src, dsts=[to] * len(helpers)),
-                    RemoteDMATransfer(dst_ids=[dst(topo, d, core) for d in direct], dma_engine_mask=bits(off), remote_sem=T.sem["cnt%d" % t],
-                                      src=src, dsts=[to] * len(direct))], local_sem=T.sem.loc)
-                sent += len(on) + len(off)
+                                      src=src, dsts=[to] * len(helpers))], local_sem=T.sem.loc)
+                sent += len(on)
         elif "done" in o:
             f(Q[e])
         else:

@@ -1,5 +1,5 @@
 from concourse.bass import DstId, RemoteDMATransfer
-from concourse.mybir import AluOpType, AxisListType, ActivationFunctionType
+from concourse.mybir import AluOpType, ActivationFunctionType
 
 ALU = AluOpType
 AF = ActivationFunctionType
@@ -7,29 +7,34 @@ N, V, C, NT, S, DG = 8, 2048, 256, 5, 48, 5
 NONE = C
 WN = C + 2 * S + 16
 PAYN, PAYW = S + 1, S + 4
-OFFS = 2036.0
-MAGIC = 12582912.0
-RH, RC, RD, RI, MW = 0, 7 * S, 8 * S + C, 8 * S + 2 * C, 8 * S + 3 * C
+MID = 1023.0
+BASE = 786432.0
+TWO23 = 8388608.0
+RH, RC, RD, RI, MW = 0, 593, 864, 1120, 1376
+
+CHUNKS = [(0, 64), (64, 128), (128, 192), (192, 256)]
+FIRST = [(0, 128), (128, 256)]
+GSTEP, GSTEPI = 32, 24
+XW = 16 * (C + S + 8)
 
 F32, BF, F16, I32, U16 = "float32", "bfloat16", "float16", "int32", "uint16"
 _SB = {
     "nbt": (V, I32), "qt": (V + 16, BF), "w0s": (C, F32), "lh": (16, F32), "s0i": (C, I32), "usi": (C, I32),
-    "cni": (NT * C, I32), "s0h": (C, F16), "usb": (C, BF), "cnb": (NT * C, BF), "ub": (NT * C + WN - C, BF),
-    "ones": (640, BF), "ident": (128, BF), "bo": (128, BF), "bo1": (128, BF), "nbo": (128, BF), "l2a": (128, BF), "l2": (128, BF),
-    "dma_": (128, F32), "dm": (128, F32), "jj": (256, BF), "z8": (144, BF), "bo8a": (128, BF), "bo8": (128, BF), "zt": (640, BF),
-    "zz": (144, BF), "i11": (128, BF), "i2k": (128, BF), "ip": (128, BF), "im": (128, BF), "sel": (640, BF),
-    "bo2": (128, BF), "bo16": (128, BF), "hb_": (C, BF), "pcb": (C, BF), "bia": (12, F32), "jnk": (3 * C, BF), "mk1": (16, BF), "rb": (C + S, F32),
-    "mki": (C + S, I32), "mki2": (C + S, I32), "mask": (C + S, BF), "ids": (C, BF), "c16": (128, BF), "pci": (8, I32),
-    "pci2": (8, I32), "cc": (144, F16), "cw": (16, F32), "zr": (576, BF), "rs16": (C + S, BF), "rs32": (72, BF), "rsx": (120, F32),
-    "th": (NT * 48, F32), "thb": (NT * 16, F32),
-    "oq": (C + S, U16), "of": (C + S, F32), "xx": (16 * (C + S), BF), "ee": (16 * (C + S), BF),
-    "sg": (16 * (C + S), BF), "d0a": (1024, F16), "d0b": (1024, F16), "thr": (C + S, F32), "yy": (C + S, F32),
-    "wc": (WN, F32), "wv": (3 * WN, F32), "w1i": (S, F32), "h32": (WN, F32), "h16": (C + S, F16), "hw": (WN, F32),
-    "fl": (3 * C, BF), "fw": (72, BF), "dbl": (16, BF), "sc": (72, BF), "rr": (120, F32), "of2": (40, U16),
-    "mm_": (MW, BF), "ga": (S, BF), "gb": (C + S, BF), "ra": (S, BF), "osu": (4, U16), "oh": (20, U16),
-    "owf": (16, F32), "owu": (16, U16), "av": (16, F32), "ssm": (S, F32), "ge": (C + S, F16), "mv": (C + S, F16),
-    "hwi": (S, F32), "sm": (C + S, F16), "sn": (C + S, F16), "swu": (20, U16), "nk": (C + S, F16), "eq": (5 * C, F16), "eqi": (5 * S, F16), "uin": (S, BF),
-    "al0": (C, BF), "col": (32, F32), "dcol": (8 * NT, BF), "tmp0": (C, F32), "tmp1": (128, F32),
+    "cni": (NT * C, I32), "s0h": (C, F16), "usb": (C, BF), "cnb": (NT * C, BF), "ub": (NT * C + WN - C, F32),
+    "ones": (640, BF), "ident": (128, BF), "bo": (128, BF), "bo1": (128, BF), "nbo": (128, BF), "boh": (128, BF), "l2a": (128, BF), "l2": (128, BF),
+    "dma_": (128, BF), "dmb": (128, BF), "dm": (128, BF), "c15": (128, BF), "jj": (256, BF), "z8": (144, BF), "bo8a": (128, BF), "bo8": (128, BF),
+    "zt": (640, BF), "zz": (144, BF), "zzh": (144, BF), "i11": (128, BF), "i2k": (128, BF), "ip": (128, BF), "im": (128, BF), "sel": (640, BF),
+    "mki": (S, I32), "mki2": (S, I32), "pick": (S, BF), "ids": (C, BF), "pci": (8, I32),
+    "pci2": (8, I32), "cc": (144, F16), "cw": (16, F32), "zr": (576, BF), "rs32": (84, BF), "rsx": (128, F32),
+    "th": (NT * 48, F32), "thb": (NT * 16, F32), "cap": (2048, BF),
+    "oq": (C + S, U16), "xx": (XW, F16), "ee": (XW, BF), "yy": (C + S, F32),
+    "wc": (WN, F32), "wv": (3 * WN, F32), "w1i": (S, F32), "h32": (WN, F32), "h16": (C, F16), "hw": (WN, F32), "pw": (WN, F32),
+    "fl": (3 * C, BF), "fw": (84, BF), "dbl": (16, BF), "sc": (84, BF), "rr": (128, F32), "of2": (40, U16),
+    "mm_": (MW, BF), "gb": (C + S, BF), "ra": (S, BF), "osu": (4, U16), "oh": (20, U16),
+    "owf": (16, F32), "owu": (16, U16), "av": (16, F32), "sg": (C + S, BF), "mv": (C + S, F16),
+    "hwi": (S, F32), "pwi": (S, F32), "swu": (20, U16), "swa": (4, U16), "nk": (C + S, F16), "nn": (C + S, F16),
+    "eq": (5 * C, BF), "eqi": (5 * S, BF), "eqa": (5 * S, BF), "uin": (S, F32),
+    "al0": (C, BF), "col": (32, F32), "dcol": (8 * NT, BF), "tmp0": (C, F32),
     "pay": (NT * PAYW, F32), "land": (NT * PAYW, F32), "payh": (NT * S, F16), "landh": (NT * S, F16), "cnt": (NT * N, BF),
 }
 SCRATCH = {k: ("sbuf", [128, w], d) for k, (w, d) in _SB.items()}
@@ -40,31 +45,11 @@ SEMAPHORES = (["ev", "ea", "ep", "eg", "loc", "outw", "outh"] + ["ld_" + x for x
               + ["arr%d" % t for t in range(NT)] + ["arh%d" % t for t in range(NT)] + ["cnt%d" % t for t in range(NT - 1)])
 ESEM = {"v": "ev", "a": "ea", "p": "ep", "g": "eg"}
 
-PAR = (1.04, 0.55, 1.56, 3.8, 5500.0, 7000.0, 90.0)
-LAT = 110.0
-SEED, ROUNDS, NOISE = 1, 4, 200.0
-WHO = {"gx": "avaaa", "sign": "vva", "y": "v", "cnb": "g", "big": "vvgg"}
-CHUNKS = [(0, 64), (64, 128), (128, 192), (192, 256)]
-CHUNK2 = [(0, 192), (192, 256)]
-HEADS = [(0, 64), (64, 160), (160, 256)]
-GSTEP = 32
-OPT = {"count": False, "rbv": False, "early": 3000.0, "wrapv": "il"}
-ORDER = (
-    "090p03020n010004050a100608071a111Q0c0e0b0d1P0v0L0V0G0S0R0H1o0t0f1q1p0I0M1v1r1d1s1i0r0J0W0X1g1k1evf1m0x0Y0F0y0s140T0u0z0Z"
-    "1R1t1Bvhvlvj0ov2v30U1u171x0gvFvnvG1H1y15vD1U1V1ww5w4wfwe1W26191C1A1X0hvE1Y0K1Z0i27200O29212gwowp1I1T2a0w2h2b2j2q1Sw20j1O"
-    "2k1N0P2lwc2r2i2m2818wt2s1b1J2I2H162u0Q0N2vwJvz0l0k0m0q232n2d2M2y2N2O2P2zwwwK2R2Q2S0A2A1c2T2X2U2B2x0E2Z2D0D302E312YwC3P2F"
-    "wV0BwL1K322G2W0C34x7381M1L393ax33pyH353q3d3B3e3C3s3g3b3f3h3E3t3i3F3j3r364I3D3u3G3l3k3H3v3m3N4G3Oxc3J3n3w3x3IxoxU3y3T3K3z"
-    "3L3Vy34K4J3Q443W3X4d4Lyeynyo3Y4M3M4f453Z4N3R4O4g4h4P4Q503A47464Ryiy84S40yUyV494p4j4x4WxSyT524a4k4q414Y4r42ys4t4Z4X5e5d4l"
-    "4uybzfzg4c5i4mzh5j5kz35l545m554yyv5nz65o5p4z5q4w4A57yB5vzr4C584D595w515x5a4E5t4FzDzb5E5y5c5s5A5FBj5G5J5B7k5Kzz5X6b606c5Y"
-    "5N5H5O5M5L5P615Q6f5R5T5SzI62635u5C6r5Z5U6g5V6465665W6h67AvAw6i6d6p7i6e686q6l696k6jAPAG6F6x7l6m6z7o6y7p6n7q6A7n7r7m6HAQ6B"
-    "7u7t7s7v706I7w6a6K6RAZ716s6C6LBzBy7A6T6S6M6tAU72AuB46J6N6V737C757B7D6WADBTBH7S7R7I6O6EAX7W767J7X7Y7Z7E6Y807K7aAoBx81827G"
-    "83B7BUBV84797L78897b7e7M7f7c7N7g7OCh8aBhBd7F8b7P8i878c889b867Q85Cd8j8e8n8o8D8T8s8E8U8rE38f8g8k8t8p8q8I8u8Y8v8J8l8z8y8w8x"
-    "8K8G9aa48H8FCm8A8V8X8W99a28Z8L908B8O9gDfCC9h8N8P918M8Q92959i94Dk8R939j9pDqDz96a59l97a99m9c9ra8a6a7aa9n9sabaq9uac9t9v98DA"
-    "9BadagafaeDKDJ9C9wah9o9Lai9dakDE9FElam9M9N9D9GDx9yDeCSao9TDOanapEF9HaEaD9PEtauaI9QaJaKaLarEj9IDRaMav9UaNaOas9SEwaPaTaQ9V"
-    "aV9Wax9Yay9ZazaUaWEHDXF3c3aAa0aXaBEGa1aYaCaSb0b4b5GVb6EZb9brbabJbfbsERbxbgbKbPbhbybQb1b2cWbbbebdbcbtbwbvbibuc1c2cUbNbLbO"
-    "bzbkbjbnblbAbmbobRbDbFbEbpbBbCb7G8F8bGc7bMc9bHbSbqGhGrGicXc4bWbXbUbVbIcad2cbccbTd3cdc5d4cYd0d1ced5cZbYbZd9d8d7dad6GCGscj"
-    "dbcBckdcc6cmdecDcnclc0ctHfcocvcucFcEdgGfcgdicwGGHddkdjHxcxdvdwdAcyGzcHdBdhdDHldCcLdEcpcIdFHzdmdGdHcAcqdndIcMdKGJcKHocNdL"
-    "dpHydJdMcQcOdNcRdOdqdrHPcSGPGTdsdtdSHTdudQdUdRe0dWdVdXHZdYe2e1e4e3e5")
+PAR = dict(cy=0.92, pcy=0.48, gr=1.56, scr=3.8, hop=3400.0, hopc=4700.0, fa=90.0, fv=25.0, fp=60.0, call=700.0, lat=130.0,
+           nb=4500.0, qs=5800.0)
+MIX = 0.5
+WHO = ['boh', 'e', 'gx', 'gx.3', 'gxi', 'i2k', 'nk0.1', 'nka', 'nki', 'of2', 'oq', 'oq.1', 'oq0', 'oqa', 'osu', 'owu', 'payw', 'pw', 'pwi', 'sel.2', 'swa', 'swui', 'th.1', 'th.2', 'th.3', 'th.4', 'thb', 'ub.3', 'ub.5', 'usb', 'wc', 'zr', 'zr.1', 'zr.3', 'zzh']
+AHEAD = {'ps5': 3000, 'w1.3': -700, 'pick': 3000, 'i11': 4700, 'eqa': -500, 'tot': 2600, 'cnb.1': 1300, 'oq': 2200, 'sel': 1500, 'dbl': 2500, 'thr': 3300, 's0h': -700, 'bo8a': 3600, 'hwi': 200, 'th.4': 100, 'ldqs': -1900, 'ra': 200, 'rs32': -1000, 'scw.1': -500, 'dm': -2900, 'w1i': -900, 'dn': -1200, 'ldw0': 300, 'f.1': 4200, 'eq.2': 2800, 'scan.1': -1400, 'zr': -1900, 'gx': 5800, 'nk': 1800, 'mki2': -1400, 'oi': 6000, 'oq0': 3100, 'eqi': 1300, 'w1.1': 2500, 'Vi': 3300, 'y': 1400, 'styw': 4000, 'rb': -2000, 'zt': 2000, 'osu': 1500, 'ps7': -700, 'f.2': -800, 'lh': -700, 'f.3': -1500, 'ge': -700, 'ones': 2300, 'owf': 100, 'th.1': 2300, 'col.2': -1900, 'th.5': 300, 'gx.1': 2300, 'gx.3': 500, 'ps4.1': 1100, 'payw': -3600, 'boh': -500, 'dma_': -700, 'scan': 1300, 'owu': 200, 'cap': -2300, 'sc': 100, 'col.1': 3700, 'up': -700, 'sch.1': -400, 'dni': -2200, 'pci2': 5400, 'ldus': 600, 'payh': -1100, 'mvi': 600, 'qt': -600, 'f': 2000, 'fw': -700, 'sel.3': 500, 'ub.5': 1900, 'refill': -900, 'oh': 1700, 'av': -4900, 'cc.2': -500, 'scan.3': -500, 'refill.1': -3100, 'zr.3': -1700, 'eqa.4': 1000, 'px': 1400, 'V.1': 1700, 'l2a': -200, 'gxi': 4800, 'rr': -500, 'hole': 2500, 'bo': 2300, 'cc': 2700, 'ident': -200, 'nin': 2300, 'ldnb': 1500, 'fi': 3000, 'e': -1800, 'o0.1': 1000, 'hba.1': 5000, 'y.2': 300, 'hba': 1000, 'al': -200, 'bo1': 800, 'i2k': -200, 'zzh': -700, 'ldhi': 500, 'ps3': -200, 'swa': -800, 'eq': 1300, 'hbli': 1200, 'cl': -100, 'nki': 200, 'thr.3': -500, 'V': 1000, 'scan.2': 3000, 'o0': 500, 'th': -600, 'col.6': 3200, 'siwi': -800, 'gxi.1': -1300, 'sco': 3800, 'cnb.3': 500, 'eq.4': -1500, 'ldlo': 500, 'eq.3': 900, 'ub.4': 3000, 'col.3': 3700, 'hbl': 200, 'tmp0': -1500, 'eqa.3': 2000, 'zz': 2300, 'eqi.2': -500, 'z8': -700, 'mm_.1': 800, 'l2': 1000, 'wv': 1000, 'rsx': -1000, 'pwi': -2000, 'V.2': -200, 'cc.3': 1000, 'oq0.1': 2000, 'uin': -500, 'siwa': 200, 'bo8': 800, 'wc.1': 2500, 'ub.3': 1200, 'pw3': 2000, 'hb': -1500, 'sel.2': -300, 'ps5.1': 3000, 'sch': -200, 'nk0': 1400, 'im': -2500, 'ps2': 500, 'scw': 200, 'c15.1': 1000, 'zr.1': 500, 'hnew': -200, 'cw': 200, 'eqi.4': -2500, 'cap.1': 300, 'ps4': -2000, 'rsx.1': 500, 'gb': -200, 'nbo': 200, 'ub': -500, 'xv': -1000, 'y.3': -200, 'ch': 200, 'col': 1200, 'cc.1': 500, 'usb': -1000, 'wc': 2000, 'scat': 200, 'wv.1': -2000, 'hb.3': -1000, 'V.3': 2000, 'db': -1000, 'eqi.1': 200, 'ip': 1000, 'dmb': -500, 'hb.1': 1000, 'mm_': 200, 'siw': -500, 'hba.2': -500}
 
 
 def A(name, c0=0, c1=None, st=1, p0=0, p1=128):
@@ -93,9 +78,8 @@ def parts(r):
 
 
 def build(T, rank, par=PAR):
-    CY, PCY, GR, SCR, HOP2, HOPC, FIXA = par
-    ops = []
-    early = [0.0]
+    CY, PCY, GR, SCR = par["cy"], par["pcy"], par["gr"], par["scr"]
+    ops, nth = [], {}
 
     def ap(r):
         if not isinstance(r, tuple):
@@ -114,7 +98,9 @@ def build(T, rank, par=PAR):
                 wr.append(r[1]); rd.append(r[2])
             else:
                 wr.append(r)
-        o = dict(alts=alts, rd=rd, wr=wr, tag=tag, eng=None, early=early[0])
+        tag = tag or wr[0][0]
+        k = nth[tag] = nth.get(tag, -1) + 1
+        o = dict(alts=alts, rd=rd, wr=wr, tag=tag, name=tag + ("." + str(k) if k else ""), eng=None)
         o.update(kw)
         ops.append(o)
         return o
@@ -128,10 +114,10 @@ def build(T, rank, par=PAR):
         rate = 1.0 if any(wide(r) for r in [out] + ins) else 0.5
         if two and all(r[0] in _SB for r in ins):
             rate *= 2
-        return 20 + max(64, n * rate) * CY
+        return par["fv"] + max(64, n * rate) * CY
 
     def acost(out, in_):
-        return 65 + nel(out) * GR * CY if in_[0] == "#" else FIXA + nel(out) * CY
+        return 65 + nel(out) * GR * CY if in_[0] == "#" else par["fa"] + nel(out) * CY
 
     def copy(out, in_, eng="v", tag=""):
         alts = {}
@@ -153,6 +139,9 @@ def build(T, rank, par=PAR):
             alts["a"] = (acost(out, in0), lambda q: q.activation(ap(out), ap(in0), act[0], bias=ap(act[1]), scale=ap(act[2])))
         return add(alts, [in0, s1, s2], [out], tag)
 
+    def lin(out, in0, scale, bias, tag=""):
+        return ts(out, in0, scale, bias, ALU.mult, ALU.add, tag, (AF.Identity, bias, scale))
+
     def tt(out, in0, in1, op, tag=""):
         return add({"v": (vcost(out, [in0, in1], True), lambda q: q.tensor_tensor(ap(out), ap(in0), ap(in1), op))}, [in0, in1], [out], tag)
 
@@ -162,9 +151,6 @@ def build(T, rank, par=PAR):
     def memset(out, val, tag=""):
         return add({"v": (vcost(out, []), lambda q: q.memset(ap(out), val))}, [], [out], tag)
 
-    def reduce_(out, in_, tag=""):
-        return add({"v": (20 + max(64, nel(in_)) * CY, lambda q: q.tensor_reduce(ap(out), ap(in_), AxisListType.X, ALU.add))}, [in_], [out], tag)
-
     def act(out, in_, func, bias=0.0, scale=1.0, accum=None, tag=""):
         if accum is None:
             f = lambda q: q.activation(ap(out), ap(in_), func, bias=ap(bias), scale=ap(scale))
@@ -172,15 +158,14 @@ def build(T, rank, par=PAR):
             f = lambda q: q.activation(ap(out), ap(in_), func, bias=ap(bias), scale=ap(scale), accum_out=ap(accum))
         return add({"a": (acost(out, in_), f)}, [in_, bias, scale], [out] + ([accum] if accum else []), tag)
 
-    def mm(trip, tag="", extra=None, opens=True, closes=True):
+    def mm(trip, tag="", opens=True, closes=True, whole=None):
         def f(q):
-            tr = trip + (extra[0]() if extra else [])
             r = None
-            for i, (o, l, x) in enumerate(tr):
-                r = q.matmul(ap(o), ap(l), ap(x), opens and i == 0, closes and i == len(tr) - 1)
+            for i, (o, l, x) in enumerate(trip):
+                r = q.matmul(ap(o), ap(l), ap(x), opens and i == 0, closes and i == len(trip) - 1)
             return r
-        cost = 60 + sum(max(64, nel(x)) * (4 if wide(x) else 1) * PCY for _, _, x in trip)
-        return add({"p": (cost, f)}, [r for tr in trip for r in tr[1:]] + (extra[1] if extra else []), [tr[0] for tr in trip], tag)
+        cost = par["fp"] + sum(max(64, nel(x)) * (4 if wide(x) else 1) * PCY for _, _, x in trip)
+        return add({"p": (cost, f)}, [r for tr in trip for r in tr[1:]], [tr[0] for tr in trip] + ([A(whole)] if whole else []), tag)
 
     def iota(out, pat, base, cm, tag=""):
         if _SB[out[0]][1] == I32:
@@ -191,6 +176,12 @@ def build(T, rank, par=PAR):
 
     def sel(out, in_, pat, cmp_, fill, base, cm, tag=""):
         return add({"g": (170 + 2 * CY * nel(out), lambda q: q.affine_select(ap(out), ap(in_), pat, cmp_, fill, base, cm))}, [in_], [out], tag)
+
+    def send(kind, t, reads):
+        return add({"g": (par["call"], (kind, t))}, reads, [], "%s%d" % (kind, t), remote=True)
+
+    def arrive(sem, writes, lat, after):
+        return add({}, [], writes, sem, done=(sem, None), lat=lat, after=after)
 
     rot = (-DG * rank) % 8
 
@@ -211,23 +202,26 @@ def build(T, rank, par=PAR):
         def f(e):
             for h0, s0, n in pieces(16):
                 e.dma_start(T[name][h0:h0 + n, :], T[buf][s0:s0 + n, 0:C]).then_inc(T.sem[sem], 16)
-        return add({q: (120.0, f)}, [A(buf, 0, C)], [], "st" + name, done=(sem, 16 * len(pieces(16))), lat=2500.0)
+        return add({q: (120.0, f)}, [A(buf, 0, C)], [], "st" + name, done=(sem, 16 * len(pieces(16))), lat=2200.0)
 
-    def O(b):
-        return A("zz", 15 - b, 143 - b)
+    def O(b, name="zz"):
+        return A(name, 15 - b, 143 - b)
 
     def O8(b):
         return A("z8", 15 - b, 143 - b, 1, 0, 8)
 
-    load("s0", "s0i", 0, C, 1, 1, "s", 2000.0)
-    load("nb", "nbt", 0, V, 16, 16, "s", 5000.0)
-    load("qs", "qt", 16, V + 16, 16, 16, "a", 5500.0)
-    load("us", "usi", 0, C, 1, NT, "a", 3000.0)
-    load("w0", "w0s", 0, C, 16, 16, "s", 5500.0)
-    load("coin", "cni", 0, NT * C, 1, 1, "s", 5500.0)
+    def SEL(p):
+        return A("sel", 128 * p, 128 * p + 128)
+
+    load("nb", "nbt", 0, V, 16, 16, "s", par["nb"])
+    load("s0", "s0i", 0, C, 1, 1, "a", 2000.0)
+    load("us", "usi", 0, C, 1, NT, "a", 2200.0)
+    load("qs", "qt", 16, V + 16, 16, 16, "s", par["qs"])["after"] = "ldnb"
+    load("w0", "w0s", 0, C, 16, 16, "s", par["qs"])["after"] = "ldqs"
+    load("coin", "cni", 0, NT * C, 1, 1, "a", 2500.0)
     memset(A("lh"), 0.0)
-    load("lo", "lh", 0, NT, 16, 16, "s", 5500.0)
-    load("hi", "lh", 8, 8 + NT, 16, 16, "s", 5500.0)
+    load("lo", "lh", 0, NT, 16, 16, "s", par["qs"])["after"] = "ldw0"
+    load("hi", "lh", 8, 8 + NT, 16, 16, "s", par["qs"])["after"] = "ldlo"
     memset(A("ones"), 1.0)
     memset(A("qt", 0, 16), 0.0)
     sel(A("z8", p1=8), A("ones", 0, 144, p1=8), [[1, 144]], ALU.is_equal, 0.0, -15, -16)
@@ -237,270 +231,238 @@ def build(T, rank, par=PAR):
     sel(A("zt", p1=40), A("ones", p1=40), [[-1, NT], [-NT, 8], [0, 16]], ALU.is_equal, 0.0, 0, 1)
     sel(A("bo1"), A("ones", 0, 128), [[-16, 8], [0, 16]], ALU.is_ge, 0.0, 0, 1)
     sel(A("bo"), A("bo1"), [[16, 8], [0, 16]], ALU.is_ge, 0.0, 15, -1)
-    ts(A("nbo"), A("bo"), -1.0, None, ALU.mult)
+    lin(A("nbo"), A("bo"), -1.0, 0.0)
+    lin(A("boh"), A("bo"), 0.5, 0.0)
     sel(A("dma_"), A("nbo"), [[-1, 128]], ALU.is_equal, 0.0, -1, 1)
-    sel(A("dm"), A("dma_"), [[-1, 128]], ALU.not_equal, 1.0, 0, 1)
+    sel(A("dmb"), A("dma_"), [[-1, 128]], ALU.not_equal, 1.0, 0, 1)
+    sel(A("dm"), A("dmb"), [[-16, 8], [-128, 16]], ALU.not_equal, 1.0, 15 * 128, 1)
     sel(A("l2a"), A("nbo"), [[-1, 128]], ALU.is_gt, 0.0, 0, 1)
-    sel(A("l2"), A("l2a"), [[-1, 128]], ALU.not_equal, -1024.0, 0, 1)
-    nmk = C + S if OPT["rbv"] else 2 * S if "l" in OPT["wrapv"] else S
-    iota(A("mki", 0, nmk), [[0, nmk // 16], [-1, 16]], 16, 1)
+    sel(A("l2"), A("l2a"), [[-1, 128]], ALU.not_equal, -2048.0, 0, 1)
+    iota(A("mki"), [[0, S // 16], [-1, 16]], 16, 1)
     iota(A("ids"), [[1, C]], 0, 0)
     iota(A("pci"), [[0, 8]], 0, 1)
     sel(A("jj"), A("ones", 0, 256), [[0, 2], [-1, 128]], ALU.is_equal, 0.0, 0, 1)
-    ts(A("i11"), A("ident"), 2.0 ** -11, None, ALU.mult)
-    ts(A("i2k"), A("ident"), -4096.0, None, ALU.mult)
-    ts(A("ip"), A("ident"), 16.0 * WN, None, ALU.mult)
-    ts(A("im"), A("ident"), -16.0 * WN, None, ALU.mult)
+    lin(A("i11"), A("ident"), 2.0 ** -11, 0.0)
+    lin(A("i2k"), A("ident"), -4096.0, 0.0)
+    lin(A("ip"), A("ident"), 16.0 * WN, 0.0)
+    lin(A("im"), A("ident"), -16.0 * WN, 0.0)
     memset(A("zz"), 0.0)
     copy(A("zz", 15, 143, 16), A("bo", 0, 128, 16))
-    ts(A("mki2", 0, nmk), A("mki", 0, nmk), 15, None, ALU.bitwise_and)
-    ts(A("mk1"), A("mki2", 0, 16), 0.0, None, ALU.is_equal)
-    if OPT["rbv"]:
-        ts(A("mask"), A("mki2"), 0.0, 16.0, ALU.is_equal, ALU.mult)
-    else:
-        ts(A("mask", 0, nmk), A("mki2", 0, nmk), 0.0, None, ALU.is_equal)
+    lin(A("zzh"), A("zz"), 0.5, 0.0)
+    memset(A("c15"), 0.0); memset(A("c15", 15, 128, 16), -16.0)
+    ts(A("mki2"), A("mki"), 15, None, ALU.bitwise_and)
+    ts(A("pick"), A("mki2"), 0.0, 4096.0, ALU.is_equal, ALU.mult)
+    ts(A("col", 24, 29), A("mki2", 0, 5), 0.0, None, ALU.is_equal)
     for p in range(5):
-        ts(A("sel", 128 * p, 128 * p + 128), A("bo"), A("mk1", p, p + 1), None, ALU.mult)
-    memset(A("c16"), 16.0)
+        lin(SEL(p), A("bo"), A("col", 24 + p, 25 + p), 0.0)
+    for t in range(1, NT):
+        lin(A("zr", 144 * (t - 1), 144 * t), A("zz"), A("col", 24 + t, 25 + t), 0.0)
     ts(A("pci2"), A("pci"), 15, None, ALU.bitwise_and)
     copy(A("col", 0, 1), A("pci2", 0, 1))
-    ts(A("col", 1, 2), A("col", 0, 1), 15.0, 18.0, ALU.is_lt, ALU.mult)
-    ts(A("col", 2, 3), A("col", 1, 2), -1.0, None, ALU.add)
+    ts(A("col", 1, 2), A("col", 0, 1), 15.0, -(16 * BASE + 8.5 * 4096 + 1), ALU.is_lt, ALU.mult)
+    ts(A("col", 2, 3), A("col", 1, 2), 1.0, None, ALU.add)
+    ts(A("col", 3, 4), A("col", 0, 1), NT + 0.5, MID + 1, ALU.is_lt, ALU.mult)
+    ts(A("col", 5, 6), A("col", 3, 4), -1.0, None, ALU.add)
     ts(A("cw"), A("ids", 0, C, 16), A("col", 0, 1), None, ALU.add)
-    memset(A("cc"), 1023.0 + RC)
-    memset(A("cc", 0, 48, 3), 1023.0)
+    memset(A("cc"), 2047.0 + RC)
+    memset(A("cc", 0, 48, 3), 2047.0)
     ts(A("cc", 2, 48, 3), A("cw"), float(RD), None, ALU.add)
     ts(A("cc", 50, 96, 3), A("cw"), float(RI), None, ALU.add)
     copy(A("cc", 98, 108, 3), A("cw", 0, 4))
-    ts(A("cc", 110, 120, 3), A("cw", 0, 4), float(RC), None, ALU.add)
-    memset(A("cc", 120, 136), 16.0 * WN)
-    memset(A("cc", 136, 144), 0.0)
-    memset(A("rs16"), 1.0); memset(A("rs16", 0, C + S, 16), 0.0)
-    if OPT["count"]:
-        ts(A("bo2"), A("bo"), -2.0, None, ALU.mult)
-        ts(A("bo16", p1=8), A("bo8", p1=8), -16.0, None, ALU.mult)
-        memset(A("col", 15, 16), 23.5)
-        ts(A("bia", 4, 7), A("cw", 0, 3), 2.0, C + 1.0, ALU.mult, ALU.add)
-    memset(A("rs32"), 1.0); memset(A("rs32", 0, 72, 52), 0.0)
+    memset(A("cc", 108, 112), 0.0)
+    memset(A("cc", 128, 144), 16.0 * WN)
+    memset(A("rs32"), 1.0); memset(A("rs32", 0, 84, 64), 0.0)
     memset(A("fw"), 0.0)
-    memset(A("rsx"), 0.0); memset(A("rsx", 0, 120, 3), 4096.0)
-    for t in range(1, NT if OPT["wrapv"] != "il" else 0):
-        ts(A("zr", 144 * (t - 1), 144 * t), A("zz"), A("mk1", t, t + 1), None, ALU.mult)
-    for name in ("d0a", "d0b"):
-        for a in (0, 512):
-            o = memset(A(name, a, a + 512), 8192.0, "big")
-            o["alts"]["g"] = sel(A(name, a, a + 512), A("ones", 0, 512), [[0, 512]], ALU.is_gt, 8192.0, 0, 0)["alts"]["g"]
-            o["rd"] = ops.pop()["rd"]
+    memset(A("rsx"), 0.0); memset(A("rsx", 0, 109, 3), 4096.0)
+    ncap = 16 * max([c1 - c0 for c0, c1 in CHUNKS] + [S])
+    memset(A("cap", 0, ncap), 2.0 ** 20); memset(A("cap", 0, ncap, 16), BASE)
     memset(A("ub", NT * C, NT * C + WN - C), 0.0)
     memset(A("wv", C, WN), 0.0); memset(A("wv", WN + C, 2 * WN), 0.0)
-    memset(A("hw", C, WN), -1.0);
+    memset(A("hw", C, WN), -1.0); memset(A("pw", C, WN), -4096.0)
     memset(A("wc", C, WN), 0.0); memset(A("h32", C, WN), 0.0)
     memset(A("th"), 9.0)
-    copy(A("mm_", RD, RI), A("ids"), "va"); copy(A("mm_", RI, MW), A("ids"), "va")
-    ts(A("usb", p1=40), A("usi", p1=40), -8.0, None, ALU.mult)
+    memset(A("mm_", RC + S, RI), 0.0); copy(A("mm_", RI, MW), A("ids"), "va")
+    lin(A("usb", p1=40), A("usi", p1=40), -8.0, 0.0)
     for t in range(NT):
         bank = A(["ps2", "ps4", "ps4", "ps5", "ps5"][t], [0, 0, 256, 0, 256][t], [256, 256, 512, 256, 512][t])
         mm([(bank, A("zt", 128 * t, 128 * t + 128, 1, 0, 40), A("usb", p1=40))])
-        copy(A("ub", C * t, C * t + C), bank, "va")
-    ts(A("s0h", p1=8), A("s0i", p1=8), 1.0, None, ALU.add)
+        lin(A("ub", C * t, C * t + C), bank, 1.0, -2.0 ** -10)
+    lin(A("s0h", p1=8), A("s0i", p1=8), 1.0, -MID)
     s0h = A("s0h", p1=8)
     mm([(A("ps3", 320, 336), O8(b), A("s0h", b, C, 16, 0, 8)) for b in range(16)])
     mm([(A("ps6", 0, C), A("bo8", p1=8), s0h)])
     mm([(A("ps1", 0, C), O8(0), s0h)])
-    ts(A("swu", 0, 16), A("ps3", 320, 336), -1.0, None, ALU.add)
-    ts(A("nk", 0, C), IND(A("nbt"), A("swu", 0, 16)), 1.0, None, ALU.add)
-    tt(A("eq", 0, C), A("nk", 0, C), A("ps6", 0, C), ALU.is_equal)
-    ts(A("tmp0"), A("ps6", 0, C), 0.0, None, ALU.is_gt)
-    copy(A("h16", 0, C), A("ps1", 0, C))
-    mm([(A("ps1", C, 2 * C), A("ident"), A("nk", 0, C)), (A("ps1", C, 2 * C), A("i2k"), A("eq", 0, C))])
-    ts(A("oq", 0, C), A("ps1", C, 2 * C), 0.0, 15.0, ALU.max, ALU.add)
-    ts(A("of", 0, C), A("ps1", C, 2 * C), 0.0, None, ALU.max, act=(AF.Relu, 0.0, 1.0))
+    lin(A("swu", 0, 16), A("ps3", 320, 336), 1.0, MID)
+    ts(A("tmp0"), A("ps6", 0, C), -MID - 0.5, None, ALU.is_gt)
+    copy(A("h16"), A("ps1", 0, C), "va")
+    for j, (c0, c1) in enumerate(FIRST):
+        nk, eq, po = A("nk", c0, c1), A("eq", c0, c1), A("ps%d" % (2 + j), 384, 384 + c1 - c0)
+        lin(nk, IND(A("nbt"), A("swu", c0 // 16, c1 // 16)), 1.0, -MID, "nk0")
+        tt(eq, nk, A("ps6", c0, c1), ALU.is_equal, "eq0")
+        mm([(po, A("ident"), nk), (po, A("i2k"), eq)], "o0")
+        lin(A("oq", c0, c1), po, 1.0, MID + 16, "oq0")
     tt(A("wc", 0, C), A("w0s"), A("tmp0"), ALU.mult)
     act(A("al0"), A("tmp0"), AF.Identity, accum=A("col", 4, 5))
     ts(A("col", 8, 9), A("col", 4, 5), -float(C), None, ALU.add)
     for t in range(NT):
-        copy(A("cnb", C * t, C * t + C, 1, 0, 8), A("cni", C * t, C * t + C, 1, 0, 8), "vg", "cnb")
+        copy(A("cnb", C * t, C * t + C, 1, 0, 8), A("cni", C * t, C * t + C, 1, 0, 8), "g", "cnb")
     mm([(A("ps7", 0, 80), O8(b), A("cnb", b, NT * C, 16, 0, 8)) for b in range(16)])
     for t in range(NT):
-        ts(A("th", 48 * t, 48 * t + 16), A("ps7", 16 * t, 16 * t + 16), 90.0, 9.0, ALU.mult, ALU.add)
-    ts(A("thb"), A("ps7", 0, 80), -90.0, 99.0, ALU.mult, ALU.add)
+        lin(A("th", 48 * t, 48 * t + 16), A("ps7", 16 * t, 16 * t + 16), 90.0, 9.0)
+    lin(A("thb"), A("ps7", 0, 80), -90.0, 99.0)
 
-    nd0 = [0]
-
-    def grow1(t, c0, c1, fb, ucol, step):
+    def sums(c0, c1, x0, fb, step, x):
         for a in range(c0, c1, step):
-            copy(A("xx", 16 * a, 16 * (a + step)), IND(A("qt"), A("oq", a, a + step)), "va", "gx")
-        mm([(fb, A("i11"), A("xx", 16 * c0 + k, 16 * c1, 16)) for k in range(16)], "f")
-        tt(A("thr", c0, c1), fb, ucol, ALU.mult, "thr")
+            copy(A("xx", x0 + 16 * (a - c0), x0 + 16 * (a - c0 + step)), IND(A("qt"), A("oq", a, a + step)), "va", "gx" + x)
+        mm([(fb, A("i11"), A("xx", x0 + k, x0 + 16 * (c1 - c0), 16)) for k in range(16)], "f" + x)
 
-    def grow2(c0, c1, vb):
-        d0 = ["d0a", "d0b"][nd0[0] % 2]; nd0[0] += 1
+    def votes(c0, c1, x0, fb, ucol, vb, x):
         n = 16 * (c1 - c0)
-        y = OFFS + 255.0 / 512.0
-        ts(A("yy", c0, c1), A("thr", c0, c1), y, None, ALU.add, tag="y", act=(AF.Identity, A("col", 13, 14), 1.0))["rd"].append(A("col", 13, 14))
-        ts(A(d0, 0, n, 16), A("yy", c0, c1), MAGIC, -MAGIC, ALU.add, ALU.add, tag="d0")
-        scan(A("ee", 16 * c0, 16 * c1), A(d0, 0, n), A("xx", 16 * c0, 16 * c1), 4096.0, ALU.min, ALU.add, "scan")
-        so = ts(A("sg", 16 * c0, 16 * c1), A("ee", 16 * c0, 16 * c1), OFFS, 2.0, ALU.is_gt, ALU.mult, "sign", act=(AF.Sign, A("col", 12, 13), 1.0))
-        so["rd"].append(A("col", 12, 13))
-        ex = (lambda: [(vb, A("ident"), A("c16", 0, c1 - c0))] if so["eng"] == "a" else [], [A("ident"), A("c16")])
-        mm([(vb, O(k), A("sg", 16 * c0 + k, 16 * c1, 16)) for k in range(15)], "V", ex)
+        tt(A("yy", c0, c1), fb, ucol, ALU.mult, "y" + x)
+        ts(A("xx", x0 - 1, x0 - 1 + n, 16), A("yy", c0, c1), 0.5 - TWO23, TWO23 + 2048, ALU.add, ALU.add, tag="thr" + x)
+        scan(A("ee", x0, x0 + n), A("cap", 0, n), A("xx", x0 - 1, x0 - 1 + n), 2.0 ** 20, ALU.min, ALU.add, "scan" + x)
+        mm([(vb, O(k), A("ee", x0 + 1 + k, x0 + n, 16)) for k in range(15)], "V" + x)
 
-    def sites(t, c0, c1, vb, dn, ph, hw, x):
-        ge, mv = A("ge", c0, c1), A("mv", c0, c1)
-        ts(ge, vb, A("col", 2, 3), None, ALU.is_gt, tag="ge" + x)
-        tt(mv, dn, ge, ALU.mult, "mv" + x)
-        mm([(ph, A("ident"), A("landh", S * (t - 1), S * t) if x else A("h16", c0, c1)), (ph, O(t + 1), mv)], "hnew" + x)
+    def sites(t, c0, c1, vb, dn, ph, old, hw, x):
+        sg, mv = A("sg", c0, c1), A("mv", c0, c1)
+        act(sg, vb, AF.Sign, bias=A("col", 2, 3), tag="ge" + x)
+        tt(mv, dn, sg, ALU.mult, "mv" + x)
+        mm([(ph, A("ident"), old), (ph, O(t + 1, "zzh"), mv)], "hnew" + x)
         if t == NT - 1:
-            ts(hw, ph, -1.0, None, ALU.add, tag="hw" + x, act=(AF.Identity, A("col", 14, 15), 1.0))["rd"].append(A("col", 14, 15))
+            ts(hw, ph, A("col", 5, 6), None, ALU.add, tag="hw" + x, act=(AF.Identity, A("col", 5, 6), 1.0))
         else:
             copy(hw, ph, "va", "hw" + x)
 
-    def head(t, c0, c1, pw, hb, po, eq, x):
-        swu, nk = A("swu", c0 // 16, c1 // 16), A("nk", c0, c1)
-        byv = ("i" if x else "l") in OPT["wrapv"]
-        if not byv:
-            mm([(pw, A("zr", 144 * (t - 1) + 15 - b, 144 * (t - 1) + 143 - b), A("h16", c0 + b, c1, 16)) for b in range(16)], "siw" + x)
-        for p in range(t, -1, -1):
-            mm([(hb[p], A("sel", 128 * p, 128 * p + 128), A("landh", S * (t - 1), S * t) if x else A("h16", c0, c1))], "hb" + x)
-        if byv:
-            tt(A("sm", c0, c1), hb[t], A("mask", 0, c1 - c0), ALU.mult, "sm" + x)
-            scan(A("sn", c0, c1), A("rs16", 0, c1 - c0), A("sm", c0, c1), 0.0, ALU.mult, ALU.add, "sn" + x)
-            pw = A("sn", c0 + 15, c1, 16)
-        ts(swu, pw, -1.0, None, ALU.add, tag="swu" + x)
-        ts(nk, IND(A("nbt"), swu), 1.0, None, ALU.add, tag="nk" + x)
-        for p in range(t + 1):
-            tt(eq[p], nk, hb[p], ALU.is_equal, "eq" + x)
-        mm([(po, A("ident"), nk)] + [(po, A("i2k"), r) for r in eq], "o" + x)
-        ts(A("oq", c0, c1), po, 0.0, 15.0, ALU.max, ALU.add, tag="oq" + x)
-        ts(A("of", c0, c1), po, 0.0, None, ALU.max, tag="of" + x, act=(AF.Relu, 0.0, 1.0))
+    def shut(nk, swu, hb, eq, po, x):
+        lin(nk, IND(A("nbt"), swu), 1.0, -MID, "nk" + x)
+        for b, e in zip(hb, eq):
+            tt(e, nk, b, ALU.is_equal, "eq" + x)
+        mm([(po, A("ident"), nk)] + [(po, A("i2k"), e) for e in eq], "o" + x)
 
-    memset(A("col", 12, 13), -OFFS)
-    memset(A("col", 13, 14), OFFS + 255.0 / 512.0)
-    memset(A("col", 14, 15), -1.0)
+    def ahead(c0, c1, sw, hb, eq, po, out, x):
+        mv, swu = A("mv", c0, c1), A("swu", c0 // 16, c1 // 16)
+        mm([(sw, O(b), A("mv", c0 + b, c1, 16)) for b in range(16)], "siw" + x)
+        mm([(hb[-1], A("boh"), mv)], "hbl" + x)
+        lin(swu, sw, 0.5, MID, "swu" + x)
+        shut(A("nn", c0, c1), swu, hb, eq, po, x)
+        copy(out, po, "va", "pw" + x)
+
     HL = A("oh", 16, 19)
+    XI = 16 * (C + len(CHUNKS) + 2)
     for t in range(NT):
         last = t == NT - 1
+        nth.clear()
         P0 = t * PAYW
         L0 = (t - 1) * PAYW
-        iota(A("mm_", 0, RC), [[0, RC // S], [2, S]], NONE + 2, 0, "refill")
-        iota(A("mm_", RC, RD), [[0, RD - RC]], NONE, 0, "refill")
+        iota(A("mm_", 0, 7 * S), [[0, 7], [2, S]], NONE + 2, 0, "refill")
+        iota(A("mm_", 7 * S, RC + S), [[0, RC - 6 * S]], NONE, 0, "refill")
+        vb, dn, ph, po, *hb = [A("ps%d" % (2 + k // 2), C * (k % 2), C * (k % 2) + C) for k in range(8)]
+        mm([(dn, A("dm"), A("nk", 0, C))] + ([(dn, A("c15"), A("ones", 0, C))] if t else []), "dn")
+        for p in range(0 if last else t + 1):
+            mm([(hb[p], SEL(p), A("h16"))], "hb")
+        for i, (c0, c1) in enumerate(CHUNKS):
+            fb, x0 = A("ps%d" % (i % 2), c0, c1), 16 * (c0 + i + 1)
+            sums(c0, c1, x0, fb, GSTEP, "")
+            tt(A("wv", WN + c0, WN + c1), fb, A("wc", c0, c1), ALU.mult, "w1")
+            votes(c0, c1, x0, fb, A("ub", C * t + c0, C * t + c1), A("ps2", c0, c1), "")
+        sites(t, 0, C, vb, dn, ph, A("h16"), A("hw", 0, C), "")
+        if not last:
+            ahead(0, C, A("ps2", C, C + 16), hb[:t + 1] + [vb], [A("eq", C * p, C * p + C) for p in range(t + 2)], po, A("pw", 0, C), "")
         if t > 0:
-            add({}, [], [A("cnt", N * (t - 1), N * t)], "arrc", done=("cnt%d" % (t - 1), None), lat=HOPC, after="sc%d" % (t - 1))
+            arrive("cnt%d" % (t - 1), [A("cnt", N * (t - 1), N * t)], par["hopc"], "sc%d" % (t - 1))
             tr = []
             for r in range(N):
                 s = (-16 * DG * (r - rank)) % 128
                 x = A("dcol", 8 * (t - 1), 8 * (t - 1) + 1) if r == rank else A("cnt", N * (t - 1) + r, N * (t - 1) + r + 1)
-                tr.append((A("ps3", 304, 305), A("jj", s, s + 128), x))
+                tr.append((A("ps6", 0, 1), A("jj", s, s + 128), x))
             mm(tr, "tot")
-            ts(A("col", 16, 17), A("ps3", 304, 305), 0.0, 1.0, ALU.is_gt, ALU.add, tag="up")
+            ts(A("col", 16, 17), A("ps6", 0, 1), 0.0, 1.0, ALU.is_gt, ALU.add, tag="up")
             ts(A("lh"), A("lh"), A("col", 16, 17), None, ALU.mult, tag="lh", act=(AF.Identity, 0.0, A("col", 16, 17)))
-        for i, (c0, c1) in enumerate(CHUNKS):
-            early[0] = 1.0 - c1 / C
-            fb = A("ps%d" % (i % 2), c0, c1)
-            grow1(t, c0, c1, fb, A("ub", C * t + c0, C * t + c1), GSTEP)
-            tt(A("wv", WN + c0, WN + c1), fb, A("wc", c0, c1), ALU.mult, "w1")
-            grow2(c0, c1, A("ps2", c0, c1))
-        mm([(A("ps3", 0, C), A("dm"), A("of", 0, C))], "dn")
-        for c0, c1 in CHUNK2:
-            early[0] = 1.0 - c1 / C
-            sites(t, c0, c1, A("ps2", c0, c1), A("ps3", c0, c1), A("ps0", C + c0, C + c1), A("hw", c0, c1), "")
-        if t > 0:
-            add({}, [], [A("land", L0, L0 + PAYW)], "arr", done=("arr%d" % (t - 1), None), lat=HOP2, after="sp%d" % (t - 1))
+            old = A("landh", S * (t - 1), S * t)
             copy(A("uin"), IND(A("ub", C * t, C * t + WN), HL), "va", "uin")
-            add({}, [], [A("landh", S * (t - 1), S * t)], "arh", done=("arh%d" % (t - 1), None), lat=HOP2 - 500, after="sh%d" % (t - 1))
-            head(t, C, C + S, A("ps3", 504, 507), [A("ps7", S * p, S * p + S) for p in range(t + 1)], A("ps3", 456, 504),
-                 [A("eqi", S * p, S * p + S) for p in range(t + 1)], "i")
-            fb = A("ps7", 240, 288)
-            grow1(t, C, C + S, fb, A("uin"), 24)
+            arrive("arh%d" % (t - 1), [old], par["hop"], "sh%d" % (t - 1))
+            arrive("arr%d" % (t - 1), [A("land", L0, L0 + PAYW)], par["hop"], "sp%d" % (t - 1))
+            sw, po, fb, vb, dn = A("ps7", 240, 243), A("ps7", 244, 292), A("ps7", 292, 340), A("ps7", 340, 388), A("ps7", 388, 436)
+            hb = [A("ps7", S * p, S * p + S) for p in range(NT)]
+            mm([(sw, A("zr", 144 * (t - 1) + 15 - b, 144 * (t - 1) + 143 - b), A("landh", S * (t - 1) + b, S * t, 16)) for b in range(16)], "siwa")
+            for p in range(t + 1):
+                mm([(hb[p], SEL(p), old)], "hba")
+            lin(A("swa", 0, 3), sw, 1.0, MID, "swa")
+            shut(A("nk", C, C + S), A("swa", 0, 3), hb[:t + 1], [A("eqa", S * p, S * p + S) for p in range(t + 1)], po, "a")
+            lin(A("oq", C, C + S), po, 1.0, MID + 16, "oqa")
+            mm([(dn, A("dm"), A("nk", C, C + S))], "dni")
+            sums(C, C + S, XI, fb, GSTEPI, "i")
             tt(A("w1i"), fb, A("land", L0, L0 + S), ALU.mult, "w1i")
             copy(IND(A("wv", WN, 2 * WN), HL), A("w1i"), tag="scw")
             if not last:
                 ts(A("col", 20, 21), A("land", L0 + S, L0 + S + 1), 0.0, float(S), ALU.max, ALU.min, tag="nin")
                 ts(A("col", 8, 9), A("col", 20, 21), A("pay", L0 + S, L0 + S + 1), 0.0, ALU.add, ALU.min, tag="db")
-            mm([(A("ps3", 360, 408), A("dm"), A("of", C, C + S))], "dni")
-            grow2(C, C + S, A("ps3", C, C + S))
-            sites(t, C, C + S, A("ps3", C, C + S), A("ps3", 360, 408), A("ps3", 408, 456), A("hwi"), "i")
+            votes(C, C + S, XI, fb, A("uin"), vb, "i")
+            sites(t, C, C + S, vb, dn, A("ps7", 436, 484), old, A("hwi"), "i")
             copy(IND(A("hw"), HL), A("hwi"), tag="sch")
+            if not last:
+                ahead(C, C + S, sw, hb[:t + 2], [A("eqi", S * p, S * p + S) for p in range(t + 2)], po, A("pwi"), "i")
+                copy(IND(A("pw"), HL), A("pwi"), tag="sco")
         W1 = A("wv", WN, WN + C)
         ts(A("fl", 2 * C, 3 * C), W1, A("lh", 8 + t, 9 + t), None, ALU.is_gt, tag="ch")
         ts(A("fl", 0, C), W1, A("lh", t, t + 1), None, ALU.is_lt, tag="cl")
         ts(A("fl", C, 2 * C), W1, 0.0, None, ALU.is_gt, tag="al", act=(AF.Sign, 0.0, 1.0))
-        ts(A("wv", 0, C), W1, 0.5, None, ALU.mult, tag="half", act=(AF.Identity, 0.0, 0.5))
-        ts(A("wv", 2 * WN, 2 * WN + C), W1, 2.0, None, ALU.mult, tag="twice", act=(AF.Identity, 0.0, 2.0))
-        mm([(A("ps7", 288, 336), O(b), A("fl", b, 3 * C, 16)) for b in range(16)], "pw")
-        tt(A("fw", 20, 68), A("ps7", 288, 336), A("th", 48 * t, 48 * t + 48), ALU.is_ge, "fw")
-        tt(A("dbl"), A("ps7", 288, 304), A("thb", 16 * t, 16 * t + 16), ALU.is_ge, "dbl")
-        die, alive, high, hole = A("fw", 20, 36), A("fw", 36, 52), A("fw", 52, 68), A("fw", 0, 16)
+        lin(A("wv", 0, C), W1, 0.5, 0.0, "half")
+        lin(A("wv", 2 * WN, 2 * WN + C), W1, 2.0, 0.0, "twice")
+        mm([(A("ps6", 16, 64), O(b), A("fl", b, 3 * C, 16)) for b in range(16)], "pw3")
+        tt(A("fw", 32, 80), A("ps6", 16, 64), A("th", 48 * t, 48 * t + 48), ALU.is_ge, "fw")
+        tt(A("dbl"), A("ps6", 16, 32), A("thb", 16 * t, 16 * t + 16), ALU.is_ge, "dbl")
+        die, alive, high, hole = A("fw", 32, 48), A("fw", 48, 64), A("fw", 64, 80), A("fw", 0, 16)
         tt(hole, die, alive, ALU.is_ge, "hole")
         scan(A("sc"), A("rs32"), A("fw"), 0.0, ALU.mult, ALU.add, "sc")
-        X = 368
-        sh, sc_ = A("sc", 0, 16), A("sc", 52, 68)
-        xa, xb, xc, xv = A("ps7", X, X + 48, 3), A("ps7", X + 1, X + 48, 3), A("ps7", X + 48, X + 96, 3), A("ps7", X + 120, X + 136)
-        ex = A("ps7", X + 136, X + 137)
-        mm([(A("ps7", X, X + 144), A("ident"), A("cc")),
-            (xv, A("ip"), A("dbl")), (xv, A("im"), die), (xv, A("im"), high),
-            (xb, A("l2"), high), (xa, A("l2"), hole), (xc, A("l2"), hole)], "px0", closes=False)
-        mm([(xa, A("bo"), sh), (xb, A("bo"), sc_), (xc, A("bo"), sh),
-            (A("ps7", X + 98, X + 108, 3), A("bo"), A("sc", 68, 72)), (A("ps7", X + 110, X + 120, 3), A("bo"), A("sc", 16, 20)),
-            (ex, A("bo"), A("sc", 68, 69)), (ex, A("nbo"), A("sc", 16, 17))], "px", opens=False)
-        scan(A("rr"), A("rsx"), A("ps7", X, X + 120), 0.0, ALU.max, ALU.min, "rr")
-        copy(A("of2"), A("rr", 2, 120, 3), tag="of2")
-        ec = A("pay", P0 + S, P0 + S + 1)
-        copy(ec, ex, "va", "e")
-        tt(A("av"), xv, alive, ALU.mult, "av")
+        X = 64
+        sh, sc_, nh = A("sc", 0, 16), A("sc", 64, 80), A("sc", 16, 32)
+        xa, xb, xc, xv = A("ps6", X, X + 48, 3), A("ps6", X + 1, X + 48, 3), A("ps6", X + 48, X + 96, 3), A("ps6", X + 128, X + 144)
+        ex = A("ps6", X + 108, X + 109)
+        mm([(A("ps6", X, X + 112), A("ident"), A("cc", 0, 112)),
+            (xb, A("l2"), high), (xa, A("l2"), hole), (xc, A("l2"), hole)], "px0", closes=False, whole="ps6")
+        mm([(xa, A("bo"), sh), (xb, A("bo"), sc_), (xb, A("nbo"), nh), (xc, A("bo"), sh), (xc, A("nbo"), nh),
+            (A("ps6", X + 98, X + 108, 3), A("bo"), A("sc", 80, 84)),
+            (ex, A("bo"), A("sc", 80, 81)), (ex, A("nbo"), A("sc", 16, 17))], "px", opens=False, whole="ps6")
+        scan(A("rr", 0, 109), A("rsx", 0, 109), A("ps6", X, X + 109), 0.0, ALU.max, ALU.min, "rr")
+        copy(A("of2", 0, 36), A("rr", 2, 108, 3), "va", "of2")
+        mm([(xv, A("ident"), A("cc", 128, 144)), (xv, A("ip"), A("dbl")), (xv, A("im"), die), (xv, A("im"), high)], "xv")
+        ee = A("rr", 108, 109)
+        copy(A("pay", P0 + S, P0 + S + 1), ee, "va", "e")
         if not last:
             dc = A("dcol", 8 * t, 8 * t + 1)
-            ts(dc, ex, A("col", 8, 9), None, ALU.subtract, tag="d")
-            add({"g": (1200.0, ("cnt", t))}, [dc], [], "sc%d" % t, remote=True)
+            ts(dc, ee, A("col", 8, 9), None, ALU.subtract, tag="d")
+            send("sc", t, [dc])
         copy(IND(A("mm_"), A("of2", 0, 16)), A("ids"), tag="scat")
-        if OPT["count"]:
-            mm([(A("ps0", 0, C), A("bo"), A("fl", 2 * C, 3 * C))], "bh")
-            mm([(A("ps1", 0, C), A("bo"), A("fl", 0, C)), (A("ps1", 0, C), A("bo2"), A("fl", C, 2 * C)),
-                (A("ps1", 0, C), A("bo16", p1=8), A("cnb", C * t, C * t + C, 1, 0, 8))], "ba")
-            ts(A("hb_"), A("ps0", 0, C), 9.0, None, ALU.is_ge, tag="hb_")
-            scan(A("pcb"), A("ones", 0, C), A("hb_"), 0.0, ALU.mult, ALU.add, "pcb")
-            act(A("al0"), A("ps1", 0, C), AF.Sign, bias=A("col", 15, 16), accum=A("col", 24, 25), tag="nhb")
-            ts(A("bia", 0, 3), A("bia", 4, 7), A("col", 24, 25), None, ALU.add, tag="bia", act=(AF.Identity, A("col", 24, 25), 1.0))
-            for a in range(3):
-                act(A("jnk", C * a, C * a + C), A("pcb"), AF.Sign, bias=A("bia", a, a + 1), scale=-2.0, accum=A("bia", 8 + a, 9 + a), tag="cnt")
-            ts(A("osu", 0, 3), A("bia", 8, 11), 0.5, C / 2.0, ALU.mult, ALU.add, tag="osu")
-        else:
-            tt(A("ga"), IND(A("mm_"), A("of2", 36, 39)), A("mask", 0, S), ALU.mult, "ga")
-            scan(A("ra"), A("rs16", 0, S), A("ga"), 0.0, ALU.mult, ALU.add, "ra")
-            copy(A("osu", 0, 3), A("ra", 15, S, 16), tag="osu")
+        tt(A("av"), xv, alive, ALU.mult, "av")
+        scan(A("ra"), A("pick"), A("mm_", RC, RC + S), 0.0, ALU.max, ALU.min, "ra")
         OS = A("osu", 0, 3)
+        copy(OS, A("ra", 15, S, 16), "va", "osu")
+        copy(A("payh", S * t, S * t + S), IND(A("hw"), OS), "va", "payh")
         copy(A("pay", P0, P0 + S), IND(A("wv", 0, WN), OS), "va", "payw")
-        copy(A("payh", S * t, S * t + S), IND(A("hw"), OS), "v", "payh")
-        add({"g": (1200.0, ("payh", t))}, [A("payh", S * t, S * t + S)], [], "sh%d" % t, remote=True)
-        add({"g": (1200.0, ("pay", t))}, [A("pay", P0, P0 + PAYN)], [], "sp%d" % t, remote=True)
-        if OPT["rbv"]:
-            tt(A("gb"), IND(A("mm_"), A("of2", 16, 35)), A("mask"), ALU.mult, "gb")
-            scan(A("rb"), A("rs16"), A("gb"), 0.0, ALU.mult, ALU.add, "rb")
-            rb = lambda n: A("rb", 15, 16 * n, 16)
-        else:
-            copy(A("gb"), IND(A("mm_"), A("of2", 16, 35)), "va", "gb")
-            mm([(A("ps3", 340, 359), O(b), A("gb", b, S + C, 16)) for b in range(16)], "rb")
-            rb = lambda n: A("ps3", 340, 340 + n)
-        ts(A("oh", 0, 19), rb(19), 1.0 / 16, None, ALU.mult, tag="oh")
-        tt(A("owf"), rb(16), A("av"), ALU.add, "owf")
-        ts(A("owu"), A("owf"), 1.0 / 16, None, ALU.mult, tag="owu")
-        copy(A("wc", 0, C), IND(A("wv", 0, 2 * WN + C), A("owu")), "va", "wc")
+        send("sh", t, [A("payh", S * t, S * t + S)])
+        send("sp", t, [A("pay", P0, P0 + PAYN)])
+        copy(A("gb"), IND(A("mm_"), A("of2", 16, 35)), "va", "gb")
+        mm([(A("ps6", 224, 243), O(b), A("gb", b, S + C, 16)) for b in range(16)], "rb")
+        lin(A("oh", 0, 19), A("ps6", 224, 243), 1.0 / 16, 0.0, "oh")
+        tt(A("owf"), A("ps6", 224, 240), A("av"), ALU.add, "owf")
+        lin(A("owu"), A("owf"), 1.0 / 16, 0.0, "owu")
         if last:
             copy(A("h32", 0, C), IND(A("hw"), A("oh", 0, 16)), "va", "h32")
         else:
-            for j, (c0, c1) in enumerate(HEADS):
-                early[0] = 1.0 - c1 / C
-                bank, w = "ps%d" % (4 + j), c1 - c0
-                copy(A("h16", c0, c1), IND(A("hw"), A("oh", c0 // 16, c1 // 16)), tag="h16")
-                head(t + 1, c0, c1, A(bank, 500, 500 + w // 16), [A(bank, w * p, w * p + w) for p in range(t + 2)], A("ps1", C + c0, C + c1),
-                     [A("eq", C * p + c0, C * p + c1) for p in range(t + 2)], "")
+            for c0, c1 in FIRST:
+                src = IND(A("pw"), A("oh", c0 // 16, c1 // 16))
+                ts(A("nk", c0, c1), src, MID + 1, 0.0, ALU.add, ALU.max, "nkg", (AF.Relu, MID + 1, 1.0))
+                lin(A("oq", c0, c1), A("nk", c0, c1), 1.0, 15.0, "oq")
+            copy(A("h16"), IND(A("hw"), A("oh", 0, 16)), "va", "h16")
+        copy(A("wc", 0, C), IND(A("wv", 0, 2 * WN + C), A("owu")), "va", "wc")
     L0 = (NT - 1) * PAYW
-    add({}, [], [A("land", L0, L0 + PAYW)], "arr", done=("arr%d" % (NT - 1), None), lat=HOP2, after="sp%d" % (NT - 1))
-    copy(IND(A("wc"), HL), A("land", L0, L0 + S), tag="scw")
-    add({}, [], [A("landh", S * (NT - 1), S * NT)], "arh", done=("arh%d" % (NT - 1), None), lat=HOP2 - 500, after="sh%d" % (NT - 1))
+    arrive("arh%d" % (NT - 1), [A("landh", S * (NT - 1), S * NT)], par["hop"], "sh%d" % (NT - 1))
+    arrive("arr%d" % (NT - 1), [A("land", L0, L0 + PAYW)], par["hop"], "sp%d" % (NT - 1))
     copy(IND(A("h32"), HL), A("landh", S * (NT - 1), S * NT), tag="sch")
-    store("yw", "wc", "s", "outw")
+    copy(IND(A("wc"), HL), A("land", L0, L0 + S), tag="scw")
     store("yh", "h32", "a", "outh")
+    store("yw", "wc", "s", "outw")
     return ops
 
 
@@ -525,46 +487,52 @@ def needs(ops):
         for kind, refs in (("r", o["rd"]), ("w", o["wr"])):
             for r in refs:
                 byname.setdefault(r[0], []).append((i, kind, r))
-        if "after" in o:
-            hard.add(tags[o["after"]])
         o["banks"] = sorted(set(r[0] for r in o["rd"] + o["wr"] if r[0] not in _SB))
         far = set()
         for j in hard:
-            far |= ops[j]["hard"]
-        o["hard"] = hard
+            far |= ops[j]["all"]
+        o["all"] = far | hard
         o["near"] = sorted(hard - far)
+        o["behind"] = tags[o["after"]] if "after" in o else None
 
 
-def place(ops, prio, eng):
-    n = len(ops)
-    left = [len(o["near"]) for o in ops]
+def place(ops, prio, par, eng=None):
+    n, lat = len(ops), par["lat"]
+    pre = [o["near"] + ([o["behind"]] if o["behind"] is not None else []) for o in ops]
+    left = [len(p) for p in pre]
     users = [[] for _ in ops]
-    for i, o in enumerate(ops):
-        for j in o["near"]:
+    for i, p in enumerate(pre):
+        for j in p:
             users[j].append(i)
     ready = [i for i in range(n) if left[i] == 0]
     busy = {e: [] for e in "vapgs"}
     bank = {"ps%d" % b: [] for b in range(8)}
-    start, end = [0.0] * n, [0.0] * n
+    start, free, end, got = [0.0] * n, [0.0] * n, [0.0] * n, [None] * n
     while ready:
         i = max(ready, key=lambda k: (prio[k], -k))
         ready.remove(i)
-        o, e = ops[i], eng[i]
-        t0 = 0.0
-        for j in o["near"]:
-            t0 = max(t0, end[j] + (0.0 if eng[j] == e == "p" or e is None else LAT))
-        if e is None:
-            start[i], end[i] = t0, t0 + o["lat"]
-        else:
-            c = o["alts"][e][0]
-            taken = [x for x in busy[e] if x[1] > t0]
-            for b in o["banks"]:
-                taken += [(s - LAT, f + LAT) for s, f, e2 in bank[b] if e2 != e and f + LAT > t0]
-            for s, f in sorted(taken):
-                if s >= t0 + c:
-                    break
-                t0 = max(t0, f)
-            start[i], end[i] = t0, t0 + c + o.get("lat", 0.0)
+        o = ops[i]
+        best = None
+        for e in ([eng[i]] if eng else [WHO[o["tag"]]] if o["tag"] in WHO else list(o["alts"]) or [None]):
+            t0 = free[o["behind"]] if o["behind"] is not None else 0.0
+            for j in o["near"]:
+                t0 = max(t0, end[j] + (0.0 if got[j] == e == "p" else lat))
+            c = 0.0
+            if e is not None:
+                c = o["alts"][e][0]
+                taken = [x for x in busy[e] if x[1] > t0]
+                for b in o["banks"]:
+                    taken += [(s - lat, f + lat) for s, f, e2 in bank[b] if e2 != e and f + lat > t0]
+                for s, f in sorted(taken):
+                    if s >= t0 + c:
+                        break
+                    t0 = max(t0, f)
+            key = t0 + c + (par.get("vb", 0.0) * c if e == "v" else 0.0)
+            if best is None or key < best[0]:
+                best = (key, e, t0, c)
+        _, e, t0, c = best
+        got[i], start[i], free[i], end[i] = e, t0, t0 + c, t0 + c + o.get("lat", 0.0)
+        if e is not None:
             busy[e].append((t0, t0 + c))
             for b in o["banks"]:
                 bank[b].append((t0, t0 + c, e))
@@ -572,7 +540,7 @@ def place(ops, prio, eng):
             left[k] -= 1
             if left[k] == 0:
                 ready.append(k)
-    return sorted(range(n), key=lambda k: (start[k], k))
+    return sorted(range(n), key=lambda k: (start[k], k)), got
 
 
 def links(ops, order, eng):
@@ -589,15 +557,17 @@ def links(ops, order, eng):
     return before, soft
 
 
-def replay(ops, order, eng, lat=LAT):
+def replay(ops, order, eng, par):
     before, soft = links(ops, order, eng)
-    n = len(ops)
+    n, lat = len(ops), par["lat"]
     start, free, end = [0.0] * n, [0.0] * n, [0.0] * n
     for i in order:
         o, e = ops[i], eng[i]
         t0 = free[before[i]] if before[i] is not None else 0.0
+        if o["behind"] is not None:
+            t0 = max(t0, free[o["behind"]])
         for j in o["near"]:
-            t0 = max(t0, end[j] + (0.0 if eng[j] == e == "p" or e is None else lat))
+            t0 = max(t0, end[j] + (0.0 if eng[j] == e == "p" else lat))
         for j in soft[i]:
             t0 = max(t0, end[j] + lat)
         start[i] = t0
@@ -606,7 +576,7 @@ def replay(ops, order, eng, lat=LAT):
     return start, free, end
 
 
-def tails(ops, order, eng, queues):
+def tails(ops, order, eng, queues, par):
     before, soft = links(ops, order, eng)
     tail = [0.0] * len(ops)
     for i in reversed(order):
@@ -614,56 +584,32 @@ def tails(ops, order, eng, queues):
         c = o["alts"][e][0] if e is not None else 0.0
         tail[i] += c + o.get("lat", 0.0)
         for j in o["near"]:
-            tail[j] = max(tail[j], tail[i] + LAT)
-        if queues and before[i] is not None:
-            tail[before[i]] = max(tail[before[i]], tail[i] - ops[before[i]].get("lat", 0.0))
+            tail[j] = max(tail[j], tail[i] + par["lat"])
+        for j in [o["behind"]] + ([before[i]] if queues else []):
+            if j is not None:
+                tail[j] = max(tail[j], tail[i] - ops[j].get("lat", 0.0))
     return tail
 
 
-def choose(ops):
-    eng, seen = [], {}
-    for o in ops:
-        a = list(o["alts"])
-        if len(a) < 2:
-            eng.append(a[0] if a else None)
-            continue
-        k = seen.get(o["tag"], 0)
-        seen[o["tag"]] = k + 1
-        pick = WHO.get(o["tag"], "a")
-        eng.append(pick[k % len(pick)])
-    return eng
+def choose(ops, who):
+    return [("v" if o["name"] in who else "a") if len(o["alts"]) > 1 else (list(o["alts"]) or [None])[0] for o in ops]
 
 
-def plan(ops, seed=SEED, rounds=ROUNDS, noise=NOISE):
-    needs(ops)
-    eng = choose(ops)
-    x = [seed]
-
-    def rnd():
-        x[0] = (x[0] * 1103515245 + 12345) % 2147483648
-        return x[0] / 2147483648.0
-    base = tails(ops, list(range(len(ops))), eng, False)
-    prio = [p + noise * rnd() + OPT["early"] * o["early"] for p, o in zip(base, ops)]
-    best = None
-    for _ in range(rounds):
-        order = place(ops, prio, eng)
-        span = max(replay(ops, order, eng)[2])
-        if best is None or span < best[0]:
-            best = (span, order)
-        t = tails(ops, order, eng, True)
-        w = rnd()
-        prio = [w * a + (1 - w) * b + noise * rnd() for a, b in zip(t, prio)]
-    return best[1], eng
+def heads(ops, eng, par):
+    end, start = [0.0] * len(ops), [0.0] * len(ops)
+    for i, o in enumerate(ops):
+        start[i] = max([end[j] + par["lat"] for j in o["near"]] + [0.0 if o["behind"] is None else start[o["behind"]]])
+        end[i] = start[i] + (o["alts"][eng[i]][0] if eng[i] else 0.0) + o.get("lat", 0.0)
+    return start
 
 
-def unpack(ops, text):
-    ab = "0123456789abcdefghijklmnopqrstuvwxyzABCDEFGHIJKLMNOPQRSTUVWXYZ"
-    order, eng = [], [None] * len(ops)
-    for i in range(0, len(text), 2):
-        second, k = divmod(62 * ab.index(text[i]) + ab.index(text[i + 1]), 1860)
-        order.append(k)
-        eng[k] = (list(ops[k]["alts"]) or [None])[second]
-    return order, eng
+def plan(par=PAR, who=WHO, ahead=AHEAD, ops=None, mix=MIX):
+    if ops is None:
+        ops = build(None, 1, par)
+        needs(ops)
+    eng = choose(ops, who)
+    late, early = tails(ops, list(range(len(ops))), eng, False, par), heads(ops, eng, par)
+    return place(ops, [(1 - mix) * a - mix * b + ahead.get(o["name"], 0.0) for a, b, o in zip(late, early, ops)], par, eng)
 
 
 PLAN = {}
@@ -685,6 +631,20 @@ def ways(T, topo, core):
     return nxt, relay, direct, share
 
 
+def slots(kind, t, r):
+    if kind == "sh":
+        return "payh", "landh", t * S, t * S, S, "arh%d" % t
+    if kind == "sp":
+        return "pay", "land", t * PAYW, t * PAYW, PAYN, "arr%d" % t
+    return "dcol", "cnt", 8 * t, N * t + r, 1, "cnt%d" % t
+
+
+def messages(T, r, what):
+    a, b, c0, d0, w, sem = slots(what[0], what[1], r)
+    to = [d for d in range(N) if d != r] if what[0] == "sc" else [(r + 1) % N]
+    return [(d, T[a][:, c0:c0 + w], lambda U: U[b][:, d0:d0 + w], sem) for d in to]
+
+
 def bits(engines):
     return sum(1 << e for e in engines)
 
@@ -694,36 +654,40 @@ def dst(topo, d, s):
     return DstId(rid=rid, pnc=pid)
 
 
+def lanes(T, topo, owner):
+    nxt, relay, direct, share = ways(T, topo, owner)
+    off = topo.engines(owner, direct[0])
+    on = [e for e in topo.engines(owner, relay[0]) if e not in off]
+    return {"sh": off, "sp": on, "sc": on}
+
+
+def write(g, T, topo, core, to, src, piece, sem, engines):
+    if len(to) == 1:
+        rid, pid = topo.addr(to[0], core)
+        g.remote_dma(piece, src, sem, T.sem.loc, pid, rid, bits(engines))
+    else:
+        g.remote_dma_fused([RemoteDMATransfer(dst_ids=[dst(topo, d, core) for d in to], dma_engine_mask=bits(engines), remote_sem=sem,
+                                              src=src, dsts=[piece] * len(to))], local_sem=T.sem.loc)
+    return len(engines)
+
+
 def hand_on(g, core, T, topo):
     for owner in T.cores:
         if core not in topo.cores_of(owner):
             continue
-        r = T.rank_of(owner)
         nxt, relay, direct, share = ways(T, topo, owner)
-        sent = 0
         if core in relay:
-            rid, pid = topo.addr(nxt, core)
-            off = topo.engines(owner, direct[0])
-            n_in = len(off) if core == relay[0] else len([e for e in topo.engines(owner, core) if e not in off])
-            n_out = len(topo.engines(core, nxt))
-            for t in range(NT):
-                piece = T.landh[:, t * S:t * S + S] if core == relay[0] else T.land[:, t * PAYW:t * PAYW + PAYN]
-                sem = T.sem[("arh%d" if core == relay[0] else "arr%d") % t]
-                g.wait_ge(sem, n_in)
-                g.remote_dma(piece, piece, sem, T.sem.loc, pid, rid, topo.mask(core, nxt))
-                sent += n_out
+            kind, to, steps = ["sh", "sp"][relay.index(core)], [nxt], NT
         elif core in share:
-            off = topo.engines(owner, direct[0])
-            n_in = len([e for e in topo.engines(owner, core) if e not in off])
-            to = share[core]
-            for t in range(NT - 1):
-                piece = T.cnt[:, N * t + r:N * t + r + 1]
-                g.wait_ge(T.sem["cnt%d" % t], n_in)
-                g.remote_dma_fused([RemoteDMATransfer(dst_ids=[dst(topo, d, core) for d in to], dma_engine_mask=topo.mask(core, to[0]),
-                                                      remote_sem=T.sem["cnt%d" % t], src=piece, dsts=[piece] * len(to))], local_sem=T.sem.loc)
-                sent += len(topo.engines(core, to[0]))
-        if sent:
-            g.wait_ge(T.sem.loc, sent)
+            kind, to, steps = "sc", share[core], NT - 1
+        else:
+            return
+        sent = 0
+        for t in range(steps):
+            _, b, _, d0, w, sem = slots(kind, t, T.rank_of(owner))
+            g.wait_ge(T.sem[sem], len(lanes(T, topo, owner)[kind]))
+            sent += write(g, T, topo, core, to, T[b][:, d0:d0 + w], T[b][:, d0:d0 + w], T.sem[sem], topo.engines(core, to[0]))
+        g.wait_ge(T.sem.loc, sent)
 
 
 def rank_program(g, core, T, topo):
@@ -732,24 +696,19 @@ def rank_program(g, core, T, topo):
         hand_on(g, core, T, topo)
         return
     nxt, relay, direct, share = ways(T, topo, core)
-    off = topo.engines(core, direct[0])
-    helpers = list(share)
-    on = [e for e in topo.engines(core, helpers[0]) if e not in off]
-    prev = T.cores[(rank - 1) % N]
-    n_arr = len(topo.engines(ways(T, topo, prev)[1][0], core))
+    first = {"sh": [relay[0]], "sp": [relay[1]], "sc": list(share)}
+    mine = lanes(T, topo, core)
+    n_arr = len(topo.engines(ways(T, topo, T.cores[(rank - 1) % N])[1][0], core))
     n_cnt = 0
     for o in T.cores:
         if o != core:
-            w = ways(T, topo, o)
-            n_cnt += sum(len(topo.engines(h, to[0])) for h, to in w[3].items() if core in to)
-    ops = build(T, rank)
+            n_cnt += sum(len(topo.engines(h, to[0])) for h, to in ways(T, topo, o)[3].items() if core in to)
     if not PLAN:
-        PLAN["it"] = unpack(ops, ORDER) if ORDER else plan(build(T, 1))
+        PLAN["it"] = plan()
     order, eng = PLAN["it"]
+    ops = build(T, rank)
     needs(ops)
     soft = links(ops, order, eng)[1]
-    for i, o in enumerate(ops):
-        o["eng"], o["soft"] = eng[i], soft[i]
     Q = {"v": g.vector, "a": g.scalar, "p": g.tensor, "g": g, "s": g.sync}
     count = {e: 0 for e in ESEM}
     for i in order:
@@ -760,43 +719,30 @@ def rank_program(g, core, T, topo):
         elif "remote" in o:
             o["sig"] = None
         else:
-            count[o["eng"]] += 1
-            o["sig"] = (ESEM[o["eng"]], count[o["eng"]])
+            count[eng[i]] += 1
+            o["sig"] = (ESEM[eng[i]], count[eng[i]])
     seen = {e: {} for e in Q}
     sent = 0
     for i in order:
-        o = ops[i]
-        e = o["eng"]
+        o, e = ops[i], eng[i]
         if e is None:
+            o["knew"] = {}
             continue
-        need = {}
-        for j in o["near"] + o["soft"]:
-            if ops[j]["eng"] == e == "p" or ops[j]["sig"] is None:
+        for j in sorted(o["near"] + soft[i], reverse=True):
+            if eng[j] == e == "p" or ops[j]["sig"] is None:
                 continue
             s, v = ops[j]["sig"]
-            need[s] = max(need.get(s, 0), v)
-        for s in sorted(need):
-            if seen[e].get(s, 0) < need[s]:
-                Q[e].wait_ge(T.sem[s], need[s])
-                seen[e][s] = need[s]
+            if seen[e].get(s, 0) < v:
+                o.setdefault("waits", {})[s] = max(o.get("waits", {}).get(s, 0), v)
+                for s2, v2 in list(ops[j]["knew"].items()) + [(s, v)]:
+                    seen[e][s2] = max(seen[e].get(s2, 0), v2)
+        for s, v in sorted(o.get("waits", {}).items()):
+            Q[e].wait_ge(T.sem[s], v)
+        o["knew"] = dict(seen[e])
         f = o["alts"][e][1]
         if "remote" in o:
-            kind, t = f
-            if kind == "pay":
-                rid, pid = topo.addr(relay[1], core)
-                g.remote_dma(T.land[:, t * PAYW:t * PAYW + PAYN], T.pay[:, t * PAYW:t * PAYW + PAYN], T.sem["arr%d" % t], T.sem.loc,
-                             pid, rid, bits(on))
-                sent += len(on)
-            elif kind == "payh":
-                rid, pid = topo.addr(relay[0], core)
-                g.remote_dma(T.landh[:, t * S:t * S + S], T.payh[:, t * S:t * S + S], T.sem["arh%d" % t], T.sem.loc, pid, rid, bits(off))
-                sent += len(off)
-            else:
-                src, to = T.dcol[:, 8 * t:8 * t + 1], T.cnt[:, N * t + rank:N * t + rank + 1]
-                g.remote_dma_fused([
-                    RemoteDMATransfer(dst_ids=[dst(topo, d, core) for d in helpers], dma_engine_mask=bits(on), remote_sem=T.sem["cnt%d" % t],
-                                      src=src, dsts=[to] * len(helpers))], local_sem=T.sem.loc)
-                sent += len(on)
+            a, b, c0, d0, w, sem = slots(f[0], f[1], rank)
+            sent += write(g, T, topo, core, first[f[0]], T[a][:, c0:c0 + w], T[b][:, d0:d0 + w], T.sem[sem], mine[f[0]])
         elif "done" in o:
             f(Q[e])
         else:

@@ -6,11 +6,13 @@ AF = ActivationFunctionType
 N, V, C, NT, S, DG = 8, 2048, 256, 5, 48, 5
 NONE = C
 WN = C + 2 * S + 16
-PAYN, PAYW = S + 1, S + 4
+PAYN, PAYW, PAYP = S + 1, S + 4, S + 112
+CUT = 256
 MID = 1023.0
 BASE = 786432.0
 TWO23 = 8388608.0
-RH, RC, RD, RI, MW = 0, 593, 864, 1120, 1376
+ID0 = 32
+RH, RC, RD, RI, MW = 0, 593, 864, 1120, 1888
 
 CHUNKS = [(0, 64), (64, 128), (128, 192), (192, 256)]
 FIRST = [(0, 128), (128, 256)]
@@ -24,18 +26,18 @@ _SB = {
     "ones": (640, BF), "ident": (128, BF), "bo": (128, BF), "bo1": (128, BF), "nbo": (128, BF), "boh": (128, BF), "l2a": (128, BF), "l2": (128, BF),
     "dma_": (128, BF), "dmb": (128, BF), "dm": (128, BF), "c15": (128, BF), "jj": (256, BF), "z8": (144, BF), "bo8a": (128, BF), "bo8": (128, BF),
     "zt": (640, BF), "zz": (144, BF), "zzh": (144, BF), "i11": (128, BF), "i2k": (128, BF), "ip": (128, BF), "im": (128, BF), "sel": (640, BF),
-    "mki": (S, I32), "mki2": (S, I32), "pick": (S, BF), "ids": (C, BF), "pci": (8, I32),
-    "pci2": (8, I32), "cc": (144, F16), "cw": (16, F32), "zr": (576, BF), "rs32": (84, BF), "rsx": (128, F32),
+    "mki": (C, I32), "mki2": (C, I32), "pik1": (C, BF), "pick": (C, BF), "ramp": (C, BF), "kept": (C + 112, F32), "ids": (C, F32), "pci": (8, I32),
+    "pci2": (8, I32), "cc": (112, F16), "cwi": (16, F32), "cw": (16, F32), "rs32": (84, BF), "rsx": (128, F32),
     "th": (NT * 48, F32), "thb": (NT * 16, F32), "cap": (2048, BF),
     "oq": (C + S, U16), "xx": (XW, F16), "ee": (XW, BF), "yy": (C + S, F32),
     "wc": (WN, F32), "wv": (3 * WN, F32), "w1i": (S, F32), "h32": (WN, F32), "h16": (C, F16), "hw": (WN, F32), "pw": (WN, F32),
-    "fl": (3 * C, BF), "fw": (84, BF), "dbl": (16, BF), "sc": (84, BF), "rr": (128, F32), "of2": (40, U16),
-    "mm_": (MW, BF), "gb": (C + S, BF), "ra": (S, BF), "osu": (4, U16), "oh": (20, U16),
-    "owf": (16, F32), "owu": (16, U16), "av": (16, F32), "sg": (C + S, BF), "mv": (C + S, F16),
+    "fl": (3 * C, BF), "fw": (84, BF), "dbl": (16, BF), "sc": (84, BF), "of2": (40, U16),
+    "mm_": (MW, F32), "gb": (C + S, F16), "ra": (S, F16), "osu": (8, U16), "oh": (40, U16),
+    "owu": (40, U16), "sg": (C + S, BF), "mv": (C + S, F16),
     "hwi": (S, F32), "pwi": (S, F32), "swu": (20, U16), "swa": (4, U16), "nk": (C + S, F16), "nn": (C + S, F16),
-    "eq": (5 * C, BF), "eqi": (5 * S, BF), "eqa": (5 * S, BF), "uin": (S, F32),
+    "eq": (5 * C, BF), "eqb": (5 * 112, BF), "eqa": (5 * S, BF), "uin": (S, F32),
     "al0": (C, BF), "col": (32, F32), "dcol": (8 * NT, BF), "tmp0": (C, F32),
-    "pay": (NT * PAYW, F32), "land": (NT * PAYW, F32), "payh": (NT * S, F16), "landh": (NT * S, F16), "cnt": (NT * N, BF),
+    "pay": (NT * PAYP, F32), "land": (NT * PAYW, F32), "payh": (NT * S, F16), "landh": (NT * S, F16), "cnt": (NT * N, BF),
 }
 SCRATCH = {k: ("sbuf", [128, w], d) for k, (w, d) in _SB.items()}
 for _b in range(8):
@@ -45,11 +47,14 @@ SEMAPHORES = (["ev", "ea", "ep", "eg", "loc", "outw", "outh"] + ["ld_" + x for x
               + ["arr%d" % t for t in range(NT)] + ["arh%d" % t for t in range(NT)] + ["cnt%d" % t for t in range(NT - 1)])
 ESEM = {"v": "ev", "a": "ea", "p": "ep", "g": "eg"}
 
-PAR = dict(cy=0.92, pcy=0.48, gr=1.56, scr=3.8, hop=3400.0, hopc=4700.0, fa=90.0, fv=25.0, fp=60.0, call=700.0, lat=130.0,
+PAR = dict(cy=0.88, pcy=0.46, gr=1.56, scr=3.8, hop=3400.0, hopc=4700.0, fa=90.0, fv=25.0, fp=60.0, call=700.0, lat=130.0,
            nb=4500.0, qs=5800.0)
 MIX = 0.5
 WHO = ['boh', 'e', 'gx', 'gx.3', 'gxi', 'i2k', 'nk0.1', 'nka', 'nki', 'of2', 'oq', 'oq.1', 'oq0', 'oqa', 'osu', 'owu', 'payw', 'pw', 'pwi', 'sel.2', 'swa', 'swui', 'th.1', 'th.2', 'th.3', 'th.4', 'thb', 'ub.3', 'ub.5', 'usb', 'wc', 'zr', 'zr.1', 'zr.3', 'zzh']
-AHEAD = {'ps5': 3000, 'w1.3': -700, 'pick': 3000, 'i11': 4700, 'eqa': -500, 'tot': 2600, 'cnb.1': 1300, 'oq': 2200, 'sel': 1500, 'dbl': 2500, 'thr': 3300, 's0h': -700, 'bo8a': 3600, 'hwi': 200, 'th.4': 100, 'ldqs': -1900, 'ra': 200, 'rs32': -1000, 'scw.1': -500, 'dm': -2900, 'w1i': -900, 'dn': -1200, 'ldw0': 300, 'f.1': 4200, 'eq.2': 2800, 'scan.1': -1400, 'zr': -1900, 'gx': 5800, 'nk': 1800, 'mki2': -1400, 'oi': 6000, 'oq0': 3100, 'eqi': 1300, 'w1.1': 2500, 'Vi': 3300, 'y': 1400, 'styw': 4000, 'rb': -2000, 'zt': 2000, 'osu': 1500, 'ps7': -700, 'f.2': -800, 'lh': -700, 'f.3': -1500, 'ge': -700, 'ones': 2300, 'owf': 100, 'th.1': 2300, 'col.2': -1900, 'th.5': 300, 'gx.1': 2300, 'gx.3': 500, 'ps4.1': 1100, 'payw': -3600, 'boh': -500, 'dma_': -700, 'scan': 1300, 'owu': 200, 'cap': -2300, 'sc': 100, 'col.1': 3700, 'up': -700, 'sch.1': -400, 'dni': -2200, 'pci2': 5400, 'ldus': 600, 'payh': -1100, 'mvi': 600, 'qt': -600, 'f': 2000, 'fw': -700, 'sel.3': 500, 'ub.5': 1900, 'refill': -900, 'oh': 1700, 'av': -4900, 'cc.2': -500, 'scan.3': -500, 'refill.1': -3100, 'zr.3': -1700, 'eqa.4': 1000, 'px': 1400, 'V.1': 1700, 'l2a': -200, 'gxi': 4800, 'rr': -500, 'hole': 2500, 'bo': 2300, 'cc': 2700, 'ident': -200, 'nin': 2300, 'ldnb': 1500, 'fi': 3000, 'e': -1800, 'o0.1': 1000, 'hba.1': 5000, 'y.2': 300, 'hba': 1000, 'al': -200, 'bo1': 800, 'i2k': -200, 'zzh': -700, 'ldhi': 500, 'ps3': -200, 'swa': -800, 'eq': 1300, 'hbli': 1200, 'cl': -100, 'nki': 200, 'thr.3': -500, 'V': 1000, 'scan.2': 3000, 'o0': 500, 'th': -600, 'col.6': 3200, 'siwi': -800, 'gxi.1': -1300, 'sco': 3800, 'cnb.3': 500, 'eq.4': -1500, 'ldlo': 500, 'eq.3': 900, 'ub.4': 3000, 'col.3': 3700, 'hbl': 200, 'tmp0': -1500, 'eqa.3': 2000, 'zz': 2300, 'eqi.2': -500, 'z8': -700, 'mm_.1': 800, 'l2': 1000, 'wv': 1000, 'rsx': -1000, 'pwi': -2000, 'V.2': -200, 'cc.3': 1000, 'oq0.1': 2000, 'uin': -500, 'siwa': 200, 'bo8': 800, 'wc.1': 2500, 'ub.3': 1200, 'pw3': 2000, 'hb': -1500, 'sel.2': -300, 'ps5.1': 3000, 'sch': -200, 'nk0': 1400, 'im': -2500, 'ps2': 500, 'scw': 200, 'c15.1': 1000, 'zr.1': 500, 'hnew': -200, 'cw': 200, 'eqi.4': -2500, 'cap.1': 300, 'ps4': -2000, 'rsx.1': 500, 'gb': -200, 'nbo': 200, 'ub': -500, 'xv': -1000, 'y.3': -200, 'ch': 200, 'col': 1200, 'cc.1': 500, 'usb': -1000, 'wc': 2000, 'scat': 200, 'wv.1': -2000, 'hb.3': -1000, 'V.3': 2000, 'db': -1000, 'eqi.1': 200, 'ip': 1000, 'dmb': -500, 'hb.1': 1000, 'mm_': 200, 'siw': -500, 'hba.2': -500}
+PERIOD = 14.0
+WHO = '+boh +col.2 +h16 +i11 +i2k +im +ip +nbo +oq0 +pick +sel.4 +th.5 +ub.1 +ub.3 +zzh 0gb 0gx.1 0gx.3 0gx.5 0gx.7 0oq 0payh 0pw 0scat 0swu gx.1 gx.3 gx.5 gx.7 gxi hw hwb of2 oq osu payh payw pw pwb'.split()
+TURNS = '+pci@-13.176 +cwi@-12.111 +mki@-12.083 +ones@-11.384 +bo1@-9.603 +z8@-9.104 +ident@-9.003 +pci2@-8.345 +th@-8.304 +cc@-8.233 +fw@-8.145 +rs32@-8.122 +zz@-7.893 +bo8a@-7.775 +cap@-7.705 +ldcoin@-7.697 +cap.1@-7.653 +ldus@-7.372 +lds0@-7.271 +rsx@-7.241 +qt@-7.236 +mki2@-6.725 +col.1@-6.715 +cc.6@-6.56 +pw@-6.506 +rsx.1@-6.453 +lh@-6.326 +cw@-6.215 +col@-6.163 +im@-6.075 +col.3@-5.814 +hw@-5.764 +i11@-5.735 +rs32.1@-5.724 +ldnb@-5.717 +tmp0@-5.583 +zz.1@-5.459 +bo@-5.435 +ps1@-5.334 +s0h@-5.3 +i2k@-5.295 +zzh@-5.285 +usb@-5.208 +cc.5@-5.164 +cnb@-5.138 +wv@-4.983 +bo8@-4.982 +cnb.1@-4.931 +ps6@-4.656 +zt@-4.519 +ps3@-4.343 0refill.1@-4.319 +ps7@-4.116 +pik1@-4.002 +cc.4@-3.992 +sel@-3.768 +ps2@-3.682 +ldqs@-3.588 +ramp@-3.479 +swu@-2.328 +mm_@-2.305 +ldw0@-2.282 +al0@-2.24 +nk0.1@-2.23 +nk0@-2.221 +nbo@-1.752 +col.2@-1.742 +boh@-1.706 +th.1@-1.625 +cc.1@-1.189 +h16@-1.179 +thb@-1.123 +ip@-1.112 +dmb@-0.916 +pick@-0.855 +cc.3@-0.735 0refill@-0.712 +col.4@-0.707 +dma_@-0.647 +dm@-0.533 +cc.2@-0.512 +eq0.1@-0.255 +eq0@-0.225 +mm_.1@-0.205 +ub.1@-0.135 +oq0@-0.11 +wc.1@0.09 0gx@0.216 +l2a@0.239 +o0@0.273 refill@0.705 +ldlo@0.805 +c15@0.986 +ps4.1@1.027 0gx.1@1.028 +l2@1.06 +o0.1@1.127 0y@1.13 gx.3@1.182 0y.1@1.236 0gx.5@1.246 0gx.3@1.256 +oq0.1@1.267 gx.1@1.308 0w1.1@1.357 gx.7@1.372 hb.1@1.377 0f@1.492 0gx.2@1.524 0gx.7@1.557 0f.1@1.816 y@1.892 0thr@1.939 +col.7@1.949 0gx.4@2.076 hb.2@2.143 hb@2.17 +ids@2.428 hb.3@2.466 gx@2.536 gx.2@2.573 f@2.587 0V@2.764 0gx.6@2.823 f.1@2.826 scan@2.851 0y.2@2.874 0f.2@2.874 +ps5@2.881 0w1@2.884 +th.2@2.942 hba@2.965 siba@2.975 gx.4@3.087 0f.3@3.099 hba.3@3.139 hba.4@3.199 gx.6@3.237 0dn@3.248 gx.5@3.289 hba.2@3.339 hba.1@3.349 swua@3.416 0w1.2@3.421 0scan@3.429 y.1@3.431 thr.1@3.431 thr@3.441 sipa@3.441 tot@3.45 0al@3.535 f.2@3.553 eqa.3@3.847 nka@3.852 up@3.857 0w1.3@3.881 0y.3@3.891 eqa.1@3.907 +jj@3.952 uin@4.049 0fw@4.087 0thr.2@4.194 endh@4.219 refill.1@4.427 eqa.2@4.484 eqa.4@4.494 +ldhi@4.496 0ch@4.516 0scan.1@4.516 0thr.1@4.526 0cl@4.536 +sel.3@4.573 oa@4.671 f.3@4.681 eqa@4.684 0scan.2@4.687 w1@4.816 lh@4.84 0pw3@4.928 0dbl@5.02 oqa@5.139 y.2@5.245 scan.1@5.255 w1.3@5.255 dn@5.265 gxi@5.322 V@5.421 0hole@5.432 w1.2@5.445 thr.2@5.455 +sel.1@5.492 endw@5.55 0V.1@5.643 +ps5.1@5.653 0px@5.659 0thr.3@5.695 y.3@5.746 gxi.1@5.927 w1.1@5.946 w1i@5.946 scan.2@5.956 0sc@6.016 +sel.2@6.079 +th.3@6.159 0rr@6.294 fi@6.298 0scan.3@6.304 yi@6.308 0px0@6.421 dnb@6.442 scan.3@6.463 thr.3@6.47 scw@6.473 cl@6.48 ch@6.503 +th.4@6.534 V.1@6.549 al@6.617 +h32@6.636 V.2@6.708 scani@6.75 twice@6.755 0twice@6.834 0V.2@6.864 0scat@6.951 0of2@7.061 0rrb@7.071 styw@7.075 0mv@7.105 half@7.138 V.3@7.178 Vi@7.226 0V.3@7.243 0pxb@7.285 0osw@7.312 pw3@7.426 0half@7.488 0ge@7.498 sib@7.567 styh@7.709 0of2b@7.769 +ub.5@7.779 ge@7.869 thri@8.127 mv@8.393 px0@8.403 0ra@8.407 0d@8.605 0gb@8.606 +ub.2@8.648 rrb@8.848 fw@8.862 px@8.939 db@9.055 dbl@9.274 mvb@9.29 hole@9.309 +ps4@9.384 sc@9.401 nk@9.423 sip@9.44 0osu@9.47 geb@9.522 sipb@9.533 0sib@9.569 swu@9.584 rr@9.592 scat@9.594 0hw@9.624 0sip@9.627 0hnew@9.671 0hb@9.712 +col.5@9.726 0swu@9.806 of2@9.896 0>sc@9.924 d@9.948 hnew@10.061 hw@10.084 0rb@10.154 sibb@10.234 0hbl@10.492 pxb@10.526 eq@10.548 eq.1@10.576 0o.1@10.598 +c15.1@10.731 of2b@10.752 hnewb@10.817 +ub.3@10.829 0>sh@10.836 0payh@10.908 hblb@10.928 0o@10.969 0nk@11.014 hbl@11.09 swub@11.111 o@11.156 eq.2@11.166 sch@11.2 osu@11.215 o.2@11.311 ob@11.311 o.1@11.381 hwb@11.395 eq.3@11.398 ra@11.4 >sc@11.672 gb@11.721 +ub@11.809 rb@11.911 eq.4@12.051 0eq@12.192 eqb@12.33 payh@12.34 nkb@12.566 eqb.2@12.576 eqb.3@12.576 0eq.1@12.698 osw@12.79 eqb.1@12.957 owu@13.006 eqb.4@13.04 0owu@13.718 pw@13.779 h32@13.873 pwb@13.877 0oq@13.908 oh@13.95 >sh@14.052 +ub.4@14.11 0wc@14.199 0oh@14.355 0o.2@14.475 +sel.4@14.636 sco@14.731 >sp@14.739 +th.5@14.78 payw@14.88 oq@15.362 wc@15.402 +wc@15.619 h16@15.849 oq.1@15.882 0payw@15.984 0h16@16.006 +col.6@16.007 0oq.1@16.061 0pw@16.232 0nkg@17.376 nkg@19.029 0>sp@19.9'
+WHEN = {x.split("@")[0]: float(x.split("@")[1]) for x in TURNS.split()}
 
 
 def A(name, c0=0, c1=None, st=1, p0=0, p1=128):
@@ -79,7 +84,7 @@ def parts(r):
 
 def build(T, rank, par=PAR):
     CY, PCY, GR, SCR = par["cy"], par["pcy"], par["gr"], par["scr"]
-    ops, nth = [], {}
+    ops, nth, step = [], {}, [-1]
 
     def ap(r):
         if not isinstance(r, tuple):
@@ -100,7 +105,7 @@ def build(T, rank, par=PAR):
                 wr.append(r)
         tag = tag or wr[0][0]
         k = nth[tag] = nth.get(tag, -1) + 1
-        o = dict(alts=alts, rd=rd, wr=wr, tag=tag, name=tag + ("." + str(k) if k else ""), eng=None)
+        o = dict(alts=alts, rd=rd, wr=wr, tag=tag, name={-1: "+", 0: "0"}.get(step[0], "") + tag + ("." + str(k) if k else ""), step=step[0], eng=None)
         o.update(kw)
         ops.append(o)
         return o
@@ -117,6 +122,8 @@ def build(T, rank, par=PAR):
         return par["fv"] + max(64, n * rate) * CY
 
     def acost(out, in_):
+        if out[0] == "#":
+            return 65 + nel(out) * SCR * CY
         return 65 + nel(out) * GR * CY if in_[0] == "#" else par["fa"] + nel(out) * CY
 
     def copy(out, in_, eng="v", tag=""):
@@ -124,9 +131,7 @@ def build(T, rank, par=PAR):
         if "v" in eng:
             alts["v"] = (vcost(out, [in_]), lambda q: q.tensor_copy(ap(out), ap(in_)))
         if "a" in eng:
-            alts["a"] = (acost(out, in_), lambda q: q.activation(ap(out), ap(in_), AF.Identity))
-        if "g" in eng:
-            alts["g"] = (170 + 2 * CY * nel(out), lambda q: q.affine_select(ap(out), ap(in_), [[0, nel(out)]], ALU.is_ge, 0.0, 0, 0))
+            alts["a"] = (acost(out, in_), lambda q: q.activation(ap(out), ap(in_), AF.Silu if out[0] == "#" else AF.Identity))
         return add(alts, [in_], [out], tag)
 
     def ts(out, in0, s1, s2, op0, op1=None, tag="", act=None):
@@ -178,7 +183,7 @@ def build(T, rank, par=PAR):
         return add({"g": (170 + 2 * CY * nel(out), lambda q: q.affine_select(ap(out), ap(in_), pat, cmp_, fill, base, cm))}, [in_], [out], tag)
 
     def send(kind, t, reads):
-        return add({"g": (par["call"], (kind, t))}, reads, [], "%s%d" % (kind, t), remote=True)
+        return add({"g": (par["call"], (kind, t))}, reads, [], "%s%d" % (kind, t), remote=True, name=(">" if t else "0>") + kind)
 
     def arrive(sem, writes, lat, after):
         return add({}, [], writes, sem, done=(sem, None), lat=lat, after=after)
@@ -238,50 +243,52 @@ def build(T, rank, par=PAR):
     sel(A("dm"), A("dmb"), [[-16, 8], [-128, 16]], ALU.not_equal, 1.0, 15 * 128, 1)
     sel(A("l2a"), A("nbo"), [[-1, 128]], ALU.is_gt, 0.0, 0, 1)
     sel(A("l2"), A("l2a"), [[-1, 128]], ALU.not_equal, -2048.0, 0, 1)
-    iota(A("mki"), [[0, S // 16], [-1, 16]], 16, 1)
-    iota(A("ids"), [[1, C]], 0, 0)
+    iota(A("mki"), [[0, 16], [-1, 16]], 16, 1)
+    iota(A("ids"), [[3, C]], ID0, 0)
+    iota(A("mm_", RI, MW), [[1, 3], [3, C]], ID0, 0)
     iota(A("pci"), [[0, 8]], 0, 1)
     sel(A("jj"), A("ones", 0, 256), [[0, 2], [-1, 128]], ALU.is_equal, 0.0, 0, 1)
     lin(A("i11"), A("ident"), 2.0 ** -11, 0.0)
     lin(A("i2k"), A("ident"), -4096.0, 0.0)
-    lin(A("ip"), A("ident"), 16.0 * WN, 0.0)
-    lin(A("im"), A("ident"), -16.0 * WN, 0.0)
+    lin(A("ip"), A("ident"), float(C), 0.0)
+    lin(A("im"), A("ident"), -float(C), 0.0)
     memset(A("zz"), 0.0)
     copy(A("zz", 15, 143, 16), A("bo", 0, 128, 16))
     lin(A("zzh"), A("zz"), 0.5, 0.0)
     memset(A("c15"), 0.0); memset(A("c15", 15, 128, 16), -16.0)
     ts(A("mki2"), A("mki"), 15, None, ALU.bitwise_and)
-    ts(A("pick"), A("mki2"), 0.0, 4096.0, ALU.is_equal, ALU.mult)
+    ts(A("pik1"), A("mki2"), 0.0, -0.5, ALU.is_equal, ALU.add)
+    lin(A("pick"), A("pik1"), 2.0 ** 18, 0.0)
     ts(A("col", 24, 29), A("mki2", 0, 5), 0.0, None, ALU.is_equal)
     for p in range(5):
         lin(SEL(p), A("bo"), A("col", 24 + p, 25 + p), 0.0)
-    for t in range(1, NT):
-        lin(A("zr", 144 * (t - 1), 144 * t), A("zz"), A("col", 24 + t, 25 + t), 0.0)
     ts(A("pci2"), A("pci"), 15, None, ALU.bitwise_and)
     copy(A("col", 0, 1), A("pci2", 0, 1))
+    lin(A("col", 6, 7), A("col", 0, 1), -4096.0, MID)
+    iota(A("ramp"), [[0, 16], [4096, 16]], 0, 0)
     ts(A("col", 1, 2), A("col", 0, 1), 15.0, -(16 * BASE + 8.5 * 4096 + 1), ALU.is_lt, ALU.mult)
     ts(A("col", 2, 3), A("col", 1, 2), 1.0, None, ALU.add)
     ts(A("col", 3, 4), A("col", 0, 1), NT + 0.5, MID + 1, ALU.is_lt, ALU.mult)
     ts(A("col", 5, 6), A("col", 3, 4), -1.0, None, ALU.add)
-    ts(A("cw"), A("ids", 0, C, 16), A("col", 0, 1), None, ALU.add)
+    iota(A("cwi"), [[16, 16]], 0, 0)
+    ts(A("cw"), A("cwi"), A("col", 0, 1), None, ALU.add)
     memset(A("cc"), 2047.0 + RC)
     memset(A("cc", 0, 48, 3), 2047.0)
     ts(A("cc", 2, 48, 3), A("cw"), float(RD), None, ALU.add)
-    ts(A("cc", 50, 96, 3), A("cw"), float(RI), None, ALU.add)
+    ts(A("cc", 50, 96, 3), A("cw"), float(RI + C), None, ALU.add)
     copy(A("cc", 98, 108, 3), A("cw", 0, 4))
-    memset(A("cc", 108, 112), 0.0)
-    memset(A("cc", 128, 144), 16.0 * WN)
+    memset(A("cc", 108, 109), 0.0); memset(A("cc", 109, 112), float(S))
     memset(A("rs32"), 1.0); memset(A("rs32", 0, 84, 64), 0.0)
     memset(A("fw"), 0.0)
     memset(A("rsx"), 0.0); memset(A("rsx", 0, 109, 3), 4096.0)
     ncap = 16 * max([c1 - c0 for c0, c1 in CHUNKS] + [S])
     memset(A("cap", 0, ncap), 2.0 ** 20); memset(A("cap", 0, ncap, 16), BASE)
     memset(A("ub", NT * C, NT * C + WN - C), 0.0)
-    memset(A("wv", C, WN), 0.0); memset(A("wv", WN + C, 2 * WN), 0.0)
+    memset(A("wv", 3 * C, 3 * WN), 0.0)
     memset(A("hw", C, WN), -1.0); memset(A("pw", C, WN), -4096.0)
     memset(A("wc", C, WN), 0.0); memset(A("h32", C, WN), 0.0)
     memset(A("th"), 9.0)
-    memset(A("mm_", RC + S, RI), 0.0); copy(A("mm_", RI, MW), A("ids"), "va")
+    iota(A("mm_", RC + S, RI), [[0, RI - RC - S]], 0, 0)
     lin(A("usb", p1=40), A("usi", p1=40), -8.0, 0.0)
     for t in range(NT):
         bank = A(["ps2", "ps4", "ps4", "ps5", "ps5"][t], [0, 0, 256, 0, 256][t], [256, 256, 512, 256, 512][t])
@@ -304,12 +311,13 @@ def build(T, rank, par=PAR):
     tt(A("wc", 0, C), A("w0s"), A("tmp0"), ALU.mult)
     act(A("al0"), A("tmp0"), AF.Identity, accum=A("col", 4, 5))
     ts(A("col", 8, 9), A("col", 4, 5), -float(C), None, ALU.add)
-    for t in range(NT):
-        copy(A("cnb", C * t, C * t + C, 1, 0, 8), A("cni", C * t, C * t + C, 1, 0, 8), "g", "cnb")
+    for a in range(0, NT * C, 640):
+        lin(A("cnb", a, a + 640, 1, 0, 8), A("cni", a, a + 640, 1, 0, 8), 1.0, 0.0)
     mm([(A("ps7", 0, 80), O8(b), A("cnb", b, NT * C, 16, 0, 8)) for b in range(16)])
     for t in range(NT):
         lin(A("th", 48 * t, 48 * t + 16), A("ps7", 16 * t, 16 * t + 16), 90.0, 9.0)
-    lin(A("thb"), A("ps7", 0, 80), -90.0, 99.0)
+    o = act(A("thb"), A("ps7", 0, 80), AF.Silu, 99.0, -90.0)
+    o["alts"]["a"] = (o["alts"]["a"][0] + 1300.0, o["alts"]["a"][1])
 
     def sums(c0, c1, x0, fb, step, x):
         for a in range(c0, c1, step):
@@ -323,51 +331,78 @@ def build(T, rank, par=PAR):
         scan(A("ee", x0, x0 + n), A("cap", 0, n), A("xx", x0 - 1, x0 - 1 + n), 2.0 ** 20, ALU.min, ALU.add, "scan" + x)
         mm([(vb, O(k), A("ee", x0 + 1 + k, x0 + n, 16)) for k in range(15)], "V" + x)
 
-    def sites(t, c0, c1, vb, dn, ph, old, hw, x):
+    def cut(r, a, b):
+        return A(r[0], r[3] + a, r[3] + b)
+
+    def sites(t, c0, c1, vb, dn, ph, runs, x):
         sg, mv = A("sg", c0, c1), A("mv", c0, c1)
         act(sg, vb, AF.Sign, bias=A("col", 2, 3), tag="ge" + x)
         tt(mv, dn, sg, ALU.mult, "mv" + x)
-        mm([(ph, A("ident"), old), (ph, O(t + 1, "zzh"), mv)], "hnew" + x)
-        if t == NT - 1:
-            ts(hw, ph, A("col", 5, 6), None, ALU.add, tag="hw" + x, act=(AF.Identity, A("col", 5, 6), 1.0))
-        else:
-            copy(hw, ph, "va", "hw" + x)
+        mm([(ph, O(t + 1, "zzh"), mv)] + [(cut(ph, a - c0, b - c0), A("ident"), old) for a, b, old, _ in runs], "hnew" + x)
+        for a, b, _, hw in runs[::-1]:
+            if t == NT - 1:
+                ts(hw, cut(ph, a - c0, b - c0), A("col", 5, 6), None, ALU.add, tag="hw" + x, act=(AF.Identity, A("col", 5, 6), 1.0))
+            else:
+                copy(hw, cut(ph, a - c0, b - c0), "va", "hw" + x)
 
     def shut(nk, swu, hb, eq, po, x):
         lin(nk, IND(A("nbt"), swu), 1.0, -MID, "nk" + x)
         for b, e in zip(hb, eq):
             tt(e, nk, b, ALU.is_equal, "eq" + x)
-        mm([(po, A("ident"), nk)] + [(po, A("i2k"), e) for e in eq], "o" + x)
+        trip = [(po, A("ident"), nk)] + [(po, A("i2k"), e) for e in eq]
+        if x:
+            mm(trip, "o" + x)
+        else:
+            mm(trip[:-2], "o", closes=False, whole=po[0])
+            mm(trip[-2:-1], "o", opens=False, closes=False, whole=po[0])
+            mm(trip[-1:], "o", opens=False, whole=po[0])
 
-    def ahead(c0, c1, sw, hb, eq, po, out, x):
+    def wrap(n, sw, lhs, src, out, x):
+        mm([(sw, lhs, src), (sw, A("ident"), A("ramp", 0, n))], "sib" + x)
+        scan(A("kept", x and C or 0, (x and C or 0) + n), A("pick", 0, n), sw, 0.0, ALU.max, ALU.min, "sip" + x)
+        ts(out, A("kept", (x and C or 0) + 15, (x and C or 0) + n, 16), A("col", 6, 7), None, ALU.add, tag="swu" + x,
+           act=(AF.Identity, A("col", 6, 7), 1.0))
+
+    def ahead(c0, c1, sw, hb, eq, po, runs, x):
         mv, swu = A("mv", c0, c1), A("swu", c0 // 16, c1 // 16)
-        mm([(sw, O(b), A("mv", c0 + b, c1, 16)) for b in range(16)], "siw" + x)
+        wrap(c1 - c0, sw, A("boh"), mv, swu, x)
         mm([(hb[-1], A("boh"), mv)], "hbl" + x)
-        lin(swu, sw, 0.5, MID, "swu" + x)
         shut(A("nn", c0, c1), swu, hb, eq, po, x)
-        copy(out, po, "va", "pw" + x)
+        for a, b, out in runs[::-1]:
+            copy(out, cut(po, a - c0, b - c0), "va", "pw" + x)
 
-    HL = A("oh", 16, 19)
     XI = 16 * (C + len(CHUNKS) + 2)
     for t in range(NT):
         last = t == NT - 1
         nth.clear()
-        P0 = t * PAYW
-        L0 = (t - 1) * PAYW
-        iota(A("mm_", 0, 7 * S), [[0, 7], [2, S]], NONE + 2, 0, "refill")
-        iota(A("mm_", 7 * S, RC + S), [[0, RC - 6 * S]], NONE, 0, "refill")
-        vb, dn, ph, po, *hb = [A("ps%d" % (2 + k // 2), C * (k % 2), C * (k % 2) + C) for k in range(8)]
-        mm([(dn, A("dm"), A("nk", 0, C))] + ([(dn, A("c15"), A("ones", 0, C))] if t else []), "dn")
+        step[0] = t
+        P0, L0 = t * PAYP, (t - 1) * PAYW
+        HL = A("oh", 20 * ((t + 1) % 2) + 16, 20 * ((t + 1) % 2) + 19)
+        HW = A("owu", HL[3], HL[4])
+        H0 = 20 * (t % 2)
+        iota(A("mm_", 0, 7 * S), [[0, 7], [6, S]], 3 * (NONE + 2) + ID0, 0, "refill")
+        iota(A("mm_", 7 * S, RC + S), [[0, RC - 6 * S]], 3 * NONE + ID0, 0, "refill")
+        end = C + S if t else C
+        vb, dn, ph, po, *hb = [A("ps%d" % (2 + k // 2), CUT * (k % 2), CUT * (k % 2) + CUT) for k in range(8)]
+        vb2, dn2, ph2, po2 = [A("ps7", (C + S - CUT) * k, (C + S - CUT) * k + end - CUT) for k in range(4)]
+        hb2 = [A(b, a, a + end - CUT) for b, a in (("ps4", 384), ("ps5", 384), ("ps3", 384), ("ps0", 256), ("ps1", 256))]
+        if CUT == C:
+            hb2 = [A("ps7", 192 + S * p, 192 + S * p + S) for p in range(NT)]
+        mm([(dn, A("dm"), A("nk", 0, CUT))] + ([(dn, A("c15"), A("ones", 0, CUT))] if t else []), "dn")
         for p in range(0 if last else t + 1):
-            mm([(hb[p], SEL(p), A("h16"))], "hb")
+            mm([(hb[p], SEL(p), A("h16", 0, CUT))], "hb")
+            if CUT < C:
+                mm([(cut(hb2[p], 0, C - CUT), SEL(p), A("h16", CUT, C))], "hbb")
         for i, (c0, c1) in enumerate(CHUNKS):
             fb, x0 = A("ps%d" % (i % 2), c0, c1), 16 * (c0 + i + 1)
             sums(c0, c1, x0, fb, GSTEP, "")
-            tt(A("wv", WN + c0, WN + c1), fb, A("wc", c0, c1), ALU.mult, "w1")
-            votes(c0, c1, x0, fb, A("ub", C * t + c0, C * t + c1), A("ps2", c0, c1), "")
-        sites(t, 0, C, vb, dn, ph, A("h16"), A("hw", 0, C), "")
+            tt(A("wv", 3 * c0 + 1, 3 * c1, 3), fb, A("wc", c0, c1), ALU.mult, "w1")
+            votes(c0, c1, x0, fb, A("ub", C * t + c0, C * t + c1), cut(vb, c0, c1) if c0 < CUT else cut(vb2, c0 - CUT, c1 - CUT), "")
+        sites(t, 0, CUT, vb, dn, ph, [(0, CUT, A("h16", 0, CUT), A("hw", 0, CUT))], "")
         if not last:
-            ahead(0, C, A("ps2", C, C + 16), hb[:t + 1] + [vb], [A("eq", C * p, C * p + C) for p in range(t + 2)], po, A("pw", 0, C), "")
+            ahead(0, CUT, dn, hb[:t + 1] + [vb], [A("eq", C * p, C * p + CUT) for p in range(t + 2)], po,
+                  [(0, CUT, A("pw", 0, CUT))], "")
+        runs = [(CUT, C, A("h16", CUT, C), A("hw", CUT, C), A("pw", CUT, C))] if CUT < C else []
         if t > 0:
             arrive("cnt%d" % (t - 1), [A("cnt", N * (t - 1), N * t)], par["hopc"], "sc%d" % (t - 1))
             tr = []
@@ -382,33 +417,36 @@ def build(T, rank, par=PAR):
             copy(A("uin"), IND(A("ub", C * t, C * t + WN), HL), "va", "uin")
             arrive("arh%d" % (t - 1), [old], par["hop"], "sh%d" % (t - 1))
             arrive("arr%d" % (t - 1), [A("land", L0, L0 + PAYW)], par["hop"], "sp%d" % (t - 1))
-            sw, po, fb, vb, dn = A("ps7", 240, 243), A("ps7", 244, 292), A("ps7", 292, 340), A("ps7", 340, 388), A("ps7", 388, 436)
-            hb = [A("ps7", S * p, S * p + S) for p in range(NT)]
-            mm([(sw, A("zr", 144 * (t - 1) + 15 - b, 144 * (t - 1) + 143 - b), A("landh", S * (t - 1) + b, S * t, 16)) for b in range(16)], "siwa")
+            po, fb = A("ps6", 256, 256 + S), A("ps6", 320, 320 + S)
+            hb = [cut(r, C - CUT, C + S - CUT) for r in hb2[:t + 1]]
+            wrap(S, A("ps7", 448, 448 + S), SEL(t), old, A("swa", 0, 3), "a")
             for p in range(t + 1):
                 mm([(hb[p], SEL(p), old)], "hba")
-            lin(A("swa", 0, 3), sw, 1.0, MID, "swa")
-            shut(A("nk", C, C + S), A("swa", 0, 3), hb[:t + 1], [A("eqa", S * p, S * p + S) for p in range(t + 1)], po, "a")
+            shut(A("nk", C, C + S), A("swa", 0, 3), hb, [A("eqa", S * p, S * p + S) for p in range(t + 1)], po, "a")
             lin(A("oq", C, C + S), po, 1.0, MID + 16, "oqa")
-            mm([(dn, A("dm"), A("nk", C, C + S))], "dni")
             sums(C, C + S, XI, fb, GSTEPI, "i")
-            tt(A("w1i"), fb, A("land", L0, L0 + S), ALU.mult, "w1i")
-            copy(IND(A("wv", WN, 2 * WN), HL), A("w1i"), tag="scw")
+            tt(A("w1i"), fb, A("land", L0 + 1, L0 + 1 + S), ALU.mult, "w1i")
+            copy(IND(A("wv"), HW), A("w1i"), tag="scw")
             if not last:
-                ts(A("col", 20, 21), A("land", L0 + S, L0 + S + 1), 0.0, float(S), ALU.max, ALU.min, tag="nin")
-                ts(A("col", 8, 9), A("col", 20, 21), A("pay", L0 + S, L0 + S + 1), 0.0, ALU.add, ALU.min, tag="db")
-            votes(C, C + S, XI, fb, A("uin"), vb, "i")
-            sites(t, C, C + S, vb, dn, A("ps7", 436, 484), old, A("hwi"), "i")
+                ts(A("col", 8, 9), A("land", L0, L0 + 1), A("pay", P0 - PAYP + 108, P0 - PAYP + 109), 0.0, ALU.add, ALU.min, tag="db")
+            votes(C, C + S, XI, fb, A("uin"), cut(vb2, C - CUT, C + S - CUT), "i")
+            runs.append((C, C + S, old, A("hwi"), A("pwi")))
+        if runs:
+            mm([(dn2, A("dm"), A("nk", CUT, end))] + ([(cut(dn2, 0, C - CUT), A("c15"), A("ones", 0, C - CUT))] if t and CUT < C else []), "dnb")
+            sites(t, CUT, end, vb2, dn2, ph2, [r[:4] for r in runs], "b")
+        if t > 0:
             copy(IND(A("hw"), HL), A("hwi"), tag="sch")
-            if not last:
-                ahead(C, C + S, sw, hb[:t + 2], [A("eqi", S * p, S * p + S) for p in range(t + 2)], po, A("pwi"), "i")
+        if runs and not last:
+            ahead(CUT, end, dn2, hb2[:t + 1] + [vb2],
+                  [A("eqb", 112 * p, 112 * p + end - CUT) for p in range(t + 2)], po2, [r[:2] + r[4:] for r in runs], "b")
+            if t > 0:
                 copy(IND(A("pw"), HL), A("pwi"), tag="sco")
-        W1 = A("wv", WN, WN + C)
+        W1 = A("wv", 1, 3 * C, 3)
         ts(A("fl", 2 * C, 3 * C), W1, A("lh", 8 + t, 9 + t), None, ALU.is_gt, tag="ch")
         ts(A("fl", 0, C), W1, A("lh", t, t + 1), None, ALU.is_lt, tag="cl")
         ts(A("fl", C, 2 * C), W1, 0.0, None, ALU.is_gt, tag="al", act=(AF.Sign, 0.0, 1.0))
-        lin(A("wv", 0, C), W1, 0.5, 0.0, "half")
-        lin(A("wv", 2 * WN, 2 * WN + C), W1, 2.0, 0.0, "twice")
+        lin(A("wv", 0, 3 * C, 3), W1, 0.5, 0.0, "half")
+        lin(A("wv", 2, 3 * C, 3), W1, 2.0, 0.0, "twice")
         mm([(A("ps6", 16, 64), O(b), A("fl", b, 3 * C, 16)) for b in range(16)], "pw3")
         tt(A("fw", 32, 80), A("ps6", 16, 64), A("th", 48 * t, 48 * t + 48), ALU.is_ge, "fw")
         tt(A("dbl"), A("ps6", 16, 32), A("thb", 16 * t, 16 * t + 16), ALU.is_ge, "dbl")
@@ -417,50 +455,47 @@ def build(T, rank, par=PAR):
         scan(A("sc"), A("rs32"), A("fw"), 0.0, ALU.mult, ALU.add, "sc")
         X = 64
         sh, sc_, nh = A("sc", 0, 16), A("sc", 64, 80), A("sc", 16, 32)
-        xa, xb, xc, xv = A("ps6", X, X + 48, 3), A("ps6", X + 1, X + 48, 3), A("ps6", X + 48, X + 96, 3), A("ps6", X + 128, X + 144)
+        xa, xb, xc, xv = A("ps6", X, X + 48, 3), A("ps6", X + 1, X + 48, 3), A("ps6", X + 48, X + 96, 3), A("ps6", X + 50, X + 96, 3)
         ex = A("ps6", X + 108, X + 109)
-        mm([(A("ps6", X, X + 112), A("ident"), A("cc", 0, 112)),
-            (xb, A("l2"), high), (xa, A("l2"), hole), (xc, A("l2"), hole)], "px0", closes=False, whole="ps6")
-        mm([(xa, A("bo"), sh), (xb, A("bo"), sc_), (xb, A("nbo"), nh), (xc, A("bo"), sh), (xc, A("nbo"), nh),
-            (A("ps6", X + 98, X + 108, 3), A("bo"), A("sc", 80, 84)),
-            (ex, A("bo"), A("sc", 80, 81)), (ex, A("nbo"), A("sc", 16, 17))], "px", opens=False, whole="ps6")
-        scan(A("rr", 0, 109), A("rsx", 0, 109), A("ps6", X, X + 109), 0.0, ALU.max, ALU.min, "rr")
-        copy(A("of2", 0, 36), A("rr", 2, 108, 3), "va", "of2")
-        mm([(xv, A("ident"), A("cc", 128, 144)), (xv, A("ip"), A("dbl")), (xv, A("im"), die), (xv, A("im"), high)], "xv")
-        ee = A("rr", 108, 109)
-        copy(A("pay", P0 + S, P0 + S + 1), ee, "va", "e")
+        mm([(A("ps6", X, X + 48), A("ident"), A("cc", 0, 48)), (xb, A("l2"), high), (xa, A("l2"), hole)], "px0", closes=False, whole="ps6")
+        mm([(xa, A("bo"), sh), (xb, A("bo"), sc_), (xb, A("nbo"), nh)], "px", opens=False, whole="ps6")
+        scan(A("pay", P0, P0 + 48), A("rsx", 0, 48), A("ps6", X, X + 48), 0.0, ALU.max, ALU.min, "rr")
+        copy(A("of2", 0, 16), A("pay", P0 + 2, P0 + 48, 3), "va", "of2")
+        mm([(A("ps6", X + 48, X + 112), A("ident"), A("cc", 48, 112)), (xv, A("ip"), A("dbl")), (xv, A("im"), high),
+            (xc, A("l2"), hole), (xc, A("bo"), sh), (xc, A("nbo"), nh), (A("ps6", X + 98, X + 108, 3), A("bo"), A("sc", 80, 84)),
+            (ex, A("bo"), A("sc", 80, 81)), (ex, A("nbo"), A("sc", 16, 17))], "pxb")
+        scan(A("pay", P0 + 48, P0 + 112), A("rsx", 48, 112), A("ps6", X + 48, X + 112), 0.0, ALU.max, ALU.min, "rrb")
+        copy(A("of2", 16, 36), A("pay", P0 + 50, P0 + 108, 3), "va", "of2b")
         if not last:
             dc = A("dcol", 8 * t, 8 * t + 1)
-            ts(dc, ee, A("col", 8, 9), None, ALU.subtract, tag="d")
+            ts(dc, A("pay", P0 + 108, P0 + 109), A("col", 8, 9), None, ALU.subtract, tag="d")
             send("sc", t, [dc])
-        copy(IND(A("mm_"), A("of2", 0, 16)), A("ids"), tag="scat")
-        tt(A("av"), xv, alive, ALU.mult, "av")
-        scan(A("ra"), A("pick"), A("mm_", RC, RC + S), 0.0, ALU.max, ALU.min, "ra")
-        OS = A("osu", 0, 3)
-        copy(OS, A("ra", 15, S, 16), "va", "osu")
-        copy(A("payh", S * t, S * t + S), IND(A("hw"), OS), "va", "payh")
-        copy(A("pay", P0, P0 + S), IND(A("wv", 0, WN), OS), "va", "payw")
+        copy(IND(A("mm_", 0, RI), A("of2", 0, 16)), A("ids"), "va", "scat")
+        scan(A("ra"), A("pick", 0, S), A("mm_", RC, RC + S), 0.0, ALU.max, ALU.min, "ra")
+        lin(A("osu", 0, 3), A("ra", 15, S, 16), 1.0 / 3, -ID0 / 3, "osu")
+        lin(A("osu", 4, 7), A("ra", 15, S, 16), 1.0, -float(ID0), "osw")
+        copy(A("payh", S * t, S * t + S), IND(A("hw"), A("osu", 0, 3)), "va", "payh")
+        copy(A("pay", P0 + 112, P0 + PAYP), IND(A("wv"), A("osu", 4, 7)), "va", "payw")
         send("sh", t, [A("payh", S * t, S * t + S)])
-        send("sp", t, [A("pay", P0, P0 + PAYN)])
+        send("sp", t, [A("pay", P0 + 111, P0 + PAYP)])
         copy(A("gb"), IND(A("mm_"), A("of2", 16, 35)), "va", "gb")
-        mm([(A("ps6", 224, 243), O(b), A("gb", b, S + C, 16)) for b in range(16)], "rb")
-        lin(A("oh", 0, 19), A("ps6", 224, 243), 1.0 / 16, 0.0, "oh")
-        tt(A("owf"), A("ps6", 224, 240), A("av"), ALU.add, "owf")
-        lin(A("owu"), A("owf"), 1.0 / 16, 0.0, "owu")
+        mm([(A("ps6", 224, 243), O(b), A("gb", b, S + C, 16)) for b in range(16)] + [(A("ps6", 240, 243), A("bo"), A("ones", 0, 3))], "rb")
+        lin(A("oh", H0, H0 + 19), A("ps6", 224, 243), 1.0 / 48, -(ID0 + 1) / 3, "oh")
+        lin(A("owu", H0, H0 + 19), A("ps6", 224, 243), 1.0 / 16, -float(ID0), "owu")
         if last:
-            copy(A("h32", 0, C), IND(A("hw"), A("oh", 0, 16)), "va", "h32")
+            copy(A("h32", 0, C), IND(A("hw"), A("oh", H0, H0 + 16)), "va", "h32")
         else:
             for c0, c1 in FIRST:
-                src = IND(A("pw"), A("oh", c0 // 16, c1 // 16))
-                ts(A("nk", c0, c1), src, MID + 1, 0.0, ALU.add, ALU.max, "nkg", (AF.Relu, MID + 1, 1.0))
-                lin(A("oq", c0, c1), A("nk", c0, c1), 1.0, 15.0, "oq")
-            copy(A("h16"), IND(A("hw"), A("oh", 0, 16)), "va", "h16")
-        copy(A("wc", 0, C), IND(A("wv", 0, 2 * WN + C), A("owu")), "va", "wc")
-    L0 = (NT - 1) * PAYW
+                lin(A("oq", c0, c1), IND(A("pw"), A("oh", H0 + c0 // 16, H0 + c1 // 16)), 1.0, MID + 16, "oq")
+            ts(A("nk", 0, C), A("oq", 0, C), -15.0, 0.0, ALU.add, ALU.max, "nkg", (AF.Relu, -15.0, 1.0))
+            copy(A("h16"), IND(A("hw"), A("oh", H0, H0 + 16)), "va", "h16")
+        copy(A("wc", 0, C), IND(A("wv"), A("owu", H0, H0 + 16)), "va", "wc")
+    L0, HL = (NT - 1) * PAYW, A("oh", H0 + 16, H0 + 19)
+    step[0] = NT
     arrive("arh%d" % (NT - 1), [A("landh", S * (NT - 1), S * NT)], par["hop"], "sh%d" % (NT - 1))
     arrive("arr%d" % (NT - 1), [A("land", L0, L0 + PAYW)], par["hop"], "sp%d" % (NT - 1))
-    copy(IND(A("h32"), HL), A("landh", S * (NT - 1), S * NT), tag="sch")
-    copy(IND(A("wc"), HL), A("land", L0, L0 + S), tag="scw")
+    copy(IND(A("h32"), HL), A("landh", S * (NT - 1), S * NT), tag="endh")
+    copy(IND(A("wc"), HL), A("land", L0 + 1, L0 + 1 + S), tag="endw")
     store("yh", "h32", "a", "outh")
     store("yw", "wc", "s", "outw")
     return ops
@@ -595,21 +630,15 @@ def choose(ops, who):
     return [("v" if o["name"] in who else "a") if len(o["alts"]) > 1 else (list(o["alts"]) or [None])[0] for o in ops]
 
 
-def heads(ops, eng, par):
-    end, start = [0.0] * len(ops), [0.0] * len(ops)
-    for i, o in enumerate(ops):
-        start[i] = max([end[j] + par["lat"] for j in o["near"]] + [0.0 if o["behind"] is None else start[o["behind"]]])
-        end[i] = start[i] + (o["alts"][eng[i]][0] if eng[i] else 0.0) + o.get("lat", 0.0)
-    return start
-
-
-def plan(par=PAR, who=WHO, ahead=AHEAD, ops=None, mix=MIX):
+def plan(par=PAR, who=WHO, when=WHEN, ops=None):
     if ops is None:
         ops = build(None, 1, par)
         needs(ops)
-    eng = choose(ops, who)
-    late, early = tails(ops, list(range(len(ops))), eng, False, par), heads(ops, eng, par)
-    return place(ops, [(1 - mix) * a - mix * b + ahead.get(o["name"], 0.0) for a, b, o in zip(late, early, ops)], par, eng)
+    key = [max(o["step"], 0) * PERIOD + when.get(o["name"], -PERIOD) for o in ops]
+    for i, o in enumerate(ops):
+        for j in o["near"] + ([] if o["behind"] is None else [o["behind"]]):
+            key[i] = max(key[i], key[j] + 0.02)
+    return sorted(range(len(ops)), key=lambda i: (key[i], i)), choose(ops, who)
 
 
 PLAN = {}
@@ -635,7 +664,7 @@ def slots(kind, t, r):
     if kind == "sh":
         return "payh", "landh", t * S, t * S, S, "arh%d" % t
     if kind == "sp":
-        return "pay", "land", t * PAYW, t * PAYW, PAYN, "arr%d" % t
+        return "pay", "land", t * PAYP + 111, t * PAYW, PAYN, "arr%d" % t
     return "dcol", "cnt", 8 * t, N * t + r, 1, "cnt%d" % t
 
 

@@ -8,22 +8,26 @@ NONE = C
 WN = C + 2 * S + 16
 PAYN, PAYW, PAYP = S + 1, S + 4, S + 112
 CUT = 256
-MID = 1023.0
+MID = 1024.0
+UP = 32.0
 BASE = 786432.0
 TWO23 = 8388608.0
 ID0 = 32
 RH, RC, RD, RI, MW = 0, 593, 864, 1120, 1888
 
-CHUNKS = [(0, 64), (64, 128), (128, 192), (192, 256)]
+CHUNKS = [(0, 128), (128, 256)]
+PIECE = 64
+PARTS = [(0, 128), (128, 256)]
+BYPE = ""
 FIRST = [(0, 128), (128, 256)]
 GSTEP, GSTEPI = 32, 24
 XW = 16 * (C + S + 8)
 
 F32, BF, F16, I32, U16 = "float32", "bfloat16", "float16", "int32", "uint16"
 _SB = {
-    "nbt": (V, I32), "qt": (V + 16, BF), "w0s": (C, F32), "lh": (16, F32), "s0i": (C, I32), "usi": (C, I32),
+    "nbt": (V, I32), "qt": (V + 16, BF), "lh": (16, F32), "s0i": (C, I32), "usi": (C, I32),
     "cni": (NT * C, I32), "s0h": (C, F16), "usb": (C, BF), "cnb": (NT * C, BF), "ub": (NT * C + WN - C, F32),
-    "ones": (640, BF), "ident": (128, BF), "bo": (128, BF), "bo1": (128, BF), "nbo": (128, BF), "boh": (128, BF), "l2a": (128, BF), "l2": (128, BF),
+    "ones": (640, BF), "ident": (128, BF), "bo": (128, BF), "bo1": (128, BF), "nbo": (128, BF), "boh": (128, BF), "bo64": (128, BF), "l2a": (128, BF), "l2": (128, BF),
     "dma_": (128, BF), "dmb": (128, BF), "dm": (128, BF), "c15": (128, BF), "jj": (256, BF), "z8": (144, BF), "bo8a": (128, BF), "bo8": (128, BF),
     "zt": (640, BF), "zz": (144, BF), "zzh": (144, BF), "i11": (128, BF), "i2k": (128, BF), "ip": (128, BF), "im": (128, BF), "sel": (640, BF),
     "mki": (C, I32), "mki2": (C, I32), "pik1": (C, BF), "pick": (C, BF), "ramp": (C, BF), "kept": (C + 112, F32), "ids": (C, F32), "pci": (8, I32),
@@ -36,8 +40,8 @@ _SB = {
     "owu": (40, U16), "sg": (C + S, BF), "mv": (C + S, F16),
     "hwi": (S, F32), "pwi": (S, F32), "swu": (20, U16), "swa": (4, U16), "nk": (C + S, F16), "nn": (C + S, F16),
     "eq": (5 * C, BF), "eqb": (5 * 112, BF), "eqa": (5 * S, BF), "uin": (S, F32),
-    "al0": (C, BF), "col": (32, F32), "dcol": (8 * NT, BF), "tmp0": (C, F32),
-    "pay": (NT * PAYP, F32), "land": (NT * PAYW, F32), "payh": (NT * S, F16), "landh": (NT * S, F16), "cnt": (NT * N, BF),
+    "al0": (C, BF), "col": (32, F32), "dcol": (8 * NT, BF),
+    "pay": (NT * PAYP, F32), "land": (NT * PAYW, F32), "payh": (NT * S + 56, F16), "landh": (NT * S + 56, F16), "cnt": (NT * N, BF),
 }
 SCRATCH = {k: ("sbuf", [128, w], d) for k, (w, d) in _SB.items()}
 for _b in range(8):
@@ -54,7 +58,9 @@ WHO = ['boh', 'e', 'gx', 'gx.3', 'gxi', 'i2k', 'nk0.1', 'nka', 'nki', 'of2', 'oq
 PERIOD = 14.0
 WHO = '+boh +col.2 +h16 +i11 +i2k +im +ip +nbo +oq0 +pick +sel.4 +th.5 +ub.1 +ub.3 +zzh 0gb 0gx.1 0gx.3 0gx.5 0gx.7 0oq 0payh 0pw 0scat 0swu gx.1 gx.3 gx.5 gx.7 gxi hw hwb of2 oq osu payh payw pw pwb'.split()
 TURNS = '+pci@-13.176 +cwi@-12.111 +mki@-12.083 +ones@-11.384 +bo1@-9.603 +z8@-9.104 +ident@-9.003 +pci2@-8.345 +th@-8.304 +cc@-8.233 +fw@-8.145 +rs32@-8.122 +zz@-7.893 +bo8a@-7.775 +cap@-7.705 +ldcoin@-7.697 +cap.1@-7.653 +ldus@-7.372 +lds0@-7.271 +rsx@-7.241 +qt@-7.236 +mki2@-6.725 +col.1@-6.715 +cc.6@-6.56 +pw@-6.506 +rsx.1@-6.453 +lh@-6.326 +cw@-6.215 +col@-6.163 +im@-6.075 +col.3@-5.814 +hw@-5.764 +i11@-5.735 +rs32.1@-5.724 +ldnb@-5.717 +tmp0@-5.583 +zz.1@-5.459 +bo@-5.435 +ps1@-5.334 +s0h@-5.3 +i2k@-5.295 +zzh@-5.285 +usb@-5.208 +cc.5@-5.164 +cnb@-5.138 +wv@-4.983 +bo8@-4.982 +cnb.1@-4.931 +ps6@-4.656 +zt@-4.519 +ps3@-4.343 0refill.1@-4.319 +ps7@-4.116 +pik1@-4.002 +cc.4@-3.992 +sel@-3.768 +ps2@-3.682 +ldqs@-3.588 +ramp@-3.479 +swu@-2.328 +mm_@-2.305 +ldw0@-2.282 +al0@-2.24 +nk0.1@-2.23 +nk0@-2.221 +nbo@-1.752 +col.2@-1.742 +boh@-1.706 +th.1@-1.625 +cc.1@-1.189 +h16@-1.179 +thb@-1.123 +ip@-1.112 +dmb@-0.916 +pick@-0.855 +cc.3@-0.735 0refill@-0.712 +col.4@-0.707 +dma_@-0.647 +dm@-0.533 +cc.2@-0.512 +eq0.1@-0.255 +eq0@-0.225 +mm_.1@-0.205 +ub.1@-0.135 +oq0@-0.11 +wc.1@0.09 0gx@0.216 +l2a@0.239 +o0@0.273 refill@0.705 +ldlo@0.805 +c15@0.986 +ps4.1@1.027 0gx.1@1.028 +l2@1.06 +o0.1@1.127 0y@1.13 gx.3@1.182 0y.1@1.236 0gx.5@1.246 0gx.3@1.256 +oq0.1@1.267 gx.1@1.308 0w1.1@1.357 gx.7@1.372 hb.1@1.377 0f@1.492 0gx.2@1.524 0gx.7@1.557 0f.1@1.816 y@1.892 0thr@1.939 +col.7@1.949 0gx.4@2.076 hb.2@2.143 hb@2.17 +ids@2.428 hb.3@2.466 gx@2.536 gx.2@2.573 f@2.587 0V@2.764 0gx.6@2.823 f.1@2.826 scan@2.851 0y.2@2.874 0f.2@2.874 +ps5@2.881 0w1@2.884 +th.2@2.942 hba@2.965 siba@2.975 gx.4@3.087 0f.3@3.099 hba.3@3.139 hba.4@3.199 gx.6@3.237 0dn@3.248 gx.5@3.289 hba.2@3.339 hba.1@3.349 swua@3.416 0w1.2@3.421 0scan@3.429 y.1@3.431 thr.1@3.431 thr@3.441 sipa@3.441 tot@3.45 0al@3.535 f.2@3.553 eqa.3@3.847 nka@3.852 up@3.857 0w1.3@3.881 0y.3@3.891 eqa.1@3.907 +jj@3.952 uin@4.049 0fw@4.087 0thr.2@4.194 endh@4.219 refill.1@4.427 eqa.2@4.484 eqa.4@4.494 +ldhi@4.496 0ch@4.516 0scan.1@4.516 0thr.1@4.526 0cl@4.536 +sel.3@4.573 oa@4.671 f.3@4.681 eqa@4.684 0scan.2@4.687 w1@4.816 lh@4.84 0pw3@4.928 0dbl@5.02 oqa@5.139 y.2@5.245 scan.1@5.255 w1.3@5.255 dn@5.265 gxi@5.322 V@5.421 0hole@5.432 w1.2@5.445 thr.2@5.455 +sel.1@5.492 endw@5.55 0V.1@5.643 +ps5.1@5.653 0px@5.659 0thr.3@5.695 y.3@5.746 gxi.1@5.927 w1.1@5.946 w1i@5.946 scan.2@5.956 0sc@6.016 +sel.2@6.079 +th.3@6.159 0rr@6.294 fi@6.298 0scan.3@6.304 yi@6.308 0px0@6.421 dnb@6.442 scan.3@6.463 thr.3@6.47 scw@6.473 cl@6.48 ch@6.503 +th.4@6.534 V.1@6.549 al@6.617 +h32@6.636 V.2@6.708 scani@6.75 twice@6.755 0twice@6.834 0V.2@6.864 0scat@6.951 0of2@7.061 0rrb@7.071 styw@7.075 0mv@7.105 half@7.138 V.3@7.178 Vi@7.226 0V.3@7.243 0pxb@7.285 0osw@7.312 pw3@7.426 0half@7.488 0ge@7.498 sib@7.567 styh@7.709 0of2b@7.769 +ub.5@7.779 ge@7.869 thri@8.127 mv@8.393 px0@8.403 0ra@8.407 0d@8.605 0gb@8.606 +ub.2@8.648 rrb@8.848 fw@8.862 px@8.939 db@9.055 dbl@9.274 mvb@9.29 hole@9.309 +ps4@9.384 sc@9.401 nk@9.423 sip@9.44 0osu@9.47 geb@9.522 sipb@9.533 0sib@9.569 swu@9.584 rr@9.592 scat@9.594 0hw@9.624 0sip@9.627 0hnew@9.671 0hb@9.712 +col.5@9.726 0swu@9.806 of2@9.896 0>sc@9.924 d@9.948 hnew@10.061 hw@10.084 0rb@10.154 sibb@10.234 0hbl@10.492 pxb@10.526 eq@10.548 eq.1@10.576 0o.1@10.598 +c15.1@10.731 of2b@10.752 hnewb@10.817 +ub.3@10.829 0>sh@10.836 0payh@10.908 hblb@10.928 0o@10.969 0nk@11.014 hbl@11.09 swub@11.111 o@11.156 eq.2@11.166 sch@11.2 osu@11.215 o.2@11.311 ob@11.311 o.1@11.381 hwb@11.395 eq.3@11.398 ra@11.4 >sc@11.672 gb@11.721 +ub@11.809 rb@11.911 eq.4@12.051 0eq@12.192 eqb@12.33 payh@12.34 nkb@12.566 eqb.2@12.576 eqb.3@12.576 0eq.1@12.698 osw@12.79 eqb.1@12.957 owu@13.006 eqb.4@13.04 0owu@13.718 pw@13.779 h32@13.873 pwb@13.877 0oq@13.908 oh@13.95 >sh@14.052 +ub.4@14.11 0wc@14.199 0oh@14.355 0o.2@14.475 +sel.4@14.636 sco@14.731 >sp@14.739 +th.5@14.78 payw@14.88 oq@15.362 wc@15.402 +wc@15.619 h16@15.849 oq.1@15.882 0payw@15.984 0h16@16.006 +col.6@16.007 0oq.1@16.061 0pw@16.232 0nkg@17.376 nkg@19.029 0>sp@19.9'
-WHEN = {x.split("@")[0]: float(x.split("@")[1]) for x in TURNS.split()}
+TURNS = "^0payh ^0osw +jj +col.5 ^0payw ^hwb* ^0eqc ^0eqc.1 ^ra ^od.1 +mm_.1 ^>sc +cap.2 ^0eqd.1 ^0rb +swu ^0eqd ^wc ^nkb* ^payh ^4ra ^sch* ^od ^pwd +nk0 0refill.1 ^eqb.1 ^eqb.3 ^0oc +ps2 ^rb _+pw ^+th.2* ^+thb.1* +ub.1 ^0oh ^0owu +cc.4 ^eqb.2 +h16* ^eqb +dma_ ^0>sh ^0oc.1 ^0od ^+ub.5* ^eqb.4 +eq0 +col.9 ^pwc ^0od.1 +nk0.1 ^4osw* +ps4 ^0h16 ^osw* ^4sch* ^payw +o0 ^ob ^+sel.2* _+ident +o0.1 ^h16 ^0wc +cc.3 +zz.1 ^0pwc* +mki2 ^owu* +ps7 +c15.1 +ldqs ^4scat _+cwi +ps4.1 ^oq.1* 4refill _+bo8a +col.6 ^+th.4* 0gx.4 hbc 4f ^0pwd* hbd.3 ^4payw* ^4osu ^oq* 4gx.3* ^sco* ^oh* gx.3* ^pwb* +col.7 4gx.1* +eq0.1 hbd.2 hbc.2 4gx.7* 4dnc ^0oq.1 0gx.2 hbd gx.2 dnd gx.1 0gx hbc.1 hbd.1 +oq0 f 4f.1 4gx.2 ^>sp _+lh f.1 4y +col ^>sf +pik1 ^+th.3* gx* ^0>sp 4gx ^nkg 4dnd 4hba.1 0f 4gx.4* +ps5 4siba 4hba.3 0gx.5 ^0oq* ^4payh 4f.2 +ps5.1 ^4rb hba.1 4sipa hba.3 0gx.1* 4f.3 _+hw f.2 4gx.6 0gx.6 4thr siba +col.3* 4hba.4 4w1 gx.4* +oq0.1* 0gx.3* 4hba.2 4eqa 4scan +dm 4uin 4hba 4gx.5 hba f.3 4tot gx.5 +dmb 0y gx.7* y sipa thr w1 ^4gb* ^^styh hba.2 gx.6 nka +ub.4 4eqa.1 ^+ub.3 eqa scan 4refill.1 ^4oh* +ldw0 +l2a swua ^^endw ^^endh +pick* +fw +thb hbc.3 0gx.7* 0f.1 0w1 4eqa.4 0f.2 4swua 4nka 4eqa.2 _+i2k* 0dnc 0thr 4eqa.3 4oa refill.1 tot eqa.2 4scan.1 eqa.3 eqa.1 4V.1 _+bo1 _+z8 4y.1 0f.3 ^4h32 y.1 scan.1 w1i +zzh 0scan 4gxi* gxi* 4w1.1 thr.1 w1.1 ^0nkg oa +ub.2 0scan.1 4V 0V uin 4thr.1 oqa ^+th.5 V +th.1* scan.3 0w1.1 fi V.1 +im _+ldnb +mm_ scan.2 4oqa dnc +ldlo 4gxi.1 _~+ones gxi.1 4scan.3 4w1i 4scan.2 4fi 0y.1 up mvc scw V.3 0cl 0ch 0V.1 0al V.2 +ldhi sibd 0pw3 4scani 4up 4half hblc 0thr.1 ^4owu* _+ldcoin pw3 gec yi hnewc sibc 4gec ch cl lh _+cc 0V.2 0dnd al ^4wc _+qt swuc 4dbl _~+ldus ged +cc.2 0px0 _+ip +ids 0scan.2 4lh ^^styw 4V.3 thri +col.2 4al 0fw Vi 4scw 4yi +l2 px0 +boh* twice 4V.2 +ramp 4cl 4ch px 4thri mvd half 0hole scani sipc refill _+c15 db _+pci2 _+rs32 4mvc fw 0hbd 0V.3 4fw 0dbl 4twice 0px 4pw3 _+bo 0sc eqc.4 _+cc.5 dbl 0mvc 0half _+bo8 hole _+cap.1 sipd 4ged 0scat sc 4Vi +sel 0scan.3 +sel.1 ^+ub +cnb.2 _+s0h* 0refill 0gec _+zz hwc* 0rr nkc _~+lds0 eqc.2 +sel.4* eqc.3 _+zt rr 0twice* _+i11 _+bo64 0hnewd +sel.3 swud geb 4hole dnb +cnb.1 4px0 0ged +h32 4sc _+rs32.1 hbld 0pxb 0of2* pxb 0sibc 0hnewc _+cc.6 _+wv 0>sc 0osu +wc eqc.1 0rrb 4mvd 0hbc 0sibd 0mvd +ps7.1 eqd.3 +col.8 _~+pci 4geb _+nbo 0gb 0sipc _+rsx.1 _+usb sibb 0swuc 0of2b* hblb eqd.2 mvb _+th 0d _+ps6 0hwc* 4rr 0nkd 4px 0sipd 4mvb 4hnewc 0hblc _+cc.1 _+col.4 _+col.1 4dnb hnewb 0hwd* nkd eqd.1 _+ps3 0ra 4hnewd 0swud* 4of2 rrb eqc of2 scat 0nkc* 0hbld +payh swub eqd _+cnb sipb _+ps1 hnewd oc.1 _+mki osu _+al0 oc 4hwc* 4hwd* 4pxb gb of2b* _+cw _+cap 4hnewb eqd.4 hwd* d >sh _~+rsx 4rrb 4hwb* 4of2b*".split()
+WHO = [x.strip("^*").lstrip("_~") for x in TURNS if x[-1] == "*"]
+WHEN = {x.strip("^*").lstrip("_~"): PERIOD * (x.count("^") - len(x) + len(x.lstrip("_~")) + i / len(TURNS)) for i, x in enumerate(TURNS)}
 
 
 def A(name, c0=0, c1=None, st=1, p0=0, p1=128):
@@ -105,7 +111,7 @@ def build(T, rank, par=PAR):
                 wr.append(r)
         tag = tag or wr[0][0]
         k = nth[tag] = nth.get(tag, -1) + 1
-        o = dict(alts=alts, rd=rd, wr=wr, tag=tag, name={-1: "+", 0: "0"}.get(step[0], "") + tag + ("." + str(k) if k else ""), step=step[0], eng=None)
+        o = dict(alts=alts, rd=rd, wr=wr, tag=tag, name={-1: "+", 0: "0", NT - 1: "4"}.get(step[0], "") + tag + ("." + str(k) if k else ""), step=step[0], eng=None)
         o.update(kw)
         ops.append(o)
         return o
@@ -222,7 +228,7 @@ def build(T, rank, par=PAR):
     load("s0", "s0i", 0, C, 1, 1, "a", 2000.0)
     load("us", "usi", 0, C, 1, NT, "a", 2200.0)
     load("qs", "qt", 16, V + 16, 16, 16, "s", par["qs"])["after"] = "ldnb"
-    load("w0", "w0s", 0, C, 16, 16, "s", par["qs"])["after"] = "ldqs"
+    load("w0", "wc", 0, C, 16, 16, "s", par["qs"])["after"] = "ldqs"
     load("coin", "cni", 0, NT * C, 1, 1, "a", 2500.0)
     memset(A("lh"), 0.0)
     load("lo", "lh", 0, NT, 16, 16, "s", par["qs"])["after"] = "ldw0"
@@ -250,7 +256,8 @@ def build(T, rank, par=PAR):
     sel(A("jj"), A("ones", 0, 256), [[0, 2], [-1, 128]], ALU.is_equal, 0.0, 0, 1)
     lin(A("i11"), A("ident"), 2.0 ** -11, 0.0)
     lin(A("i2k"), A("ident"), -4096.0, 0.0)
-    lin(A("ip"), A("ident"), float(C), 0.0)
+    o = act(A("ip"), A("ident"), AF.Silu, 0.0, float(C))
+    o["alts"]["a"] = (o["alts"]["a"][0] + 1300.0, o["alts"]["a"][1])
     lin(A("im"), A("ident"), -float(C), 0.0)
     memset(A("zz"), 0.0)
     copy(A("zz", 15, 143, 16), A("bo", 0, 128, 16))
@@ -264,11 +271,14 @@ def build(T, rank, par=PAR):
         lin(SEL(p), A("bo"), A("col", 24 + p, 25 + p), 0.0)
     ts(A("pci2"), A("pci"), 15, None, ALU.bitwise_and)
     copy(A("col", 0, 1), A("pci2", 0, 1))
-    lin(A("col", 6, 7), A("col", 0, 1), -4096.0, MID)
+    lin(A("col", 6, 7), A("col", 0, 1), -4096.0, MID - 1)
+    lin(A("col", 7, 8), A("col", 0, 1), -4096.0, -1.0)
+    ts(A("col", 9, 10), A("col", 0, 1), 0.5, MID, ALU.is_gt, ALU.mult)
+    lin(A("bo64"), A("bo"), MID / 16, 0.0)
     iota(A("ramp"), [[0, 16], [4096, 16]], 0, 0)
     ts(A("col", 1, 2), A("col", 0, 1), 15.0, -(16 * BASE + 8.5 * 4096 + 1), ALU.is_lt, ALU.mult)
     ts(A("col", 2, 3), A("col", 1, 2), 1.0, None, ALU.add)
-    ts(A("col", 3, 4), A("col", 0, 1), NT + 0.5, MID + 1, ALU.is_lt, ALU.mult)
+    ts(A("col", 3, 4), A("col", 0, 1), NT + 0.5, -MID, ALU.is_gt, ALU.mult)
     ts(A("col", 5, 6), A("col", 3, 4), -1.0, None, ALU.add)
     iota(A("cwi"), [[16, 16]], 0, 0)
     ts(A("cw"), A("cwi"), A("col", 0, 1), None, ALU.add)
@@ -281,11 +291,12 @@ def build(T, rank, par=PAR):
     memset(A("rs32"), 1.0); memset(A("rs32", 0, 84, 64), 0.0)
     memset(A("fw"), 0.0)
     memset(A("rsx"), 0.0); memset(A("rsx", 0, 109, 3), 4096.0)
-    ncap = 16 * max([c1 - c0 for c0, c1 in CHUNKS] + [S])
-    memset(A("cap", 0, ncap), 2.0 ** 20); memset(A("cap", 0, ncap, 16), BASE)
+    ncap = 16 * PIECE
+    memset(A("cap", 0, ncap // 2), 2.0 ** 20); memset(A("cap", ncap // 2, ncap), 2.0 ** 20); memset(A("cap", 0, ncap, 16), BASE)
     memset(A("ub", NT * C, NT * C + WN - C), 0.0)
     memset(A("wv", 3 * C, 3 * WN), 0.0)
-    memset(A("hw", C, WN), -1.0); memset(A("pw", C, WN), -4096.0)
+    memset(A("hw", C, WN), -1.0); memset(A("pw", C, WN), 0.0)
+    memset(A("payh", NT * S, NT * S + 50), 0.0)
     memset(A("wc", C, WN), 0.0); memset(A("h32", C, WN), 0.0)
     memset(A("th"), 9.0)
     iota(A("mm_", RC + S, RI), [[0, RI - RC - S]], 0, 0)
@@ -294,42 +305,44 @@ def build(T, rank, par=PAR):
         bank = A(["ps2", "ps4", "ps4", "ps5", "ps5"][t], [0, 0, 256, 0, 256][t], [256, 256, 512, 256, 512][t])
         mm([(bank, A("zt", 128 * t, 128 * t + 128, 1, 0, 40), A("usb", p1=40))])
         lin(A("ub", C * t, C * t + C), bank, 1.0, -2.0 ** -10)
-    lin(A("s0h", p1=8), A("s0i", p1=8), 1.0, -MID)
+    lin(A("s0h", p1=8), A("s0i", p1=8), 1.0, 1.0)
     s0h = A("s0h", p1=8)
     mm([(A("ps3", 320, 336), O8(b), A("s0h", b, C, 16, 0, 8)) for b in range(16)])
     mm([(A("ps6", 0, C), A("bo8", p1=8), s0h)])
     mm([(A("ps1", 0, C), O8(0), s0h)])
-    lin(A("swu", 0, 16), A("ps3", 320, 336), 1.0, MID)
-    ts(A("tmp0"), A("ps6", 0, C), -MID - 0.5, None, ALU.is_gt)
-    copy(A("h16"), A("ps1", 0, C), "va")
+    lin(A("swu", 0, 16), A("ps3", 320, 336), 1.0, -1.0)
+    act(A("al0"), A("ps6", 0, C), AF.Relu, 1.0, -1.0, accum=A("col", 4, 5))
+    ts(A("h16"), A("ps1", 0, C), A("col", 9, 10), None, ALU.add, act=(AF.Identity, A("col", 9, 10), 1.0))
     for j, (c0, c1) in enumerate(FIRST):
         nk, eq, po = A("nk", c0, c1), A("eq", c0, c1), A("ps%d" % (2 + j), 384, 384 + c1 - c0)
-        lin(nk, IND(A("nbt"), A("swu", c0 // 16, c1 // 16)), 1.0, -MID, "nk0")
+        lin(nk, IND(A("nbt"), A("swu", c0 // 16, c1 // 16)), 1.0, 1.0, "nk0")
         tt(eq, nk, A("ps6", c0, c1), ALU.is_equal, "eq0")
-        mm([(po, A("ident"), nk), (po, A("i2k"), eq)], "o0")
-        lin(A("oq", c0, c1), po, 1.0, MID + 16, "oq0")
-    tt(A("wc", 0, C), A("w0s"), A("tmp0"), ALU.mult)
-    act(A("al0"), A("tmp0"), AF.Identity, accum=A("col", 4, 5))
-    ts(A("col", 8, 9), A("col", 4, 5), -float(C), None, ALU.add)
-    for a in range(0, NT * C, 640):
-        lin(A("cnb", a, a + 640, 1, 0, 8), A("cni", a, a + 640, 1, 0, 8), 1.0, 0.0)
-    mm([(A("ps7", 0, 80), O8(b), A("cnb", b, NT * C, 16, 0, 8)) for b in range(16)])
+        mm([(po, A("ident"), nk), (po, A("i2k"), A("al0", c0, c1)), (po, A("i2k"), eq)], "o0")
+        lin(A("oq", c0, c1), po, 1.0, 15.0, "oq0")
+    lin(A("col", 8, 9), A("col", 4, 5), -1.0, 0.0)
+    for a, b in ((0, C), (C, 3 * C), (3 * C, NT * C)):
+        lin(A("cnb", a, b, 1, 0, 8), A("cni", a, b, 1, 0, 8), 1.0, 0.0)
+    for a, b in ((0, C), (C, NT * C)):
+        mm([(A("ps7", a // 16, b // 16), O8(k), A("cnb", a + k, b, 16, 0, 8)) for k in range(16)])
+    lin(A("thb", 0, 16), A("ps7", 0, 16), -90.0, 99.0)
     for t in range(NT):
         lin(A("th", 48 * t, 48 * t + 16), A("ps7", 16 * t, 16 * t + 16), 90.0, 9.0)
-    o = act(A("thb"), A("ps7", 0, 80), AF.Silu, 99.0, -90.0)
-    o["alts"]["a"] = (o["alts"]["a"][0] + 1300.0, o["alts"]["a"][1])
+    lin(A("thb", 16, 80), A("ps7", 16, 80), -90.0, 99.0)
 
     def sums(c0, c1, x0, fb, step, x):
         for a in range(c0, c1, step):
             copy(A("xx", x0 + 16 * (a - c0), x0 + 16 * (a - c0 + step)), IND(A("qt"), A("oq", a, a + step)), "va", "gx" + x)
-        mm([(fb, A("i11"), A("xx", x0 + k, x0 + 16 * (c1 - c0), 16)) for k in range(16)], "f" + x)
+        for a in range(0, c1 - c0, PIECE):
+            b = min(a + PIECE, c1 - c0)
+            mm([(cut(fb, a, b), A("i11"), A("xx", x0 + 16 * a + k, x0 + 16 * b, 16)) for k in range(16)], "f" + x)
 
     def votes(c0, c1, x0, fb, ucol, vb, x):
-        n = 16 * (c1 - c0)
         tt(A("yy", c0, c1), fb, ucol, ALU.mult, "y" + x)
-        ts(A("xx", x0 - 1, x0 - 1 + n, 16), A("yy", c0, c1), 0.5 - TWO23, TWO23 + 2048, ALU.add, ALU.add, tag="thr" + x)
-        scan(A("ee", x0, x0 + n), A("cap", 0, n), A("xx", x0 - 1, x0 - 1 + n), 2.0 ** 20, ALU.min, ALU.add, "scan" + x)
-        mm([(vb, O(k), A("ee", x0 + 1 + k, x0 + n, 16)) for k in range(15)], "V" + x)
+        ts(A("xx", x0 - 1, x0 - 1 + 16 * (c1 - c0), 16), A("yy", c0, c1), 0.5 - TWO23, TWO23 + 2048, ALU.add, ALU.add, tag="thr" + x)
+        for a in range(0, c1 - c0, PIECE):
+            n, z = 16 * min(PIECE, c1 - c0 - a), x0 + 16 * a
+            scan(A("ee", z, z + n), A("cap", 0, n), A("xx", z - 1, z - 1 + n), 2.0 ** 20, ALU.min, ALU.add, "scan" + x)
+            mm([(cut(vb, a, a + n // 16), O(k), A("ee", z + 1 + k, z + n, 16)) for k in range(15)], "V" + x)
 
     def cut(r, a, b):
         return A(r[0], r[3] + a, r[3] + b)
@@ -343,33 +356,37 @@ def build(T, rank, par=PAR):
             if t == NT - 1:
                 ts(hw, cut(ph, a - c0, b - c0), A("col", 5, 6), None, ALU.add, tag="hw" + x, act=(AF.Identity, A("col", 5, 6), 1.0))
             else:
-                copy(hw, cut(ph, a - c0, b - c0), "va", "hw" + x)
+                lin(hw, cut(ph, a - c0, b - c0), UP, 0.0, "hw" + x)
 
     def shut(nk, swu, hb, eq, po, x):
-        lin(nk, IND(A("nbt"), swu), 1.0, -MID, "nk" + x)
+        lin(nk, IND(A("nbt"), swu), 1.0, 1.0, "nk" + x)
         for b, e in zip(hb, eq):
             tt(e, nk, b, ALU.is_equal, "eq" + x)
         trip = [(po, A("ident"), nk)] + [(po, A("i2k"), e) for e in eq]
-        if x:
+        if x in "ab":
             mm(trip, "o" + x)
         else:
-            mm(trip[:-2], "o", closes=False, whole=po[0])
-            mm(trip[-2:-1], "o", opens=False, closes=False, whole=po[0])
-            mm(trip[-1:], "o", opens=False, whole=po[0])
+            mm(trip[:-1], "o" + x, closes=False, whole=po[0])
+            mm(trip[-1:], "o" + x, opens=False, whole=po[0])
 
-    def wrap(n, sw, lhs, src, out, x):
+    def wrap(n, sw, lhs, src, out, x, k0=C):
         mm([(sw, lhs, src), (sw, A("ident"), A("ramp", 0, n))], "sib" + x)
-        scan(A("kept", x and C or 0, (x and C or 0) + n), A("pick", 0, n), sw, 0.0, ALU.max, ALU.min, "sip" + x)
-        ts(out, A("kept", (x and C or 0) + 15, (x and C or 0) + n, 16), A("col", 6, 7), None, ALU.add, tag="swu" + x,
-           act=(AF.Identity, A("col", 6, 7), 1.0))
+        scan(A("kept", k0, k0 + n), A("pick", 0, n), sw, 0.0, ALU.max, ALU.min, "sip" + x)
+        back = A("col", 7, 8) if x == "a" else A("col", 6, 7)
+        ts(out, A("kept", k0 + 15, k0 + n, 16), back, None, ALU.add, tag="swu" + x, act=(AF.Identity, back, 1.0))
 
     def ahead(c0, c1, sw, hb, eq, po, runs, x):
         mv, swu = A("mv", c0, c1), A("swu", c0 // 16, c1 // 16)
-        wrap(c1 - c0, sw, A("boh"), mv, swu, x)
-        mm([(hb[-1], A("boh"), mv)], "hbl" + x)
+        if x in BYPE:
+            sw = cut(sw, 0, (c1 - c0) // 16)
+            mm([(sw, O(b), A("mv", c0 + b, c1, 16)) for b in range(16)], "sib" + x)
+            lin(swu, sw, 0.5, MID - 1, "swu" + x)
+        else:
+            wrap(c1 - c0, sw, A("boh"), mv, swu, x, c0)
+        mm([(hb[-1], A("boh"), mv), (hb[-1], A("bo64"), A("ones", 0, c1 - c0))], "hbl" + x)
         shut(A("nn", c0, c1), swu, hb, eq, po, x)
         for a, b, out in runs[::-1]:
-            copy(out, cut(po, a - c0, b - c0), "va", "pw" + x)
+            ts(out, cut(po, a - c0, b - c0), 0.0, UP, ALU.max, ALU.mult, "pw" + x, (AF.Relu, 0.0, UP))
 
     XI = 16 * (C + len(CHUNKS) + 2)
     for t in range(NT):
@@ -383,26 +400,25 @@ def build(T, rank, par=PAR):
         iota(A("mm_", 0, 7 * S), [[0, 7], [6, S]], 3 * (NONE + 2) + ID0, 0, "refill")
         iota(A("mm_", 7 * S, RC + S), [[0, RC - 6 * S]], 3 * NONE + ID0, 0, "refill")
         end = C + S if t else C
-        vb, dn, ph, po, *hb = [A("ps%d" % (2 + k // 2), CUT * (k % 2), CUT * (k % 2) + CUT) for k in range(8)]
-        vb2, dn2, ph2, po2 = [A("ps7", (C + S - CUT) * k, (C + S - CUT) * k + end - CUT) for k in range(4)]
-        hb2 = [A(b, a, a + end - CUT) for b, a in (("ps4", 384), ("ps5", 384), ("ps3", 384), ("ps0", 256), ("ps1", 256))]
-        if CUT == C:
-            hb2 = [A("ps7", 192 + S * p, 192 + S * p + S) for p in range(NT)]
-        mm([(dn, A("dm"), A("nk", 0, CUT))] + ([(dn, A("c15"), A("ones", 0, CUT))] if t else []), "dn")
-        for p in range(0 if last else t + 1):
-            mm([(hb[p], SEL(p), A("h16", 0, CUT))], "hb")
-            if CUT < C:
-                mm([(cut(hb2[p], 0, C - CUT), SEL(p), A("h16", CUT, C))], "hbb")
-        for i, (c0, c1) in enumerate(CHUNKS):
-            fb, x0 = A("ps%d" % (i % 2), c0, c1), 16 * (c0 + i + 1)
-            sums(c0, c1, x0, fb, GSTEP, "")
-            tt(A("wv", 3 * c0 + 1, 3 * c1, 3), fb, A("wc", c0, c1), ALU.mult, "w1")
-            votes(c0, c1, x0, fb, A("ub", C * t + c0, C * t + c1), cut(vb, c0, c1) if c0 < CUT else cut(vb2, c0 - CUT, c1 - CUT), "")
-        sites(t, 0, CUT, vb, dn, ph, [(0, CUT, A("h16", 0, CUT), A("hw", 0, CUT))], "")
-        if not last:
-            ahead(0, CUT, dn, hb[:t + 1] + [vb], [A("eq", C * p, C * p + CUT) for p in range(t + 2)], po,
-                  [(0, CUT, A("pw", 0, CUT))], "")
-        runs = [(CUT, C, A("h16", CUT, C), A("hw", CUT, C), A("pw", CUT, C))] if CUT < C else []
+        vb2, dn2, ph2, po2, *hb2 = [A("ps7", S * k, S * k + S) for k in range(4 + NT)]
+        for j, (h0, h1) in enumerate(PARTS):
+            w, x = h1 - h0, "cd"[j]
+            room = [4 * h0 + k * w for k in range(4)] + [4 * C + 4 * h0 + k * w for k in range(4)]
+            vb, dn, ph, po, *hb = [A("ps%d" % (2 + a // 512), a % 512, a % 512 + w) for a in room]
+            mm([(dn, A("dm"), A("nk", h0, h1)), (dn, A("c15"), A("ones", 0, w))], "dn" + x)
+            for p in range(0 if last else t + 1):
+                mm([(hb[p], SEL(p), A("h16", h0, h1))], "hb" + x)
+            for i, (c0, c1) in enumerate(CHUNKS):
+                if h0 <= c0 < h1:
+                    fb, x0 = A("ps%d" % (i % 2), c0, c1), 16 * (c0 + i + 1)
+                    sums(c0, c1, x0, fb, GSTEP, "")
+                    tt(A("wv", 3 * c0 + 1, 3 * c1, 3), fb, A("wc", c0, c1), ALU.mult, "w1")
+                    votes(c0, c1, x0, fb, A("ub", C * t + c0, C * t + c1), cut(vb, c0 - h0, c1 - h0), "")
+            sites(t, h0, h1, vb, dn, ph, [(h0, h1, A("h16", h0, h1), A("hw", h0, h1))], x)
+            if not last:
+                ahead(h0, h1, dn, hb[:t + 1] + [vb], [A("eq", C * p + h0, C * p + h1) for p in range(t + 2)], po,
+                      [(h0, h1, A("pw", h0, h1))], x)
+        runs = []
         if t > 0:
             arrive("cnt%d" % (t - 1), [A("cnt", N * (t - 1), N * t)], par["hopc"], "sc%d" % (t - 1))
             tr = []
@@ -423,7 +439,7 @@ def build(T, rank, par=PAR):
             for p in range(t + 1):
                 mm([(hb[p], SEL(p), old)], "hba")
             shut(A("nk", C, C + S), A("swa", 0, 3), hb, [A("eqa", S * p, S * p + S) for p in range(t + 1)], po, "a")
-            lin(A("oq", C, C + S), po, 1.0, MID + 16, "oqa")
+            lin(A("oq", C, C + S), po, 1.0, 15.0, "oqa")
             sums(C, C + S, XI, fb, GSTEPI, "i")
             tt(A("w1i"), fb, A("land", L0 + 1, L0 + 1 + S), ALU.mult, "w1i")
             copy(IND(A("wv"), HW), A("w1i"), tag="scw")
@@ -432,15 +448,15 @@ def build(T, rank, par=PAR):
             votes(C, C + S, XI, fb, A("uin"), cut(vb2, C - CUT, C + S - CUT), "i")
             runs.append((C, C + S, old, A("hwi"), A("pwi")))
         if runs:
-            mm([(dn2, A("dm"), A("nk", CUT, end))] + ([(cut(dn2, 0, C - CUT), A("c15"), A("ones", 0, C - CUT))] if t and CUT < C else []), "dnb")
+            mm([(dn2, A("dm"), A("nk", CUT, end)), (dn2, A("c15"), A("ones", 0, end - CUT))], "dnb")
             sites(t, CUT, end, vb2, dn2, ph2, [r[:4] for r in runs], "b")
         if t > 0:
-            copy(IND(A("hw"), HL), A("hwi"), tag="sch")
+            copy(IND(A("hw"), HL), A("hwi"), "v" if last else "va", "sch")
         if runs and not last:
             ahead(CUT, end, dn2, hb2[:t + 1] + [vb2],
                   [A("eqb", 112 * p, 112 * p + end - CUT) for p in range(t + 2)], po2, [r[:2] + r[4:] for r in runs], "b")
             if t > 0:
-                copy(IND(A("pw"), HL), A("pwi"), tag="sco")
+                copy(IND(A("pw"), HL), A("pwi"), "va", "sco")
         W1 = A("wv", 1, 3 * C, 3)
         ts(A("fl", 2 * C, 3 * C), W1, A("lh", 8 + t, 9 + t), None, ALU.is_gt, tag="ch")
         ts(A("fl", 0, C), W1, A("lh", t, t + 1), None, ALU.is_lt, tag="cl")
@@ -474,10 +490,13 @@ def build(T, rank, par=PAR):
         scan(A("ra"), A("pick", 0, S), A("mm_", RC, RC + S), 0.0, ALU.max, ALU.min, "ra")
         lin(A("osu", 0, 3), A("ra", 15, S, 16), 1.0 / 3, -ID0 / 3, "osu")
         lin(A("osu", 4, 7), A("ra", 15, S, 16), 1.0, -float(ID0), "osw")
-        copy(A("payh", S * t, S * t + S), IND(A("hw"), A("osu", 0, 3)), "va", "payh")
+        lin(A("payh", S * t, S * t + S), IND(A("hw"), A("osu", 0, 3)), 1.0 if last else 1 / UP, 0.0, "payh")
         copy(A("pay", P0 + 112, P0 + PAYP), IND(A("wv"), A("osu", 4, 7)), "va", "payw")
-        send("sh", t, [A("payh", S * t, S * t + S)])
-        send("sp", t, [A("pay", P0 + 111, P0 + PAYP)])
+        if last:
+            send("sf", t, [A("payh", S * t, S * t + 2 * PAYN), A("pay", P0 + 111, P0 + PAYP)])
+        else:
+            send("sh", t, [A("payh", S * t, S * t + S)])
+            send("sp", t, [A("pay", P0 + 111, P0 + PAYP)])
         copy(A("gb"), IND(A("mm_"), A("of2", 16, 35)), "va", "gb")
         mm([(A("ps6", 224, 243), O(b), A("gb", b, S + C, 16)) for b in range(16)] + [(A("ps6", 240, 243), A("bo"), A("ones", 0, 3))], "rb")
         lin(A("oh", H0, H0 + 19), A("ps6", 224, 243), 1.0 / 48, -(ID0 + 1) / 3, "oh")
@@ -486,14 +505,14 @@ def build(T, rank, par=PAR):
             copy(A("h32", 0, C), IND(A("hw"), A("oh", H0, H0 + 16)), "va", "h32")
         else:
             for c0, c1 in FIRST:
-                lin(A("oq", c0, c1), IND(A("pw"), A("oh", H0 + c0 // 16, H0 + c1 // 16)), 1.0, MID + 16, "oq")
-            ts(A("nk", 0, C), A("oq", 0, C), -15.0, 0.0, ALU.add, ALU.max, "nkg", (AF.Relu, -15.0, 1.0))
-            copy(A("h16"), IND(A("hw"), A("oh", H0, H0 + 16)), "va", "h16")
+                lin(A("oq", c0, c1), IND(A("pw"), A("oh", H0 + c0 // 16, H0 + c1 // 16)), 1 / UP, 15.0, "oq")
+            lin(A("nk", 0, C), A("oq", 0, C), 1.0, -15.0, "nkg")
+            lin(A("h16"), IND(A("hw"), A("oh", H0, H0 + 16)), 1 / UP, 0.0, "h16")
         copy(A("wc", 0, C), IND(A("wv"), A("owu", H0, H0 + 16)), "va", "wc")
     L0, HL = (NT - 1) * PAYW, A("oh", H0 + 16, H0 + 19)
     step[0] = NT
-    arrive("arh%d" % (NT - 1), [A("landh", S * (NT - 1), S * NT)], par["hop"], "sh%d" % (NT - 1))
-    arrive("arr%d" % (NT - 1), [A("land", L0, L0 + PAYW)], par["hop"], "sp%d" % (NT - 1))
+    arrive("arh%d" % (NT - 1), [A("landh", S * (NT - 1), S * NT)], par["hop"], "sf%d" % (NT - 1))
+    arrive("arr%d" % (NT - 1), [A("land", L0, L0 + PAYW)], par["hop"], "sf%d" % (NT - 1))
     copy(IND(A("h32"), HL), A("landh", S * (NT - 1), S * NT), tag="endh")
     copy(IND(A("wc"), HL), A("land", L0 + 1, L0 + 1 + S), tag="endw")
     store("yh", "h32", "a", "outh")
@@ -637,7 +656,7 @@ def plan(par=PAR, who=WHO, when=WHEN, ops=None):
     key = [max(o["step"], 0) * PERIOD + when.get(o["name"], -PERIOD) for o in ops]
     for i, o in enumerate(ops):
         for j in o["near"] + ([] if o["behind"] is None else [o["behind"]]):
-            key[i] = max(key[i], key[j] + 0.02)
+            key[i] = max(key[i], key[j] + 1e-5)
     return sorted(range(len(ops)), key=lambda i: (key[i], i)), choose(ops, who)
 
 
@@ -662,13 +681,15 @@ def ways(T, topo, core):
 
 def slots(kind, t, r):
     if kind == "sh":
-        return "payh", "landh", t * S, t * S, S, "arh%d" % t
+        return "payh", "landh", t * S, t * S, S if t < NT - 1 else 2 * PAYN, "arh%d" % t
     if kind == "sp":
         return "pay", "land", t * PAYP + 111, t * PAYW, PAYN, "arr%d" % t
     return "dcol", "cnt", 8 * t, N * t + r, 1, "cnt%d" % t
 
 
 def messages(T, r, what):
+    if what[0] == "sf":
+        return messages(T, r, ("sh", what[1])) + messages(T, r, ("sp", what[1]))
     a, b, c0, d0, w, sem = slots(what[0], what[1], r)
     to = [d for d in range(N) if d != r] if what[0] == "sc" else [(r + 1) % N]
     return [(d, T[a][:, c0:c0 + w], lambda U: U[b][:, d0:d0 + w], sem) for d in to]
@@ -683,11 +704,10 @@ def dst(topo, d, s):
     return DstId(rid=rid, pnc=pid)
 
 
-def lanes(T, topo, owner):
-    nxt, relay, direct, share = ways(T, topo, owner)
-    off = topo.engines(owner, direct[0])
-    on = [e for e in topo.engines(owner, relay[0]) if e not in off]
-    return {"sh": off, "sp": on, "sc": on}
+def lanes(T, topo, owner, kind, t):
+    every = topo.engines(owner, ways(T, topo, owner)[1][0])
+    half = len(every) // 2
+    return every if t < NT - 1 else every[:half] if kind == "sh" else every[half:]
 
 
 def write(g, T, topo, core, to, src, piece, sem, engines):
@@ -714,7 +734,8 @@ def hand_on(g, core, T, topo):
         sent = 0
         for t in range(steps):
             _, b, _, d0, w, sem = slots(kind, t, T.rank_of(owner))
-            g.wait_ge(T.sem[sem], len(lanes(T, topo, owner)[kind]))
+            g.wait_ge(T.sem[sem], len(lanes(T, topo, owner, kind, t)))
+            w = S if kind == "sh" else w
             sent += write(g, T, topo, core, to, T[b][:, d0:d0 + w], T[b][:, d0:d0 + w], T.sem[sem], topo.engines(core, to[0]))
         g.wait_ge(T.sem.loc, sent)
 
@@ -726,7 +747,6 @@ def rank_program(g, core, T, topo):
         return
     nxt, relay, direct, share = ways(T, topo, core)
     first = {"sh": [relay[0]], "sp": [relay[1]], "sc": list(share)}
-    mine = lanes(T, topo, core)
     n_arr = len(topo.engines(ways(T, topo, T.cores[(rank - 1) % N])[1][0], core))
     n_cnt = 0
     for o in T.cores:
@@ -769,9 +789,18 @@ def rank_program(g, core, T, topo):
             Q[e].wait_ge(T.sem[s], v)
         o["knew"] = dict(seen[e])
         f = o["alts"][e][1]
-        if "remote" in o:
+        if "remote" in o and f[0] == "sf":
+            both = []
+            for kind in ("sh", "sp"):
+                a, b, c0, d0, w, sem = slots(kind, f[1], rank)
+                mine = lanes(T, topo, core, kind, f[1])
+                both.append(RemoteDMATransfer(dst_ids=[dst(topo, first[kind][0], core)], dma_engine_mask=bits(mine), remote_sem=T.sem[sem],
+                                              src=T[a][:, c0:c0 + w], dst=T[b][:, d0:d0 + w]))
+                sent += len(mine)
+            g.remote_dma_fused(both, local_sem=T.sem.loc)
+        elif "remote" in o:
             a, b, c0, d0, w, sem = slots(f[0], f[1], rank)
-            sent += write(g, T, topo, core, first[f[0]], T[a][:, c0:c0 + w], T[b][:, d0:d0 + w], T.sem[sem], mine[f[0]])
+            sent += write(g, T, topo, core, first[f[0]], T[a][:, c0:c0 + w], T[b][:, d0:d0 + w], T.sem[sem], lanes(T, topo, core, f[0], f[1]))
         elif "done" in o:
             f(Q[e])
         else:

from concourse.bass import DstId, RemoteDMATransfer
from concourse.mybir import AluOpType, ActivationFunctionType

ALU = AluOpType
AF = ActivationFunctionType
N, V, C, NT, S, DG = 8, 2048, 256, 5, 48, 5
NONE = C
WN = C + 2 * S + 16
PAYN, PAYW, PAYP = S + 1, S + 4, S + 112
CUT = 256
MID = 1024.0
UP = 32.0
BASE = 786432.0
TWO23 = 8388608.0
ID0 = 32
RH, RC, RD, RI, MW = 0, 593, 864, 1120, 1888

CHUNKS = [(0, 128), (128, 256)]
PIECE = 64
PARTS = [(0, 128), (128, 256)]
BYPE = ""
FIRST = [(0, 128), (128, 256)]
GSTEP, GSTEPI = 32, 24
XW = 16 * (C + S + 8)

F32, BF, F16, I32, U16 = "float32", "bfloat16", "float16", "int32", "uint16"
_SB = {
    "nbt": (V, I32), "qt": (V + 16, BF), "lh": (16, F32), "s0i": (C, I32), "usi": (C, I32),
    "cni": (NT * C, I32), "s0h": (C, F16), "usb": (C, BF), "cnb": (NT * C, BF), "ub": (NT * C + WN - C, F32),
    "ones": (640, BF), "ident": (128, BF), "bo": (128, BF), "bo1": (128, BF), "nbo": (128, BF), "boh": (128, BF), "bo64": (128, BF), "l2a": (128, BF), "l2": (128, BF),
    "dma_": (128, BF), "dmb": (128, BF), "dm": (128, BF), "c15": (128, BF), "jj": (256, BF), "z8": (144, BF), "bo8a": (128, BF), "bo8": (128, BF),
    "zt": (640, BF), "zz": (144, BF), "zzh": (144, BF), "i11": (128, BF), "i2k": (128, BF), "ip": (128, BF), "im": (128, BF), "sel": (640, BF),
    "mki": (C, I32), "mki2": (C, I32), "pik1": (C, BF), "pick": (C, BF), "ramp": (C, BF), "kept": (C + 112, F32), "ids": (C, F32), "pci": (8, I32),
    "pci2": (8, I32), "cc": (112, F16), "cwi": (16, F32), "cw": (16, F32), "rs32": (84, BF), "rsx": (128, F32),
    "th": (NT * 48, F32), "thb": (NT * 16, F32), "cap": (2048, BF),
    "oq": (C + S, U16), "xx": (XW, F16), "ee": (XW, BF), "yy": (C + S, F32),
    "wc": (WN, F32), "wv": (3 * WN, F32), "w1i": (S, F32), "h32": (WN, F32), "h16": (C, F16), "hw": (WN, F32), "pw": (WN, F32),
    "fl": (3 * C, BF), "fw": (84, BF), "dbl": (16, BF), "sc": (84, BF), "of2": (40, U16),
    "mm_": (MW, F32), "gb": (C + S, F16), "ra": (S, F16), "osu": (8, U16), "oh": (40, U16),
    "owu": (40, U16), "sg": (C + S, BF), "mv": (C + S, F16),
    "hwi": (S, F32), "pwi": (S, F32), "swu": (20, U16), "swa": (4, U16), "nk": (C + S, F16), "nn": (C + S, F16),
    "eq": (5 * C, BF), "eqb": (5 * 112, BF), "eqa": (5 * S, BF), "uin": (S, F32),
    "al0": (C, BF), "col": (32, F32), "dcol": (8 * NT, BF),
    "pay": (NT * PAYP, F32), "land": (NT * PAYW, F32), "payh": (NT * S + 56, F16), "landh": (NT * S + 56, F16), "cnt": (NT * N, BF),
}
SCRATCH = {k: ("sbuf", [128, w], d) for k, (w, d) in _SB.items()}
for _b in range(8):
    SCRATCH["ps%d" % _b] = ("psum", [128, 512], F32)
_LOADS = ["s0", "nb", "qs", "w0", "us", "coin", "lo", "hi"]
SEMAPHORES = (["ev", "ea", "ep", "eg", "loc", "outw", "outh"] + ["ld_" + x for x in _LOADS]
              + ["arr%d" % t for t in range(NT)] + ["arh%d" % t for t in range(NT)] + ["cnt%d" % t for t in range(NT - 1)])
ESEM = {"v": "ev", "a": "ea", "p": "ep", "g": "eg"}

PAR = dict(cy=0.88, pcy=0.46, gr=1.56, scr=3.8, hop=3400.0, hopc=4700.0, fa=90.0, fv=25.0, fp=60.0, call=700.0, lat=130.0,
           nb=4500.0, qs=5800.0)
MIX = 0.5
WHO = ['boh', 'e', 'gx', 'gx.3', 'gxi', 'i2k', 'nk0.1', 'nka', 'nki', 'of2', 'oq', 'oq.1', 'oq0', 'oqa', 'osu', 'owu', 'payw', 'pw', 'pwi', 'sel.2', 'swa', 'swui', 'th.1', 'th.2', 'th.3', 'th.4', 'thb', 'ub.3', 'ub.5', 'usb', 'wc', 'zr', 'zr.1', 'zr.3', 'zzh']
PERIOD = 14.0
WHO = '+boh +col.2 +h16 +i11 +i2k +im +ip +nbo +oq0 +pick +sel.4 +th.5 +ub.1 +ub.3 +zzh 0gb 0gx.1 0gx.3 0gx.5 0gx.7 0oq 0payh 0pw 0scat 0swu gx.1 gx.3 gx.5 gx.7 gxi hw hwb of2 oq osu payh payw pw pwb'.split()
TURNS = '+pci@-13.176 +cwi@-12.111 +mki@-12.083 +ones@-11.384 +bo1@-9.603 +z8@-9.104 +ident@-9.003 +pci2@-8.345 +th@-8.304 +cc@-8.233 +fw@-8.145 +rs32@-8.122 +zz@-7.893 +bo8a@-7.775 +cap@-7.705 +ldcoin@-7.697 +cap.1@-7.653 +ldus@-7.372 +lds0@-7.271 +rsx@-7.241 +qt@-7.236 +mki2@-6.725 +col.1@-6.715 +cc.6@-6.56 +pw@-6.506 +rsx.1@-6.453 +lh@-6.326 +cw@-6.215 +col@-6.163 +im@-6.075 +col.3@-5.814 +hw@-5.764 +i11@-5.735 +rs32.1@-5.724 +ldnb@-5.717 +tmp0@-5.583 +zz.1@-5.459 +bo@-5.435 +ps1@-5.334 +s0h@-5.3 +i2k@-5.295 +zzh@-5.285 +usb@-5.208 +cc.5@-5.164 +cnb@-5.138 +wv@-4.983 +bo8@-4.982 +cnb.1@-4.931 +ps6@-4.656 +zt@-4.519 +ps3@-4.343 0refill.1@-4.319 +ps7@-4.116 +pik1@-4.002 +cc.4@-3.992 +sel@-3.768 +ps2@-3.682 +ldqs@-3.588 +ramp@-3.479 +swu@-2.328 +mm_@-2.305 +ldw0@-2.282 +al0@-2.24 +nk0.1@-2.23 +nk0@-2.221 +nbo@-1.752 +col.2@-1.742 +boh@-1.706 +th.1@-1.625 +cc.1@-1.189 +h16@-1.179 +thb@-1.123 +ip@-1.112 +dmb@-0.916 +pick@-0.855 +cc.3@-0.735 0refill@-0.712 +col.4@-0.707 +dma_@-0.647 +dm@-0.533 +cc.2@-0.512 +eq0.1@-0.255 +eq0@-0.225 +mm_.1@-0.205 +ub.1@-0.135 +oq0@-0.11 +wc.1@0.09 0gx@0.216 +l2a@0.239 +o0@0.273 refill@0.705 +ldlo@0.805 +c15@0.986 +ps4.1@1.027 0gx.1@1.028 +l2@1.06 +o0.1@1.127 0y@1.13 gx.3@1.182 0y.1@1.236 0gx.5@1.246 0gx.3@1.256 +oq0.1@1.267 gx.1@1.308 0w1.1@1.357 gx.7@1.372 hb.1@1.377 0f@1.492 0gx.2@1.524 0gx.7@1.557 0f.1@1.816 y@1.892 0thr@1.939 +col.7@1.949 0gx.4@2.076 hb.2@2.143 hb@2.17 +ids@2.428 hb.3@2.466 gx@2.536 gx.2@2.573 f@2.587 0V@2.764 0gx.6@2.823 f.1@2.826 scan@2.851 0y.2@2.874 0f.2@2.874 +ps5@2.881 0w1@2.884 +th.2@2.942 hba@2.965 siba@2.975 gx.4@3.087 0f.3@3.099 hba.3@3.139 hba.4@3.199 gx.6@3.237 0dn@3.248 gx.5@3.289 hba.2@3.339 hba.1@3.349 swua@3.416 0w1.2@3.421 0scan@3.429 y.1@3.431 thr.1@3.431 thr@3.441 sipa@3.441 tot@3.45 0al@3.535 f.2@3.553 eqa.3@3.847 nka@3.852 up@3.857 0w1.3@3.881 0y.3@3.891 eqa.1@3.907 +jj@3.952 uin@4.049 0fw@4.087 0thr.2@4.194 endh@4.219 refill.1@4.427 eqa.2@4.484 eqa.4@4.494 +ldhi@4.496 0ch@4.516 0scan.1@4.516 0thr.1@4.526 0cl@4.536 +sel.3@4.573 oa@4.671 f.3@4.681 eqa@4.684 0scan.2@4.687 w1@4.816 lh@4.84 0pw3@4.928 0dbl@5.02 oqa@5.139 y.2@5.245 scan.1@5.255 w1.3@5.255 dn@5.265 gxi@5.322 V@5.421 0hole@5.432 w1.2@5.445 thr.2@5.455 +sel.1@5.492 endw@5.55 0V.1@5.643 +ps5.1@5.653 0px@5.659 0thr.3@5.695 y.3@5.746 gxi.1@5.927 w1.1@5.946 w1i@5.946 scan.2@5.956 0sc@6.016 +sel.2@6.079 +th.3@6.159 0rr@6.294 fi@6.298 0scan.3@6.304 yi@6.308 0px0@6.421 dnb@6.442 scan.3@6.463 thr.3@6.47 scw@6.473 cl@6.48 ch@6.503 +th.4@6.534 V.1@6.549 al@6.617 +h32@6.636 V.2@6.708 scani@6.75 twice@6.755 0twice@6.834 0V.2@6.864 0scat@6.951 0of2@7.061 0rrb@7.071 styw@7.075 0mv@7.105 half@7.138 V.3@7.178 Vi@7.226 0V.3@7.243 0pxb@7.285 0osw@7.312 pw3@7.426 0half@7.488 0ge@7.498 sib@7.567 styh@7.709 0of2b@7.769 +ub.5@7.779 ge@7.869 thri@8.127 mv@8.393 px0@8.403 0ra@8.407 0d@8.605 0gb@8.606 +ub.2@8.648 rrb@8.848 fw@8.862 px@8.939 db@9.055 dbl@9.274 mvb@9.29 hole@9.309 +ps4@9.384 sc@9.401 nk@9.423 sip@9.44 0osu@9.47 geb@9.522 sipb@9.533 0sib@9.569 swu@9.584 rr@9.592 scat@9.594 0hw@9.624 0sip@9.627 0hnew@9.671 0hb@9.712 +col.5@9.726 0swu@9.806 of2@9.896 0>sc@9.924 d@9.948 hnew@10.061 hw@10.084 0rb@10.154 sibb@10.234 0hbl@10.492 pxb@10.526 eq@10.548 eq.1@10.576 0o.1@10.598 +c15.1@10.731 of2b@10.752 hnewb@10.817 +ub.3@10.829 0>sh@10.836 0payh@10.908 hblb@10.928 0o@10.969 0nk@11.014 hbl@11.09 swub@11.111 o@11.156 eq.2@11.166 sch@11.2 osu@11.215 o.2@11.311 ob@11.311 o.1@11.381 hwb@11.395 eq.3@11.398 ra@11.4 >sc@11.672 gb@11.721 +ub@11.809 rb@11.911 eq.4@12.051 0eq@12.192 eqb@12.33 payh@12.34 nkb@12.566 eqb.2@12.576 eqb.3@12.576 0eq.1@12.698 osw@12.79 eqb.1@12.957 owu@13.006 eqb.4@13.04 0owu@13.718 pw@13.779 h32@13.873 pwb@13.877 0oq@13.908 oh@13.95 >sh@14.052 +ub.4@14.11 0wc@14.199 0oh@14.355 0o.2@14.475 +sel.4@14.636 sco@14.731 >sp@14.739 +th.5@14.78 payw@14.88 oq@15.362 wc@15.402 +wc@15.619 h16@15.849 oq.1@15.882 0payw@15.984 0h16@16.006 +col.6@16.007 0oq.1@16.061 0pw@16.232 0nkg@17.376 nkg@19.029 0>sp@19.9'
TURNS = "^0payh ^0osw +jj +col.5 ^0payw ^hwb* ^0eqc ^0eqc.1 ^ra ^od.1 +mm_.1 ^>sc +cap.2 ^0eqd.1 ^0rb +swu ^0eqd ^wc ^nkb* ^payh ^4ra ^sch* ^od ^pwd +nk0 0refill.1 ^eqb.1 ^eqb.3 ^0oc +ps2 ^rb _+pw ^+th.2* ^+thb.1* +ub.1 ^0oh ^0owu +cc.4 ^eqb.2 +h16* ^eqb +dma_ ^0>sh ^0oc.1 ^0od ^+ub.5* ^eqb.4 +eq0 +col.9 ^pwc ^0od.1 +nk0.1 ^4osw* +ps4 ^0h16 ^osw* ^4sch* ^payw +o0 ^ob ^+sel.2* _+ident +o0.1 ^h16 ^0wc +cc.3 +zz.1 ^0pwc* +mki2 ^owu* +ps7 +c15.1 +ldqs ^4scat _+cwi +ps4.1 ^oq.1* 4refill _+bo8a +col.6 ^+th.4* 0gx.4 hbc 4f ^0pwd* hbd.3 ^4payw* ^4osu ^oq* 4gx.3* ^sco* ^oh* gx.3* ^pwb* +col.7 4gx.1* +eq0.1 hbd.2 hbc.2 4gx.7* 4dnc ^0oq.1 0gx.2 hbd gx.2 dnd gx.1 0gx hbc.1 hbd.1 +oq0 f 4f.1 4gx.2 ^>sp _+lh f.1 4y +col ^>sf +pik1 ^+th.3* gx* ^0>sp 4gx ^nkg 4dnd 4hba.1 0f 4gx.4* +ps5 4siba 4hba.3 0gx.5 ^0oq* ^4payh 4f.2 +ps5.1 ^4rb hba.1 4sipa hba.3 0gx.1* 4f.3 _+hw f.2 4gx.6 0gx.6 4thr siba +col.3* 4hba.4 4w1 gx.4* +oq0.1* 0gx.3* 4hba.2 4eqa 4scan +dm 4uin 4hba 4gx.5 hba f.3 4tot gx.5 +dmb 0y gx.7* y sipa thr w1 ^4gb* ^^styh hba.2 gx.6 nka +ub.4 4eqa.1 ^+ub.3 eqa scan 4refill.1 ^4oh* +ldw0 +l2a swua ^^endw ^^endh +pick* +fw +thb hbc.3 0gx.7* 0f.1 0w1 4eqa.4 0f.2 4swua 4nka 4eqa.2 _+i2k* 0dnc 0thr 4eqa.3 4oa refill.1 tot eqa.2 4scan.1 eqa.3 eqa.1 4V.1 _+bo1 _+z8 4y.1 0f.3 ^4h32 y.1 scan.1 w1i +zzh 0scan 4gxi* gxi* 4w1.1 thr.1 w1.1 ^0nkg oa +ub.2 0scan.1 4V 0V uin 4thr.1 oqa ^+th.5 V +th.1* scan.3 0w1.1 fi V.1 +im _+ldnb +mm_ scan.2 4oqa dnc +ldlo 4gxi.1 _~+ones gxi.1 4scan.3 4w1i 4scan.2 4fi 0y.1 up mvc scw V.3 0cl 0ch 0V.1 0al V.2 +ldhi sibd 0pw3 4scani 4up 4half hblc 0thr.1 ^4owu* _+ldcoin pw3 gec yi hnewc sibc 4gec ch cl lh _+cc 0V.2 0dnd al ^4wc _+qt swuc 4dbl _~+ldus ged +cc.2 0px0 _+ip +ids 0scan.2 4lh ^^styw 4V.3 thri +col.2 4al 0fw Vi 4scw 4yi +l2 px0 +boh* twice 4V.2 +ramp 4cl 4ch px 4thri mvd half 0hole scani sipc refill _+c15 db _+pci2 _+rs32 4mvc fw 0hbd 0V.3 4fw 0dbl 4twice 0px 4pw3 _+bo 0sc eqc.4 _+cc.5 dbl 0mvc 0half _+bo8 hole _+cap.1 sipd 4ged 0scat sc 4Vi +sel 0scan.3 +sel.1 ^+ub +cnb.2 _+s0h* 0refill 0gec _+zz hwc* 0rr nkc _~+lds0 eqc.2 +sel.4* eqc.3 _+zt rr 0twice* _+i11 _+bo64 0hnewd +sel.3 swud geb 4hole dnb +cnb.1 4px0 0ged +h32 4sc _+rs32.1 hbld 0pxb 0of2* pxb 0sibc 0hnewc _+cc.6 _+wv 0>sc 0osu +wc eqc.1 0rrb 4mvd 0hbc 0sibd 0mvd +ps7.1 eqd.3 +col.8 _~+pci 4geb _+nbo 0gb 0sipc _+rsx.1 _+usb sibb 0swuc 0of2b* hblb eqd.2 mvb _+th 0d _+ps6 0hwc* 4rr 0nkd 4px 0sipd 4mvb 4hnewc 0hblc _+cc.1 _+col.4 _+col.1 4dnb hnewb 0hwd* nkd eqd.1 _+ps3 0ra 4hnewd 0swud* 4of2 rrb eqc of2 scat 0nkc* 0hbld +payh swub eqd _+cnb sipb _+ps1 hnewd oc.1 _+mki osu _+al0 oc 4hwc* 4hwd* 4pxb gb of2b* _+cw _+cap 4hnewb eqd.4 hwd* d >sh _~+rsx 4rrb 4hwb* 4of2b*".split()
WHO = [x.strip("^*").lstrip("_~") for x in TURNS if x[-1] == "*"]
WHEN = {x.strip("^*").lstrip("_~"): PERIOD * (x.count("^") - len(x) + len(x.lstrip("_~")) + i / len(TURNS)) for i, x in enumerate(TURNS)}


def A(name, c0=0, c1=None, st=1, p0=0, p1=128):
    if c1 is None:
        c1 = _SB[name][0] if name in _SB else 512
    return (name, p0, p1, c0, c1, st)


def nel(r):
    return 16 * nel(r[2]) if r[0] == "#" else len(range(r[3], r[4], r[5]))


def IND(win, off):
    return ("#", win, off)


def wide(r):
    r = r[1] if r[0] == "#" else r
    return r[0] not in _SB or _SB[r[0]][1] in (F32, I32)


def parts(r):
    if not isinstance(r, tuple):
        return []
    return [r[1], r[2]] if r[0] == "#" else [r]


def build(T, rank, par=PAR):
    CY, PCY, GR, SCR = par["cy"], par["pcy"], par["gr"], par["scr"]
    ops, nth, step = [], {}, [-1]

    def ap(r):
        if not isinstance(r, tuple):
            return r
        if r[0] == "#":
            return ap(r[1]).indirect(ap(r[2]))
        if r[5] == 1:
            return T[r[0]][r[1]:r[2], r[3]:r[4]]
        return T[r[0]][r[1]:r[2], r[3]:r[4]:r[5]]

    def add(alts, reads, writes, tag="", **kw):
        rd = [x for r in reads for x in parts(r)]
        wr = []
        for r in writes:
            if r[0] == "#":
                wr.append(r[1]); rd.append(r[2])
            else:
                wr.append(r)
        tag = tag or wr[0][0]
        k = nth[tag] = nth.get(tag, -1) + 1
        o = dict(alts=alts, rd=rd, wr=wr, tag=tag, name={-1: "+", 0: "0", NT - 1: "4"}.get(step[0], "") + tag + ("." + str(k) if k else ""), step=step[0], eng=None)
        o.update(kw)
        ops.append(o)
        return o

    def vcost(out, ins, two=False):
        if out[0] == "#":
            return 50 + nel(out) * SCR * CY
        if ins and ins[0][0] == "#":
            return 50 + nel(out) * GR * CY
        n = nel(out)
        rate = 1.0 if any(wide(r) for r in [out] + ins) else 0.5
        if two and all(r[0] in _SB for r in ins):
            rate *= 2
        return par["fv"] + max(64, n * rate) * CY

    def acost(out, in_):
        if out[0] == "#":
            return 65 + nel(out) * SCR * CY
        return 65 + nel(out) * GR * CY if in_[0] == "#" else par["fa"] + nel(out) * CY

    def copy(out, in_, eng="v", tag=""):
        alts = {}
        if "v" in eng:
            alts["v"] = (vcost(out, [in_]), lambda q: q.tensor_copy(ap(out), ap(in_)))
        if "a" in eng:
            alts["a"] = (acost(out, in_), lambda q: q.activation(ap(out), ap(in_), AF.Silu if out[0] == "#" else AF.Identity))
        return add(alts, [in_], [out], tag)

    def ts(out, in0, s1, s2, op0, op1=None, tag="", act=None):
        if op1 is None:
            f = lambda q: q.tensor_scalar(ap(out), ap(in0), ap(s1), None, op0)
        else:
            f = lambda q: q.tensor_scalar(ap(out), ap(in0), ap(s1), ap(s2), op0, op1)
        alts = {"v": (vcost(out, [in0]), f)}
        if act is not None:
            alts["a"] = (acost(out, in0), lambda q: q.activation(ap(out), ap(in0), act[0], bias=ap(act[1]), scale=ap(act[2])))
        return add(alts, [in0, s1, s2], [out], tag)

    def lin(out, in0, scale, bias, tag=""):
        return ts(out, in0, scale, bias, ALU.mult, ALU.add, tag, (AF.Identity, bias, scale))

    def tt(out, in0, in1, op, tag=""):
        return add({"v": (vcost(out, [in0, in1], True), lambda q: q.tensor_tensor(ap(out), ap(in0), ap(in1), op))}, [in0, in1], [out], tag)

    def scan(out, d0, d1, init, op0, op1, tag=""):
        return add({"v": (vcost(out, [d0, d1]), lambda q: q.tensor_tensor_scan(ap(out), ap(d0), ap(d1), init, op0, op1))}, [d0, d1], [out], tag)

    def memset(out, val, tag=""):
        return add({"v": (vcost(out, []), lambda q: q.memset(ap(out), val))}, [], [out], tag)

    def act(out, in_, func, bias=0.0, scale=1.0, accum=None, tag=""):
        if accum is None:
            f = lambda q: q.activation(ap(out), ap(in_), func, bias=ap(bias), scale=ap(scale))
        else:
            f = lambda q: q.activation(ap(out), ap(in_), func, bias=ap(bias), scale=ap(scale), accum_out=ap(accum))
        return add({"a": (acost(out, in_), f)}, [in_, bias, scale], [out] + ([accum] if accum else []), tag)

    def mm(trip, tag="", opens=True, closes=True, whole=None):
        def f(q):
            r = None
            for i, (o, l, x) in enumerate(trip):
                r = q.matmul(ap(o), ap(l), ap(x), opens and i == 0, closes and i == len(trip) - 1)
            return r
        cost = par["fp"] + sum(max(64, nel(x)) * (4 if wide(x) else 1) * PCY for _, _, x in trip)
        return add({"p": (cost, f)}, [r for tr in trip for r in tr[1:]], [tr[0] for tr in trip] + ([A(whole)] if whole else []), tag)

    def iota(out, pat, base, cm, tag=""):
        if _SB[out[0]][1] == I32:
            f = lambda q: q.iota(ap(out), pat, base, cm)
        else:
            f = lambda q: q.iota(ap(out), pat, base, cm, allow_small_or_imprecise_dtypes=True)
        return add({"g": (130 + 2 * CY * nel(out), f)}, [], [out], tag)

    def sel(out, in_, pat, cmp_, fill, base, cm, tag=""):
        return add({"g": (170 + 2 * CY * nel(out), lambda q: q.affine_select(ap(out), ap(in_), pat, cmp_, fill, base, cm))}, [in_], [out], tag)

    def send(kind, t, reads):
        return add({"g": (par["call"], (kind, t))}, reads, [], "%s%d" % (kind, t), remote=True, name=(">" if t else "0>") + kind)

    def arrive(sem, writes, lat, after):
        return add({}, [], writes, sem, done=(sem, None), lat=lat, after=after)

    rot = (-DG * rank) % 8

    def pieces(rows):
        if rot == 0:
            return [(0, 0, 8 * rows)]
        return [(0, rot * rows, (8 - rot) * rows), ((8 - rot) * rows, 0, rot * rows)]

    def load(name, buf, c0, c1, rows_h, rows_c, q, lat):
        ph, pc = pieces(rows_h), pieces(rows_c)

        def f(e):
            for (h0, _, hn), (_, s0, sn) in zip(ph, pc):
                e.dma_start(T[buf][s0:s0 + sn, c0:c1], T[name][h0:h0 + hn, :]).then_inc(T.sem["ld_" + name], 16)
        return add({q: (60.0 * len(ph), f)}, [], [A(buf, c0, c1)], "ld" + name, done=("ld_" + name, 16 * len(ph)), lat=lat)

    def store(name, buf, q, sem):
        def f(e):
            for h0, s0, n in pieces(16):
                e.dma_start(T[name][h0:h0 + n, :], T[buf][s0:s0 + n, 0:C]).then_inc(T.sem[sem], 16)
        return add({q: (120.0, f)}, [A(buf, 0, C)], [], "st" + name, done=(sem, 16 * len(pieces(16))), lat=2200.0)

    def O(b, name="zz"):
        return A(name, 15 - b, 143 - b)

    def O8(b):
        return A("z8", 15 - b, 143 - b, 1, 0, 8)

    def SEL(p):
        return A("sel", 128 * p, 128 * p + 128)

    load("nb", "nbt", 0, V, 16, 16, "s", par["nb"])
    load("s0", "s0i", 0, C, 1, 1, "a", 2000.0)
    load("us", "usi", 0, C, 1, NT, "a", 2200.0)
    load("qs", "qt", 16, V + 16, 16, 16, "s", par["qs"])["after"] = "ldnb"
    load("w0", "wc", 0, C, 16, 16, "s", par["qs"])["after"] = "ldqs"
    load("coin", "cni", 0, NT * C, 1, 1, "a", 2500.0)
    memset(A("lh"), 0.0)
    load("lo", "lh", 0, NT, 16, 16, "s", par["qs"])["after"] = "ldw0"
    load("hi", "lh", 8, 8 + NT, 16, 16, "s", par["qs"])["after"] = "ldlo"
    memset(A("ones"), 1.0)
    memset(A("qt", 0, 16), 0.0)
    sel(A("z8", p1=8), A("ones", 0, 144, p1=8), [[1, 144]], ALU.is_equal, 0.0, -15, -16)
    sel(A("bo8a", p1=8), A("ones", 0, 128, p1=8), [[1, 128]], ALU.is_ge, 0.0, 0, -16)
    sel(A("bo8", p1=8), A("bo8a", p1=8), [[-1, 128]], ALU.is_ge, 0.0, 15, 16)
    sel(A("ident"), A("ones", 0, 128), [[-1, 128]], ALU.is_equal, 0.0, 0, 1)
    sel(A("zt", p1=40), A("ones", p1=40), [[-1, NT], [-NT, 8], [0, 16]], ALU.is_equal, 0.0, 0, 1)
    sel(A("bo1"), A("ones", 0, 128), [[-16, 8], [0, 16]], ALU.is_ge, 0.0, 0, 1)
    sel(A("bo"), A("bo1"), [[16, 8], [0, 16]], ALU.is_ge, 0.0, 15, -1)
    lin(A("nbo"), A("bo"), -1.0, 0.0)
    lin(A("boh"), A("bo"), 0.5, 0.0)
    sel(A("dma_"), A("nbo"), [[-1, 128]], ALU.is_equal, 0.0, -1, 1)
    sel(A("dmb"), A("dma_"), [[-1, 128]], ALU.not_equal, 1.0, 0, 1)
    sel(A("dm"), A("dmb"), [[-16, 8], [-128, 16]], ALU.not_equal, 1.0, 15 * 128, 1)
    sel(A("l2a"), A("nbo"), [[-1, 128]], ALU.is_gt, 0.0, 0, 1)
    sel(A("l2"), A("l2a"), [[-1, 128]], ALU.not_equal, -2048.0, 0, 1)
    iota(A("mki"), [[0, 16], [-1, 16]], 16, 1)
    iota(A("ids"), [[3, C]], ID0, 0)
    iota(A("mm_", RI, MW), [[1, 3], [3, C]], ID0, 0)
    iota(A("pci"), [[0, 8]], 0, 1)
    sel(A("jj"), A("ones", 0, 256), [[0, 2], [-1, 128]], ALU.is_equal, 0.0, 0, 1)
    lin(A("i11"), A("ident"), 2.0 ** -11, 0.0)
    lin(A("i2k"), A("ident"), -4096.0, 0.0)
    o = act(A("ip"), A("ident"), AF.Silu, 0.0, float(C))
    o["alts"]["a"] = (o["alts"]["a"][0] + 1300.0, o["alts"]["a"][1])
    lin(A("im"), A("ident"), -float(C), 0.0)
    memset(A("zz"), 0.0)
    copy(A("zz", 15, 143, 16), A("bo", 0, 128, 16))
    lin(A("zzh"), A("zz"), 0.5, 0.0)
    memset(A("c15"), 0.0); memset(A("c15", 15, 128, 16), -16.0)
    ts(A("mki2"), A("mki"), 15, None, ALU.bitwise_and)
    ts(A("pik1"), A("mki2"), 0.0, -0.5, ALU.is_equal, ALU.add)
    lin(A("pick"), A("pik1"), 2.0 ** 18, 0.0)
    ts(A("col", 24, 29), A("mki2", 0, 5), 0.0, None, ALU.is_equal)
    for p in range(5):
        lin(SEL(p), A("bo"), A("col", 24 + p, 25 + p), 0.0)
    ts(A("pci2"), A("pci"), 15, None, ALU.bitwise_and)
    copy(A("col", 0, 1), A("pci2", 0, 1))
    lin(A("col", 6, 7), A("col", 0, 1), -4096.0, MID - 1)
    lin(A("col", 7, 8), A("col", 0, 1), -4096.0, -1.0)
    ts(A("col", 9, 10), A("col", 0, 1), 0.5, MID, ALU.is_gt, ALU.mult)
    lin(A("bo64"), A("bo"), MID / 16, 0.0)
    iota(A("ramp"), [[0, 16], [4096, 16]], 0, 0)
    ts(A("col", 1, 2), A("col", 0, 1), 15.0, -(16 * BASE + 8.5 * 4096 + 1), ALU.is_lt, ALU.mult)
    ts(A("col", 2, 3), A("col", 1, 2), 1.0, None, ALU.add)
    ts(A("col", 3, 4), A("col", 0, 1), NT + 0.5, -MID, ALU.is_gt, ALU.mult)
    ts(A("col", 5, 6), A("col", 3, 4), -1.0, None, ALU.add)
    iota(A("cwi"), [[16, 16]], 0, 0)
    ts(A("cw"), A("cwi"), A("col", 0, 1), None, ALU.add)
    memset(A("cc"), 2047.0 + RC)
    memset(A("cc", 0, 48, 3), 2047.0)
    ts(A("cc", 2, 48, 3), A("cw"), float(RD), None, ALU.add)
    ts(A("cc", 50, 96, 3), A("cw"), float(RI + C), None, ALU.add)
    copy(A("cc", 98, 108, 3), A("cw", 0, 4))
    memset(A("cc", 108, 109), 0.0); memset(A("cc", 109, 112), float(S))
    memset(A("rs32"), 1.0); memset(A("rs32", 0, 84, 64), 0.0)
    memset(A("fw"), 0.0)
    memset(A("rsx"), 0.0); memset(A("rsx", 0, 109, 3), 4096.0)
    ncap = 16 * PIECE
    memset(A("cap", 0, ncap // 2), 2.0 ** 20); memset(A("cap", ncap // 2, ncap), 2.0 ** 20); memset(A("cap", 0, ncap, 16), BASE)
    memset(A("ub", NT * C, NT * C + WN - C), 0.0)
    memset(A("wv", 3 * C, 3 * WN), 0.0)
    memset(A("hw", C, WN), -1.0); memset(A("pw", C, WN), 0.0)
    memset(A("payh", NT * S, NT * S + 50), 0.0)
    memset(A("wc", C, WN), 0.0); memset(A("h32", C, WN), 0.0)
    memset(A("th"), 9.0)
    iota(A("mm_", RC + S, RI), [[0, RI - RC - S]], 0, 0)
    lin(A("usb", p1=40), A("usi", p1=40), -8.0, 0.0)
    for t in range(NT):
        bank = A(["ps2", "ps4", "ps4", "ps5", "ps5"][t], [0, 0, 256, 0, 256][t], [256, 256, 512, 256, 512][t])
        mm([(bank, A("zt", 128 * t, 128 * t + 128, 1, 0, 40), A("usb", p1=40))])
        lin(A("ub", C * t, C * t + C), bank, 1.0, -2.0 ** -10)
    lin(A("s0h", p1=8), A("s0i", p1=8), 1.0, 1.0)
    s0h = A("s0h", p1=8)
    mm([(A("ps3", 320, 336), O8(b), A("s0h", b, C, 16, 0, 8)) for b in range(16)])
    mm([(A("ps6", 0, C), A("bo8", p1=8), s0h)])
    mm([(A("ps1", 0, C), O8(0), s0h)])
    lin(A("swu", 0, 16), A("ps3", 320, 336), 1.0, -1.0)
    act(A("al0"), A("ps6", 0, C), AF.Relu, 1.0, -1.0, accum=A("col", 4, 5))
    ts(A("h16"), A("ps1", 0, C), A("col", 9, 10), None, ALU.add, act=(AF.Identity, A("col", 9, 10), 1.0))
    for j, (c0, c1) in enumerate(FIRST):
        nk, eq, po = A("nk", c0, c1), A("eq", c0, c1), A("ps%d" % (2 + j), 384, 384 + c1 - c0)
        lin(nk, IND(A("nbt"), A("swu", c0 // 16, c1 // 16)), 1.0, 1.0, "nk0")
        tt(eq, nk, A("ps6", c0, c1), ALU.is_equal, "eq0")
        mm([(po, A("ident"), nk), (po, A("i2k"), A("al0", c0, c1)), (po, A("i2k"), eq)], "o0")
        lin(A("oq", c0, c1), po, 1.0, 15.0, "oq0")
    lin(A("col", 8, 9), A("col", 4, 5), -1.0, 0.0)
    for a, b in ((0, C), (C, 3 * C), (3 * C, NT * C)):
        lin(A("cnb", a, b, 1, 0, 8), A("cni", a, b, 1, 0, 8), 1.0, 0.0)
    for a, b in ((0, C), (C, NT * C)):
        mm([(A("ps7", a // 16, b // 16), O8(k), A("cnb", a + k, b, 16, 0, 8)) for k in range(16)])
    lin(A("thb", 0, 16), A("ps7", 0, 16), -90.0, 99.0)
    for t in range(NT):
        lin(A("th", 48 * t, 48 * t + 16), A("ps7", 16 * t, 16 * t + 16), 90.0, 9.0)
    lin(A("thb", 16, 80), A("ps7", 16, 80), -90.0, 99.0)

    def sums(c0, c1, x0, fb, step, x):
        for a in range(c0, c1, step):
            copy(A("xx", x0 + 16 * (a - c0), x0 + 16 * (a - c0 + step)), IND(A("qt"), A("oq", a, a + step)), "va", "gx" + x)
        for a in range(0, c1 - c0, PIECE):
            b = min(a + PIECE, c1 - c0)
            mm([(cut(fb, a, b), A("i11"), A("xx", x0 + 16 * a + k, x0 + 16 * b, 16)) for k in range(16)], "f" + x)

    def votes(c0, c1, x0, fb, ucol, vb, x):
        tt(A("yy", c0, c1), fb, ucol, ALU.mult, "y" + x)
        ts(A("xx", x0 - 1, x0 - 1 + 16 * (c1 - c0), 16), A("yy", c0, c1), 0.5 - TWO23, TWO23 + 2048, ALU.add, ALU.add, tag="thr" + x)
        for a in range(0, c1 - c0, PIECE):
            n, z = 16 * min(PIECE, c1 - c0 - a), x0 + 16 * a
            scan(A("ee", z, z + n), A("cap", 0, n), A("xx", z - 1, z - 1 + n), 2.0 ** 20, ALU.min, ALU.add, "scan" + x)
            mm([(cut(vb, a, a + n // 16), O(k), A("ee", z + 1 + k, z + n, 16)) for k in range(15)], "V" + x)

    def cut(r, a, b):
        return A(r[0], r[3] + a, r[3] + b)

    def sites(t, c0, c1, vb, dn, ph, runs, x):
        sg, mv = A("sg", c0, c1), A("mv", c0, c1)
        act(sg, vb, AF.Sign, bias=A("col", 2, 3), tag="ge" + x)
        tt(mv, dn, sg, ALU.mult, "mv" + x)
        mm([(ph, O(t + 1, "zzh"), mv)] + [(cut(ph, a - c0, b - c0), A("ident"), old) for a, b, old, _ in runs], "hnew" + x)
        for a, b, _, hw in runs[::-1]:
            if t == NT - 1:
                ts(hw, cut(ph, a - c0, b - c0), A("col", 5, 6), None, ALU.add, tag="hw" + x, act=(AF.Identity, A("col", 5, 6), 1.0))
            else:
                lin(hw, cut(ph, a - c0, b - c0), UP, 0.0, "hw" + x)

    def shut(nk, swu, hb, eq, po, x):
        lin(nk, IND(A("nbt"), swu), 1.0, 1.0, "nk" + x)
        for b, e in zip(hb, eq):
            tt(e, nk, b, ALU.is_equal, "eq" + x)
        trip = [(po, A("ident"), nk)] + [(po, A("i2k"), e) for e in eq]
        if x in "ab":
            mm(trip, "o" + x)
        else:
            mm(trip[:-1], "o" + x, closes=False, whole=po[0])
            mm(trip[-1:], "o" + x, opens=False, whole=po[0])

    def wrap(n, sw, lhs, src, out, x, k0=C):
        mm([(sw, lhs, src), (sw, A("ident"), A("ramp", 0, n))], "sib" + x)
        scan(A("kept", k0, k0 + n), A("pick", 0, n), sw, 0.0, ALU.max, ALU.min, "sip" + x)
        back = A("col", 7, 8) if x == "a" else A("col", 6, 7)
        ts(out, A("kept", k0 + 15, k0 + n, 16), back, None, ALU.add, tag="swu" + x, act=(AF.Identity, back, 1.0))

    def ahead(c0, c1, sw, hb, eq, po, runs, x):
        mv, swu = A("mv", c0, c1), A("swu", c0 // 16, c1 // 16)
        if x in BYPE:
            sw = cut(sw, 0, (c1 - c0) // 16)
            mm([(sw, O(b), A("mv", c0 + b, c1, 16)) for b in range(16)], "sib" + x)
            lin(swu, sw, 0.5, MID - 1, "swu" + x)
        else:
            wrap(c1 - c0, sw, A("boh"), mv, swu, x, c0)
        mm([(hb[-1], A("boh"), mv), (hb[-1], A("bo64"), A("ones", 0, c1 - c0))], "hbl" + x)
        shut(A("nn", c0, c1), swu, hb, eq, po, x)
        for a, b, out in runs[::-1]:
            ts(out, cut(po, a - c0, b - c0), 0.0, UP, ALU.max, ALU.mult, "pw" + x, (AF.Relu, 0.0, UP))

    XI = 16 * (C + len(CHUNKS) + 2)
    for t in range(NT):
        last = t == NT - 1
        nth.clear()
        step[0] = t
        P0, L0 = t * PAYP, (t - 1) * PAYW
        HL = A("oh", 20 * ((t + 1) % 2) + 16, 20 * ((t + 1) % 2) + 19)
        HW = A("owu", HL[3], HL[4])
        H0 = 20 * (t % 2)
        iota(A("mm_", 0, 7 * S), [[0, 7], [6, S]], 3 * (NONE + 2) + ID0, 0, "refill")
        iota(A("mm_", 7 * S, RC + S), [[0, RC - 6 * S]], 3 * NONE + ID0, 0, "refill")
        end = C + S if t else C
        vb2, dn2, ph2, po2, *hb2 = [A("ps7", S * k, S * k + S) for k in range(4 + NT)]
        for j, (h0, h1) in enumerate(PARTS):
            w, x = h1 - h0, "cd"[j]
            room = [4 * h0 + k * w for k in range(4)] + [4 * C + 4 * h0 + k * w for k in range(4)]
            vb, dn, ph, po, *hb = [A("ps%d" % (2 + a // 512), a % 512, a % 512 + w) for a in room]
            mm([(dn, A("dm"), A("nk", h0, h1)), (dn, A("c15"), A("ones", 0, w))], "dn" + x)
            for p in range(0 if last else t + 1):
                mm([(hb[p], SEL(p), A("h16", h0, h1))], "hb" + x)
            for i, (c0, c1) in enumerate(CHUNKS):
                if h0 <= c0 < h1:
                    fb, x0 = A("ps%d" % (i % 2), c0, c1), 16 * (c0 + i + 1)
                    sums(c0, c1, x0, fb, GSTEP, "")
                    tt(A("wv", 3 * c0 + 1, 3 * c1, 3), fb, A("wc", c0, c1), ALU.mult, "w1")
                    votes(c0, c1, x0, fb, A("ub", C * t + c0, C * t + c1), cut(vb, c0 - h0, c1 - h0), "")
            sites(t, h0, h1, vb, dn, ph, [(h0, h1, A("h16", h0, h1), A("hw", h0, h1))], x)
            if not last:
                ahead(h0, h1, dn, hb[:t + 1] + [vb], [A("eq", C * p + h0, C * p + h1) for p in range(t + 2)], po,
                      [(h0, h1, A("pw", h0, h1))], x)
        runs = []
        if t > 0:
            arrive("cnt%d" % (t - 1), [A("cnt", N * (t - 1), N * t)], par["hopc"], "sc%d" % (t - 1))
            tr = []
            for r in range(N):
                s = (-16 * DG * (r - rank)) % 128
                x = A("dcol", 8 * (t - 1), 8 * (t - 1) + 1) if r == rank else A("cnt", N * (t - 1) + r, N * (t - 1) + r + 1)
                tr.append((A("ps6", 0, 1), A("jj", s, s + 128), x))
            mm(tr, "tot")
            ts(A("col", 16, 17), A("ps6", 0, 1), 0.0, 1.0, ALU.is_gt, ALU.add, tag="up")
            ts(A("lh"), A("lh"), A("col", 16, 17), None, ALU.mult, tag="lh", act=(AF.Identity, 0.0, A("col", 16, 17)))
            old = A("landh", S * (t - 1), S * t)
            copy(A("uin"), IND(A("ub", C * t, C * t + WN), HL), "va", "uin")
            arrive("arh%d" % (t - 1), [old], par["hop"], "sh%d" % (t - 1))
            arrive("arr%d" % (t - 1), [A("land", L0, L0 + PAYW)], par["hop"], "sp%d" % (t - 1))
            po, fb = A("ps6", 256, 256 + S), A("ps6", 320, 320 + S)
            hb = [cut(r, C - CUT, C + S - CUT) for r in hb2[:t + 1]]
            wrap(S, A("ps7", 448, 448 + S), SEL(t), old, A("swa", 0, 3), "a")
            for p in range(t + 1):
                mm([(hb[p], SEL(p), old)], "hba")
            shut(A("nk", C, C + S), A("swa", 0, 3), hb, [A("eqa", S * p, S * p + S) for p in range(t + 1)], po, "a")
            lin(A("oq", C, C + S), po, 1.0, 15.0, "oqa")
            sums(C, C + S, XI, fb, GSTEPI, "i")
            tt(A("w1i"), fb, A("land", L0 + 1, L0 + 1 + S), ALU.mult, "w1i")
            copy(IND(A("wv"), HW), A("w1i"), tag="scw")
            if not last:
                ts(A("col", 8, 9), A("land", L0, L0 + 1), A("pay", P0 - PAYP + 108, P0 - PAYP + 109), 0.0, ALU.add, ALU.min, tag="db")
            votes(C, C + S, XI, fb, A("uin"), cut(vb2, C - CUT, C + S - CUT), "i")
            runs.append((C, C + S, old, A("hwi"), A("pwi")))
        if runs:
            mm([(dn2, A("dm"), A("nk", CUT, end)), (dn2, A("c15"), A("ones", 0, end - CUT))], "dnb")
            sites(t, CUT, end, vb2, dn2, ph2, [r[:4] for r in runs], "b")
        if t > 0:
            copy(IND(A("hw"), HL), A("hwi"), "v" if last else "va", "sch")
        if runs and not last:
            ahead(CUT, end, dn2, hb2[:t + 1] + [vb2],
                  [A("eqb", 112 * p, 112 * p + end - CUT) for p in range(t + 2)], po2, [r[:2] + r[4:] for r in runs], "b")
            if t > 0:
                copy(IND(A("pw"), HL), A("pwi"), "va", "sco")
        W1 = A("wv", 1, 3 * C, 3)
        ts(A("fl", 2 * C, 3 * C), W1, A("lh", 8 + t, 9 + t), None, ALU.is_gt, tag="ch")
        ts(A("fl", 0, C), W1, A("lh", t, t + 1), None, ALU.is_lt, tag="cl")
        ts(A("fl", C, 2 * C), W1, 0.0, None, ALU.is_gt, tag="al", act=(AF.Sign, 0.0, 1.0))
        lin(A("wv", 0, 3 * C, 3), W1, 0.5, 0.0, "half")
        lin(A("wv", 2, 3 * C, 3), W1, 2.0, 0.0, "twice")
        mm([(A("ps6", 16, 64), O(b), A("fl", b, 3 * C, 16)) for b in range(16)], "pw3")
        tt(A("fw", 32, 80), A("ps6", 16, 64), A("th", 48 * t, 48 * t + 48), ALU.is_ge, "fw")
        tt(A("dbl"), A("ps6", 16, 32), A("thb", 16 * t, 16 * t + 16), ALU.is_ge, "dbl")
        die, alive, high, hole = A("fw", 32, 48), A("fw", 48, 64), A("fw", 64, 80), A("fw", 0, 16)
        tt(hole, die, alive, ALU.is_ge, "hole")
        scan(A("sc"), A("rs32"), A("fw"), 0.0, ALU.mult, ALU.add, "sc")
        X = 64
        sh, sc_, nh = A("sc", 0, 16), A("sc", 64, 80), A("sc", 16, 32)
        xa, xb, xc, xv = A("ps6", X, X + 48, 3), A("ps6", X + 1, X + 48, 3), A("ps6", X + 48, X + 96, 3), A("ps6", X + 50, X + 96, 3)
        ex = A("ps6", X + 108, X + 109)
        mm([(A("ps6", X, X + 48), A("ident"), A("cc", 0, 48)), (xb, A("l2"), high), (xa, A("l2"), hole)], "px0", closes=False, whole="ps6")
        mm([(xa, A("bo"), sh), (xb, A("bo"), sc_), (xb, A("nbo"), nh)], "px", opens=False, whole="ps6")
        scan(A("pay", P0, P0 + 48), A("rsx", 0, 48), A("ps6", X, X + 48), 0.0, ALU.max, ALU.min, "rr")
        copy(A("of2", 0, 16), A("pay", P0 + 2, P0 + 48, 3), "va", "of2")
        mm([(A("ps6", X + 48, X + 112), A("ident"), A("cc", 48, 112)), (xv, A("ip"), A("dbl")), (xv, A("im"), high),
            (xc, A("l2"), hole), (xc, A("bo"), sh), (xc, A("nbo"), nh), (A("ps6", X + 98, X + 108, 3), A("bo"), A("sc", 80, 84)),
            (ex, A("bo"), A("sc", 80, 81)), (ex, A("nbo"), A("sc", 16, 17))], "pxb")
        scan(A("pay", P0 + 48, P0 + 112), A("rsx", 48, 112), A("ps6", X + 48, X + 112), 0.0, ALU.max, ALU.min, "rrb")
        copy(A("of2", 16, 36), A("pay", P0 + 50, P0 + 108, 3), "va", "of2b")
        if not last:
            dc = A("dcol", 8 * t, 8 * t + 1)
            ts(dc, A("pay", P0 + 108, P0 + 109), A("col", 8, 9), None, ALU.subtract, tag="d")
            send("sc", t, [dc])
        copy(IND(A("mm_", 0, RI), A("of2", 0, 16)), A("ids"), "va", "scat")
        scan(A("ra"), A("pick", 0, S), A("mm_", RC, RC + S), 0.0, ALU.max, ALU.min, "ra")
        lin(A("osu", 0, 3), A("ra", 15, S, 16), 1.0 / 3, -ID0 / 3, "osu")
        lin(A("osu", 4, 7), A("ra", 15, S, 16), 1.0, -float(ID0), "osw")
        lin(A("payh", S * t, S * t + S), IND(A("hw"), A("osu", 0, 3)), 1.0 if last else 1 / UP, 0.0, "payh")
        copy(A("pay", P0 + 112, P0 + PAYP), IND(A("wv"), A("osu", 4, 7)), "va", "payw")
        if last:
            send("sf", t, [A("payh", S * t, S * t + 2 * PAYN), A("pay", P0 + 111, P0 + PAYP)])
        else:
            send("sh", t, [A("payh", S * t, S * t + S)])
            send("sp", t, [A("pay", P0 + 111, P0 + PAYP)])
        copy(A("gb"), IND(A("mm_"), A("of2", 16, 35)), "va", "gb")
        mm([(A("ps6", 224, 243), O(b), A("gb", b, S + C, 16)) for b in range(16)] + [(A("ps6", 240, 243), A("bo"), A("ones", 0, 3))], "rb")
        lin(A("oh", H0, H0 + 19), A("ps6", 224, 243), 1.0 / 48, -(ID0 + 1) / 3, "oh")
        lin(A("owu", H0, H0 + 19), A("ps6", 224, 243), 1.0 / 16, -float(ID0), "owu")
        if last:
            copy(A("h32", 0, C), IND(A("hw"), A("oh", H0, H0 + 16)), "va", "h32")
        else:
            for c0, c1 in FIRST:
                lin(A("oq", c0, c1), IND(A("pw"), A("oh", H0 + c0 // 16, H0 + c1 // 16)), 1 / UP, 15.0, "oq")
            lin(A("nk", 0, C), A("oq", 0, C), 1.0, -15.0, "nkg")
            lin(A("h16"), IND(A("hw"), A("oh", H0, H0 + 16)), 1 / UP, 0.0, "h16")
        copy(A("wc", 0, C), IND(A("wv"), A("owu", H0, H0 + 16)), "va", "wc")
    L0, HL = (NT - 1) * PAYW, A("oh", H0 + 16, H0 + 19)
    step[0] = NT
    arrive("arh%d" % (NT - 1), [A("landh", S * (NT - 1), S * NT)], par["hop"], "sf%d" % (NT - 1))
    arrive("arr%d" % (NT - 1), [A("land", L0, L0 + PAYW)], par["hop"], "sf%d" % (NT - 1))
    copy(IND(A("h32"), HL), A("landh", S * (NT - 1), S * NT), tag="endh")
    copy(IND(A("wc"), HL), A("land", L0 + 1, L0 + 1 + S), tag="endw")
    store("yh", "h32", "a", "outh")
    store("yw", "wc", "s", "outw")
    return ops


def meet(a, b):
    if a[0] != b[0] or a[4] <= b[3] or b[4] <= a[3]:
        return False
    if a[5] == b[5] and a[5] > 1 and (a[3] - b[3]) % a[5] != 0:
        return False
    return True


def needs(ops):
    byname, tags = {}, {}
    for i, o in enumerate(ops):
        tags[o["tag"]] = i
        hard = set()
        for kind, refs in (("r", o["rd"]), ("w", o["wr"])):
            for r in refs:
                for j, k2, r2 in byname.get(r[0], []):
                    if j != i and (kind == "w" or k2 == "w") and meet(r, r2):
                        hard.add(j)
        for kind, refs in (("r", o["rd"]), ("w", o["wr"])):
            for r in refs:
                byname.setdefault(r[0], []).append((i, kind, r))
        o["banks"] = sorted(set(r[0] for r in o["rd"] + o["wr"] if r[0] not in _SB))
        far = set()
        for j in hard:
            far |= ops[j]["all"]
        o["all"] = far | hard
        o["near"] = sorted(hard - far)
        o["behind"] = tags[o["after"]] if "after" in o else None


def place(ops, prio, par, eng=None):
    n, lat = len(ops), par["lat"]
    pre = [o["near"] + ([o["behind"]] if o["behind"] is not None else []) for o in ops]
    left = [len(p) for p in pre]
    users = [[] for _ in ops]
    for i, p in enumerate(pre):
        for j in p:
            users[j].append(i)
    ready = [i for i in range(n) if left[i] == 0]
    busy = {e: [] for e in "vapgs"}
    bank = {"ps%d" % b: [] for b in range(8)}
    start, free, end, got = [0.0] * n, [0.0] * n, [0.0] * n, [None] * n
    while ready:
        i = max(ready, key=lambda k: (prio[k], -k))
        ready.remove(i)
        o = ops[i]
        best = None
        for e in ([eng[i]] if eng else [WHO[o["tag"]]] if o["tag"] in WHO else list(o["alts"]) or [None]):
            t0 = free[o["behind"]] if o["behind"] is not None else 0.0
            for j in o["near"]:
                t0 = max(t0, end[j] + (0.0 if got[j] == e == "p" else lat))
            c = 0.0
            if e is not None:
                c = o["alts"][e][0]
                taken = [x for x in busy[e] if x[1] > t0]
                for b in o["banks"]:
                    taken += [(s - lat, f + lat) for s, f, e2 in bank[b] if e2 != e and f + lat > t0]
                for s, f in sorted(taken):
                    if s >= t0 + c:
                        break
                    t0 = max(t0, f)
            key = t0 + c + (par.get("vb", 0.0) * c if e == "v" else 0.0)
            if best is None or key < best[0]:
                best = (key, e, t0, c)
        _, e, t0, c = best
        got[i], start[i], free[i], end[i] = e, t0, t0 + c, t0 + c + o.get("lat", 0.0)
        if e is not None:
            busy[e].append((t0, t0 + c))
            for b in o["banks"]:
                bank[b].append((t0, t0 + c, e))
        for k in users[i]:
            left[k] -= 1
            if left[k] == 0:
                ready.append(k)
    return sorted(range(n), key=lambda k: (start[k], k)), got


def links(ops, order, eng):
    last, lastb, before, soft = {}, {}, [None] * len(ops), [[] for _ in ops]
    for i in order:
        e = eng[i]
        if e is not None:
            before[i] = last.get(e)
            last[e] = i
        for b in ops[i]["banks"]:
            d = lastb.setdefault(b, {})
            soft[i] += [j for e2, j in d.items() if e2 != e]
            d[e] = i
    return before, soft


def replay(ops, order, eng, par):
    before, soft = links(ops, order, eng)
    n, lat = len(ops), par["lat"]
    start, free, end = [0.0] * n, [0.0] * n, [0.0] * n
    for i in order:
        o, e = ops[i], eng[i]
        t0 = free[before[i]] if before[i] is not None else 0.0
        if o["behind"] is not None:
            t0 = max(t0, free[o["behind"]])
        for j in o["near"]:
            t0 = max(t0, end[j] + (0.0 if eng[j] == e == "p" else lat))
        for j in soft[i]:
            t0 = max(t0, end[j] + lat)
        start[i] = t0
        free[i] = t0 + (o["alts"][e][0] if e is not None else 0.0)
        end[i] = free[i] + o.get("lat", 0.0)
    return start, free, end


def tails(ops, order, eng, queues, par):
    before, soft = links(ops, order, eng)
    tail = [0.0] * len(ops)
    for i in reversed(order):
        o, e = ops[i], eng[i]
        c = o["alts"][e][0] if e is not None else 0.0
        tail[i] += c + o.get("lat", 0.0)
        for j in o["near"]:
            tail[j] = max(tail[j], tail[i] + par["lat"])
        for j in [o["behind"]] + ([before[i]] if queues else []):
            if j is not None:
                tail[j] = max(tail[j], tail[i] - ops[j].get("lat", 0.0))
    return tail


def choose(ops, who):
    return [("v" if o["name"] in who else "a") if len(o["alts"]) > 1 else (list(o["alts"]) or [None])[0] for o in ops]


def plan(par=PAR, who=WHO, when=WHEN, ops=None):
    if ops is None:
        ops = build(None, 1, par)
        needs(ops)
    key = [max(o["step"], 0) * PERIOD + when.get(o["name"], -PERIOD) for o in ops]
    for i, o in enumerate(ops):
        for j in o["near"] + ([] if o["behind"] is None else [o["behind"]]):
            key[i] = max(key[i], key[j] + 1e-5)
    return sorted(range(len(ops)), key=lambda i: (key[i], i)), choose(ops, who)


PLAN = {}


def ways(T, topo, core):
    rank = T.rank_of(core)
    nxt = T.cores[(rank + 1) % N]
    others = [c for c in T.cores if c != core]
    direct = [c for c in others if topo.may_write(core, c)]
    far = [c for c in others if c not in direct]
    free = [c for c in topo.cores_of(core) if T.rank_of(c) is None and all(topo.may_write(c, d) for d in far)]
    free.sort(key=lambda c: topo.die(c) != topo.die(core))
    relay, helpers = free[0:2], free[2:4]
    share = {h: far[i::len(helpers)] for i, h in enumerate(helpers)}
    near = [c for c in topo.cores_of(core) if T.rank_of(c) is None and c not in free and all(topo.may_write(c, d) for d in direct)]
    near.sort(key=lambda c: topo.die(c) != topo.die(core))
    share[near[0]] = direct
    return nxt, relay, direct, share


def slots(kind, t, r):
    if kind == "sh":
        return "payh", "landh", t * S, t * S, S if t < NT - 1 else 2 * PAYN, "arh%d" % t
    if kind == "sp":
        return "pay", "land", t * PAYP + 111, t * PAYW, PAYN, "arr%d" % t
    return "dcol", "cnt", 8 * t, N * t + r, 1, "cnt%d" % t


def messages(T, r, what):
    if what[0] == "sf":
        return messages(T, r, ("sh", what[1])) + messages(T, r, ("sp", what[1]))
    a, b, c0, d0, w, sem = slots(what[0], what[1], r)
    to = [d for d in range(N) if d != r] if what[0] == "sc" else [(r + 1) % N]
    return [(d, T[a][:, c0:c0 + w], lambda U: U[b][:, d0:d0 + w], sem) for d in to]


def bits(engines):
    return sum(1 << e for e in engines)


def dst(topo, d, s):
    rid, pid = topo.addr(d, s)
    return DstId(rid=rid, pnc=pid)


def lanes(T, topo, owner, kind, t):
    every = topo.engines(owner, ways(T, topo, owner)[1][0])
    half = len(every) // 2
    return every if t < NT - 1 else every[:half] if kind == "sh" else every[half:]


def write(g, T, topo, core, to, src, piece, sem, engines):
    if len(to) == 1:
        rid, pid = topo.addr(to[0], core)
        g.remote_dma(piece, src, sem, T.sem.loc, pid, rid, bits(engines))
    else:
        g.remote_dma_fused([RemoteDMATransfer(dst_ids=[dst(topo, d, core) for d in to], dma_engine_mask=bits(engines), remote_sem=sem,
                                              src=src, dsts=[piece] * len(to))], local_sem=T.sem.loc)
    return len(engines)


def hand_on(g, core, T, topo):
    for owner in T.cores:
        if core not in topo.cores_of(owner):
            continue
        nxt, relay, direct, share = ways(T, topo, owner)
        if core in relay:
            kind, to, steps = ["sh", "sp"][relay.index(core)], [nxt], NT
        elif core in share:
            kind, to, steps = "sc", share[core], NT - 1
        else:
            return
        sent = 0
        for t in range(steps):
            _, b, _, d0, w, sem = slots(kind, t, T.rank_of(owner))
            g.wait_ge(T.sem[sem], len(lanes(T, topo, owner, kind, t)))
            w = S if kind == "sh" else w
            sent += write(g, T, topo, core, to, T[b][:, d0:d0 + w], T[b][:, d0:d0 + w], T.sem[sem], topo.engines(core, to[0]))
        g.wait_ge(T.sem.loc, sent)


def rank_program(g, core, T, topo):
    rank = T.rank_of(core)
    if rank is None:
        hand_on(g, core, T, topo)
        return
    nxt, relay, direct, share = ways(T, topo, core)
    first = {"sh": [relay[0]], "sp": [relay[1]], "sc": list(share)}
    n_arr = len(topo.engines(ways(T, topo, T.cores[(rank - 1) % N])[1][0], core))
    n_cnt = 0
    for o in T.cores:
        if o != core:
            n_cnt += sum(len(topo.engines(h, to[0])) for h, to in ways(T, topo, o)[3].items() if core in to)
    if not PLAN:
        PLAN["it"] = plan()
    order, eng = PLAN["it"]
    ops = build(T, rank)
    needs(ops)
    soft = links(ops, order, eng)[1]
    Q = {"v": g.vector, "a": g.scalar, "p": g.tensor, "g": g, "s": g.sync}
    count = {e: 0 for e in ESEM}
    for i in order:
        o = ops[i]
        if "done" in o:
            s, v = o["done"]
            o["sig"] = (s, v if v is not None else (n_arr if s.startswith("ar") else n_cnt))
        elif "remote" in o:
            o["sig"] = None
        else:
            count[eng[i]] += 1
            o["sig"] = (ESEM[eng[i]], count[eng[i]])
    seen = {e: {} for e in Q}
    sent = 0
    for i in order:
        o, e = ops[i], eng[i]
        if e is None:
            o["knew"] = {}
            continue
        for j in sorted(o["near"] + soft[i], reverse=True):
            if eng[j] == e == "p" or ops[j]["sig"] is None:
                continue
            s, v = ops[j]["sig"]
            if seen[e].get(s, 0) < v:
                o.setdefault("waits", {})[s] = max(o.get("waits", {}).get(s, 0), v)
                for s2, v2 in list(ops[j]["knew"].items()) + [(s, v)]:
                    seen[e][s2] = max(seen[e].get(s2, 0), v2)
        for s, v in sorted(o.get("waits", {}).items()):
            Q[e].wait_ge(T.sem[s], v)
        o["knew"] = dict(seen[e])
        f = o["alts"][e][1]
        if "remote" in o and f[0] == "sf":
            both = []
            for kind in ("sh", "sp"):
                a, b, c0, d0, w, sem = slots(kind, f[1], rank)
                mine = lanes(T, topo, core, kind, f[1])
                both.append(RemoteDMATransfer(dst_ids=[dst(topo, first[kind][0], core)], dma_engine_mask=bits(mine), remote_sem=T.sem[sem],
                                              src=T[a][:, c0:c0 + w], dst=T[b][:, d0:d0 + w]))
                sent += len(mine)
            g.remote_dma_fused(both, local_sem=T.sem.loc)
        elif "remote" in o:
            a, b, c0, d0, w, sem = slots(f[0], f[1], rank)
            sent += write(g, T, topo, core, first[f[0]], T[a][:, c0:c0 + w], T[b][:, d0:d0 + w], T.sem[sem], lanes(T, topo, core, f[0], f[1]))
        elif "done" in o:
            f(Q[e])
        else:
            f(Q[e]).then_inc(T.sem[ESEM[e]], 1)
    g.wait_ge(T.sem.loc, sent)
    for e in ESEM:
        g.wait_ge(T.sem[ESEM[e]], count[e])
    for o in ops:
        if "done" in o:
            g.wait_ge(T.sem[o["sig"][0]], o["sig"][1])
